import numpy as np, ml_dtypes
CORES = [16,18,20,22]
N = 4
BF = ml_dtypes.bfloat16
def gentries(a):
    return np.ascontiguousarray(a.reshape(8, 16, -1).transpose(0, 2, 1)).reshape(8, -1)
def gtable(e):
    e = np.asarray(e); return np.ascontiguousarray(e.reshape(8, -1, 16).transpose(0, 2, 1)).reshape(128, -1).astype(np.int32)
A, H, S, ST, RO, R = 1024, 4096, 128, 6, 3, 12
def atoms(rng, reach):
    off = np.concatenate([np.arange(-reach, 0), np.arange(1, reach + 1)])
    ch = off[np.argsort(rng.random((8, A, 2 * reach)), axis=-1)[..., :16]]
    ch = ch * (rng.random((8, A, 1)) >= 0.03125)
    pos = (np.arange(A)[None, :, None] + ch) % A
    nb = np.zeros((8, 16, A), np.int64)
    for g in range(8):
        o = rng.permutation(A); nb[g][:, o] = o[pos[g]].T
    return nb
def parts(rng, reach=R):
    nb = atoms(rng, reach); e = rng.integers(0, 256, (N, 8, 16, H)); s0 = rng.integers(0, A, (N, 8, RO, S))
    return nb, e, s0, rng.integers(0, 256, (N, 8, 16, S)), rng.integers(70 * ST, 210 * ST, (N, 8, 16))
def layers(rng):
    m = (A - 1) // (2 * ST - 1); lay = rng.permutation(A - 1)[:m * (2 * ST - 1)].reshape(2 * ST - 1, m); nb = rng.integers(0, A, (16, A))
    nb[:8, lay[0]] = rng.choice(lay[1], (8, m)); nb[8:, lay[0]] = rng.choice(lay[ST], (8, m))
    for i in range(1, 2 * ST - 1):
        nb[:, lay[i]] = A - 1 if i in (ST - 1, 2 * ST - 2) else rng.choice(lay[i + 1], (16, m))
    return nb, lay[0]
def owned(rng):
    n = 2 * ST; free = np.ones(A, bool); taken = np.zeros(H, bool); c = np.zeros((S, n), np.int64)
    for j in range(S):
        for m in range(n):
            x = rng.permutation(np.flatnonzero(free)); hs = []
            if m >= 2: hs.append(place(c[j, m - 2], c[j, m - 1], x))
            if m == n - 1: hs += [place(c[j, m - 1], x, c[j, 0]), place(x, c[j, 0], c[j, 1])]
            good = np.ones(x.shape, bool)
            for a in range(len(hs)):
                good &= ~taken[hs[a]]
                for b in range(a): good &= hs[a] != hs[b]
            i = int(np.argmax(good)); c[j, m] = x[i]; free[x[i]] = False
            for h in hs: taken[h[i]] = True
    nb = rng.integers(0, A, (16, A)); nb[:8, c[:, 0]] = c[:, 1]; nb[8:, c[:, 0]] = c[:, n - 1]
    for m in range(1, ST):
        nb[:, c[:, m]] = c[:, m + 1]; nb[:, c[:, n - m]] = c[:, n - m - 1]
    return nb, c[:, 0]
def pack(nb, e, s0, q, th):
    return {"nb": np.repeat(nb.reshape(1, 128, A), N, axis=0).astype(np.int32), "ang": e.reshape(N, 128, H).astype(np.float32).astype(BF),
            "st": np.stack([gtable(a.reshape(8, -1)) for a in s0]), "q": q.reshape(N, 128, S).astype(np.float32).astype(BF), "th": th.reshape(N, 128, 1).astype(np.int32)}
def setup_inputs(rng):
    return pack(*parts(rng))
def setup_inputs_ties(rng):
    nb, e, s0, q, th = parts(rng); v = np.arange(A)[None, :]
    nb[0] = 8 * (v >> 3) + rng.integers(0, 8, (16, A)); e[:, 0] = rng.choice(np.array([0, 192, 255, 255, 255]), (N, 1, H)); q[:, 0] = 0
    e[:, 1] = 10 * rng.integers(0, 2, (N, 16, H)); q[:, 1] = 10 * rng.integers(0, 2, (N, 16, S)); th[:, 1] = 10 * rng.integers(1, ST + 1, (N, 16))
    e[:, 2] = rng.choice(np.array([0, 3, 4, 255]), (N, 1, H)); q[:, 2] = 4; th[:, 2] = rng.integers(255, 520, (N, 1))
    e[:, 3] = 7; q[:, 3] = rng.integers(0, 256, (N, 16, S)); th[:, 3] = 7 * rng.integers(3, 2 * ST, (N, 16))
    e[:, 4] = rng.choice(np.array([100, 156]), (N, 16, H)); q[:, 4] = 128
    e[:, 5] = e[:, 5] * rng.integers(0, 2, (N, 16, H))
    for r in range(N):
        for g, n in ((5, 9), (6, 8), (7, 16)): th[r, g] = np.where(rng.permutation(16) < n, 0, 4095)
    return pack(nb, e, s0, q, th)
def setup_inputs_repeats(rng):
    nb, e, s0, q, th = parts(rng, 8)
    s0[:, ::2] = rng.choice(np.array([0, A - 1, A // 2, 5]), (N, 4, RO, S))
    e[:, 1::2] = e[:1, 1::2].copy(); q[:, 2::4] = q[:, 2::4, :, :1].copy()
    return pack(nb, e, s0, q, th >> 1)
def setup_inputs_stuck(rng):
    nb, e, s0, q, th = parts(rng); v = np.arange(A)[None, :]; k = np.arange(16)[:, None]
    nb[0] = 4 * (v >> 2) + rng.integers(0, 4, (16, A))
    nb[1, :8] = v; nb[2, 8:] = v
    nb[3] = v ^ rng.integers(0, 2, (16, A)); nb[3, ::8] = v ^ 1; nb[4] = v
    nb[5] = nb[5][rng.integers(0, 4, (16, A)), np.repeat(v, 16, axis=0)]
    nb[6] = 8 * (v >> 3) + rng.integers(0, 8, (16, A))
    x = v & 127; nb[7] = np.where(x == 0, v + 16 + k, np.where((x < 16) | (x >= 16 * (ST - 2)), v - x, v + 16))
    for g in (0, 3, 4, 6): th[:, g] = rng.integers(0, 800, (N, 16))
    s0[:, :, :, 0] = 0; s0[:, :, :, S - 1] = A - 1
    s0[:, 7] = 128 * rng.integers(0, A >> 7, (N, RO, S)) + rng.integers(1, 16, (N, RO, S))
    s0[0, 3] = rng.integers(256, A, (RO, 1)); th[0, 3] = 0
    return pack(nb, e, s0, q, th)
def setup_inputs_far(rng):
    nb, e, s0, q, th = parts(rng)
    for g in range(8):
        nb[g], a = layers(rng); s0[:, g] = rng.choice(a, (N, RO, S))
    if 2 * ST * S <= A:
        nb[1], a = owned(rng); s0[:, 1] = a[np.argsort(rng.random((N, RO, S)), axis=-1)]
    th = rng.integers(200 * ST, 300 * ST, (N, 8, 16)); th[2:, 5] = 4095; th[2:, 6] = 0; th[:2] = 0
    e[:, 2] = rng.integers(224, 256, (N, 16, H)); th[:, 2] = rng.integers(min(2048, 448 * ST), 448 * ST + 1, (N, 16))
    e[:, 3] = 255; th[:, 3] = 510 * ST; th[2:, 3, :8] = 510 * ST + 1
    return pack(nb, e, s0, q, th)
def setup_inputs_spread(rng):
    nb, e, s0, q, th = parts(rng); v = np.arange(A)[None, :]; k = np.arange(16)[:, None]
    e = (np.exp2(8 * rng.random((N, 8, 1, H))) * rng.random((N, 8, 16, H))).astype(np.int64)
    q = (np.exp2(8 * rng.random((N, 8, 1, S))) * rng.random((N, 8, 16, S))).astype(np.int64)
    th = np.minimum(np.exp2(12 * rng.random((N, 8, 16))).astype(np.int64), 4095)
    s0 = np.minimum((A * rng.random((N, 8, RO, S)) ** 3).astype(np.int64), A - 1)
    c = v & 3; nb[0] = 4 * rng.integers(0, A >> 2, (16, A)) + np.where(c >= 2, c, np.where(k < 8, 2, 3))
    s0[:, 0] = 4 * (s0[:, 0] >> 2) + rng.integers(0, 2, (N, RO, S))
    nb[2:4] = rng.integers(0, A, (2, 16, A))
    return pack(nb, e, s0, q, th)
def check_inputs(d):
    bad = []
    for k, lo, hi in (("nb", 0, A - 1), ("ang", 0, 255), ("st", 0, A - 1), ("q", 0, 255), ("th", 0, 4095)):
        v = np.asarray(d[k]).astype(np.float64)
        if not np.all((v >= lo) & (v <= hi)): bad.append("range of " + k)
        elif not np.all(v == np.floor(v)): bad.append(k + " holds numbers that aren't whole")
    if np.any(d["nb"] != d["nb"][:1]): bad.append("nb isn't alike on all ranks")
    return bad
def place(p, v, n):
    return ((((2 * p + 1) * (2 * n + 1)) >> 4) + 37 * v) & (H - 1)
def walk(e, v0, w, rows, nbr):
    path = [v0]; kk = np.arange(16)[None, :, None]
    for i in range(ST):
        v = path[i]; p = path[max(i - 1, 0)]
        n = np.take_along_axis(nbr, v[:, None, :], 2)
        h = place(p[:, None, :], v[:, None, :], n)
        x = np.take_along_axis(e, h.reshape(8, 1, 16 * S), 2).reshape(8, 16, 16, S)
        sc = np.add.reduce(np.abs(x - w[:, :, None, :]), axis=1)
        bar = np.any(np.stack(path)[:, :, None, :] == n[None], axis=0)
        if i == 0: bar = bar | (kk < rows) | (kk >= rows + 8)
        sc = np.where(bar, 2 ** 20, sc); k = np.argmin(sc, axis=1)[:, None, :]
        ok = np.take_along_axis(sc, k, 1)[:, 0] < 2 ** 20
        path.append(np.where(ok, np.take_along_axis(n, k, 1)[:, 0], v))
    return np.stack(path)
def reference(nb, ang, st, q, th):
    e = np.asarray(ang, np.float32).astype(np.int32).reshape(N, 8, 16, H); w = np.asarray(q, np.float32).astype(np.int32).reshape(N, 8, 16, S)
    lim = th.astype(np.int64).reshape(N, 8, 16, 1); nbr = nb.astype(np.int64).reshape(N, 8, 16, A)
    sl = np.stack([gentries(a) for a in st]).astype(np.int64).reshape(N, 8, RO, S)
    rings = np.zeros((N, 8, 16, RO, S), np.int64); m = np.arange(16)[None, :, None]
    for t in range(RO):
        new = []
        for r in range(N):
            s = (r + 1 + t % (N - 1)) % N
            pa = walk(e[r], sl[r, :, t], w[r], 0, nbr[r]); pb = walk(e[s], sl[r, :, t], w[r], 8, nbr[s])
            eq = pa[1:, None] == pb[None, 1:]; eq[0, 0] = False
            eq = eq.reshape(ST * ST, 8, S); found = np.any(eq, axis=0); f = np.argmax(eq, axis=0)
            i = f // ST + 1; j = f - (i - 1) * ST + 1; ln = np.where(found, i + j, 0)[:, None, :]; i = i[:, None, :]
            ca = np.take_along_axis(pa.transpose(1, 0, 2), np.minimum(m, i), 1); cb = np.take_along_axis(pb.transpose(1, 0, 2), np.clip(ln - m, 0, ST), 1)
            c = np.where(m <= i, ca, cb); live = m < ln
            before = np.take_along_axis(c, np.clip(np.where(m == 0, ln - 1, m - 1), 0, 15), 1)
            after = np.take_along_axis(c, np.clip(np.where(m == ln - 1, 0, m + 1), 0, 15), 1)
            h = place(before, c, after)
            x = np.take_along_axis(e[r], h.reshape(8, 1, 16 * S), 2).reshape(8, 16, 16, S)
            tot = np.add.reduce(np.where(live[:, None], x, 0), axis=2)
            heavy = found & (np.add.reduce((tot >= lim[r]).astype(np.int64), axis=1) >= 9)
            use = live & heavy[:, None, :]; gg = np.broadcast_to(np.arange(8)[:, None, None], h.shape)
            mark = np.zeros((8, H), bool); mark[gg[use], h[use]] = True
            new.append(np.where(mark[:, None, :], e[r] - (e[r] >> 2), e[r])); rings[r, :, :, t] = np.where(live, c, -1)
        e = np.stack(new)
    return {"ye": e.reshape(N, 128, H).astype(np.float32).astype(BF), "yr": rings.reshape(N, 128, RO * S).astype(np.float32)}

@@ -1,0 +1,450 @@
+from concourse.bass import DstId, RemoteDMATransfer
+from concourse.mybir import AluOpType as O, ActivationFunctionType as F
+
+N, RO, ST, NCH = 4, 3, 6, 2
+NTS = 19
+SCRATCH, SHAPE, WIDE, PLACE = {}, {}, {}, {}
+SEMAPHORES = ["sv", "ss", "sp", "sg", "as0", "aq", "ar0", "ar1", "ar2", "loc"] + ["d%d" % i for i in range(16)]
+QSEM = {"V": "sv", "S": "ss", "P": "sp", "G": "sg"}
+POOL = {"float32": "poolf", "bfloat16": "poolb", "float16": "poolh", "int32": "pooli", "uint16": "poolu"}
+APART = "stu sr0 sr1 sr2 qa qr0 qr1 qr2 sti thi".split()
+
+
+def sb(name, shape, dtype="float32"):
+    SCRATCH[name] = ("sbuf", shape, dtype)
+
+
+def many(dtype, cols, names):
+    for n in names.split():
+        if cols > 768 or n in APART: sb(n, [128, cols], dtype); continue
+        pool = SCRATCH.setdefault(POOL[dtype], ("sbuf", [128, 0], dtype)); PLACE[n] = (POOL[dtype], pool[1][1]); SHAPE[n] = [128, cols]; WIDE[n] = dtype in ("float32", "int32")
+        pool[1][1] += -(-cols // 32) * 32
+
+
+many("int32", 1024, "nbi"); many("float32", 1024, "NBO IDT"); many("bfloat16", 4112, "E"); many("bfloat16", 4096, "G4")
+many("bfloat16", 128, "qa qr0 qr1 qr2"); many("int32", 24, "sti"); many("uint16", 24, "stu sr0 sr1 sr2"); many("int32", 1, "thi"); many("float32", 1, "thf")
+many("int32", 8, "pci"); many("float32", 8, "pcf C8 Pick mcol"); many("float16", 8, "C8h"); many("bfloat16", 8, "B32 B16")
+many("float32", 136, "CI S1 PermO SEG T1 T3"); many("bfloat16", 136, "BIGP BIGA BIGB crN crA crB"); many("float32", 128, "CG CR If I296f dA dB"); many("float32", 288, "JX SEGJ")
+many("float16", 128, "Ih I64 I296 ShB ShA G0"); many("bfloat16", 128, "one m296 Ib nIb m4Ib m64Ib m256Ib p4Ib Blk EQG Dm S01 CR0")
+many("float32", 16, "PHE PRE"); many("float32", 2, "half"); many("float16", 640, "SelJ"); many("bfloat16", 2048, "SelT")
+many("bfloat16", 2048, "xC mC"); many("float32", 128, "tn0 tn1 OSC")
+sb("AL2", [128, 8, 16]); sb("EQ", [128, 8, 36], "bfloat16"); many("float32", 288, "FJ"); many("float16", 128, "BLs PL PA0 CS"); many("int32", 128, "IR")
+many("float32", 128, "TT LF APs HF"); many("bfloat16", 128, "FN L0 L1 i0 MA MA64 Lm MN ML hiB TH NH LOT HIT"); many("bfloat16", 640, "MB"); many("float16", 768, "PB")
+many("bfloat16", 8192, "OHL THH"); many("float32", 520, "CT"); many("bfloat16", 512, "NM"); many("bfloat16", 256, "NM2"); many("float32", 384, "YR")
+for _p in "AB":
+    for _d, _c, _l in (("float32", 128, "n t1"), ("int32", 128, "t2 t3"), ("uint16", 128, "hu"), ("bfloat16", 2048, "x m"), ("bfloat16", 768, "mk"), ("float32", 136, "RM R2"),
+                       ("bfloat16", 136, "NQ"), ("float16", 128, "SP RR RD"), ("uint16", 8, "li")):
+        many(_d, _c, " ".join(n + _p for n in _l.split()))
+    for _n in ("k", "n", "o1", "o2"): SCRATCH["p" + _n + _p] = ("psum", [128, 512], "float32")
+for _t in range(RO):
+    many("uint16", 128, "hu0%d" % _t); many("bfloat16", 128, "mk0%d" % _t); many("float32", 128, "NC%d OA%d OB%d" % (_t, _t, _t))
+    sb("BL%d" % _t, [128, 8, 16]); sb("BR%d" % _t, [128, 8, 16])
+SHAPE.update({k: s[1] for k, s in SCRATCH.items()})
+PSUM = {k for k, s in SCRATCH.items() if s[0] == "psum"}
+WIDE.update({k: s[2] in ("float32", "int32") for k, s in SCRATCH.items()})
+
+
+def v(name, *idx):
+    sh = SHAPE[name]; reg = []; n = 1; full = list(idx) + [slice(None)] * (len(sh) - len(idx)); off = PLACE[name][1] if name in PLACE else 0
+    for i, (ix, d) in enumerate(zip(full, sh)):
+        if isinstance(ix, slice):
+            a, b, s = ix.indices(d); k = len(range(a, b, s)); reg.append((a, a + (k - 1) * s + 1, s))
+            if i: n *= k
+            if i == 1: full[i] = slice(a + off, a + off + (k - 1) * s + 1, s)
+        else:
+            reg.append((ix, ix + 1, 1))
+    return (name, tuple(full), tuple(reg), n)
+
+
+ALL = slice(None)
+
+
+def c(name, a=None, b=None, s=None): return v(name, ALL, slice(a, b, s))
+
+
+def row(name): return v(name, slice(0, 1), ALL)
+
+
+def ap(T, w): return T[PLACE[w[0]][0] if w[0] in PLACE else w[0]][w[1]]
+
+
+def overlap(r, q):
+    for (a, b, s), (d, e, u) in zip(r, q):
+        if a >= e or d >= b: return False
+        if s == u and s > 1 and (a - d) % s: return False
+    return True
+
+
+def covers(r, q): return all(s == 1 and a <= d and b >= e for (a, b, s), (d, e, u) in zip(r, q))
+
+
+def add(G, q, fn, R, W, dur, grp=None, sem=None):
+    i = len(G["ops"]); deps = {}
+    for w, isw in [(x, False) for x in R] + [(x, True) for x in W]:
+        name, reg = w[0], w[2]; keep = []
+        for e in G["acc"].get(name, ()):
+            j, r2, w2, g2 = e
+            if j == i: keep.append(e); continue
+            same = G["ops"][j]["q"] == q and q in QSEM; ov = overlap(reg, r2); hit = None
+            if name in PSUM and not same: hit = True
+            elif name in PSUM and q == "P":
+                if grp is None or grp != g2: hit = False
+            elif ov and (isw or w2): hit = True
+            if hit is not None: deps[j] = deps.get(j, False) or hit
+            if not (isw and ov and covers(reg, r2) and grp is None): keep.append(e)
+        keep.append((i, reg, isw, grp)); G["acc"][name] = keep
+    G["ops"].append({"q": q, "fn": fn, "deps": deps, "dur": dur, "sem": sem, "to": W[0][0] if W else ""})
+    return i
+
+
+VC = 0.00083
+
+
+def vcost(n, f): return max(64, n * f) * VC
+
+
+def two(*ws): return all(not WIDE[w[0]] for w in ws)
+
+
+def vtt(G, o, a, b, op):
+    add(G, "V", lambda g, T: g.vector.tensor_tensor(ap(T, o), ap(T, a), ap(T, b), op), [a, b], [o], vcost(o[3], 1 if (a[0] in PSUM or b[0] in PSUM) else 2))
+
+
+def vts(G, o, a, s1, op0, s2=None, op1=None):
+    def fn(g, T):
+        x = ap(T, s1) if isinstance(s1, tuple) else s1
+        if op1 is None: return g.vector.tensor_scalar(ap(T, o), ap(T, a), x, None, op0)
+        return g.vector.tensor_scalar(ap(T, o), ap(T, a), x, s2, op0, op1)
+    add(G, "V", fn, [a] + ([s1] if isinstance(s1, tuple) else []), [o], vcost(o[3], 0.5 if two(o, a) else 1))
+
+
+def vcp(G, o, a): add(G, "V", lambda g, T: g.vector.tensor_copy(ap(T, o), ap(T, a)), [a], [o], vcost(o[3], 0.5 if two(o, a) else 1))
+
+
+def vscan(G, o, a, b, op0, op1):
+    add(G, "V", lambda g, T: g.vector.tensor_tensor_scan(ap(T, o), ap(T, a), ap(T, b), 0.0, op0, op1), [a, b], [o], vcost(o[3], 0.5 if two(o, a, b) else 1))
+
+
+def vset(G, o, x): add(G, "V", lambda g, T: g.vector.memset(ap(T, o), x), [], [o], vcost(o[3], 1))
+
+
+def vgat(G, o, w, off):
+    add(G, "V", lambda g, T: g.vector.tensor_copy(ap(T, o), ap(T, w).indirect(ap(T, off))), [w, off], [o], o[3] * VC * 1.5 + 0.05)
+
+
+def act(G, o, a, func=F.Copy, bias=0.0, scale=1.0):
+    add(G, "S", lambda g, T: g.scalar.activation(ap(T, o), ap(T, a), func, bias=bias, scale=scale), [a], [o], o[3] * VC + 0.02)
+
+
+def gat(G, o, w, off):
+    add(G, "S", lambda g, T: g.scalar.activation(ap(T, o), ap(T, w).indirect(ap(T, off)), F.Copy), [w, off], [o], o[3] * VC * 1.5 + 0.065)
+
+
+def gather_all(G, x, hu):
+    n = 128 // NCH
+    for h in range(NCH): gat(G, c(x, 16 * n * h, 16 * n * (h + 1)), c("E"), c(hu, n * h, n * (h + 1)))
+
+
+def mm(G, o, l, r, start=True, stop=True, grp=None):
+    add(G, "P", lambda g, T: g.tensor.matmul(ap(T, o), ap(T, l), ap(T, r), start, stop), [l, r], [o], max(min(64, l[3]), r[3]) * (4 if WIDE[l[0]] else 1) * 0.0005, grp=grp)
+
+
+def group(G, o, terms):
+    for i, (l, r) in enumerate(terms): mm(G, o, l, r, i == 0, i == len(terms) - 1)
+
+
+def iota(G, o, pat, base, cm, small=True):
+    def fn(g, T):
+        if small: return g.iota(ap(T, o), pat, base, cm, allow_small_or_imprecise_dtypes=True)
+        return g.iota(ap(T, o), pat, base, cm)
+    add(G, "G", fn, [], [o], 0.13 + o[3] * 2 * VC)
+
+
+def dma(G, fn, R, W, dur):
+    k = "d%d" % G["nd"][0]; G["nd"][0] += 1; add(G, "Y", fn, R, W, dur, sem=(k, 16))
+
+
+LATER = {"mA": 2.0, "mB": 2.0, "mC": 2.0, "mkA": 2.0, "mkB": 2.0}
+
+
+def schedule(G):
+    ops = G["ops"]; n = len(ops); succ = [[] for _ in ops]; need = [0] * n
+    for i, o in enumerate(ops):
+        need[i] = len(o["deps"])
+        for d in o["deps"]: succ[d].append(i)
+
+    def lat(d, i): return 0.0 if not ops[i]["deps"][d] else (0.06 if ops[d]["q"] == ops[i]["q"] else 0.1)
+    far = [0.0] * n; pr = [0.0] * n
+    for i in range(n - 1, -1, -1):
+        far[i] = ops[i]["dur"] + max([far[s] + lat(i, s) for s in succ[i]] + [0.0]); pr[i] = far[i] - LATER.get(ops[i]["to"], 0.0)
+    free = {q: 0.0 for q in "VSPGYN"}; ready = {q: [] for q in free}; rt = [0.0] * n; order = []
+    for i in range(n):
+        if not need[i]: ready[ops[i]["q"]].append(i)
+    while len(order) < n:
+        best = None
+        for q in free:
+            if not ready[q]: continue
+            t0 = max(free[q], min(rt[i] for i in ready[q]))
+            i = max((j for j in ready[q] if rt[j] <= t0 + 1e-9), key=lambda j: (pr[j], -j))
+            if best is None or t0 < best[0]: best = (t0, i)
+        t0, i = best; q = ops[i]["q"]; ready[q].remove(i); order.append(i); end = t0 + ops[i]["dur"]; free[q] = end if q in QSEM else t0 + 0.1
+        for s in succ[i]:
+            rt[s] = max(rt[s], end + lat(i, s)); need[s] -= 1
+            if not need[s]: ready[ops[s]["q"]].append(s)
+        ops[i]["t"] = (t0, end)
+    return order
+
+
+def emit(G, order, g, T):
+    ops = G["ops"]; eng = {"V": g.vector, "S": g.scalar, "P": g.tensor, "G": g, "Y": g.sync}
+    clock = {q: {} for q in eng}; snap = {}; cnt = {q: 0 for q in QSEM}; done = {}
+    for i in order:
+        o = ops[i]; q = o["q"]
+        if q == "N": done[i] = o["sem"]; snap[i] = {}; continue
+        ck = clock[q]; want = {}
+        for d, w in o["deps"].items():
+            if w:
+                s, x = done[d]
+                if ck.get(s, 0) < x and want.get(s, (0, 0))[0] < x: want[s] = (x, d)
+        for s, (x, d) in sorted(want.items(), key=lambda z: -z[1][1]):
+            if ck.get(s, 0) >= x: continue
+            eng[q].wait_ge(T.sem[s], x); ck[s] = x
+            for s2, x2 in snap[d].items():
+                if ck.get(s2, 0) < x2: ck[s2] = x2
+        snap[i] = dict(ck); ins = o["fn"](g, T)
+        if o["sem"] is not None:
+            if q == "Y": ins.then_inc(T.sem[o["sem"][0]], o["sem"][1])
+            done[i] = o["sem"]
+        else:
+            cnt[q] += 1; ins.then_inc(T.sem[QSEM[q]], 1); done[i] = (QSEM[q], cnt[q])
+    for q in QSEM: g.wait_ge(T.sem[QSEM[q]], cnt[q])
+    for k in range(G["nd"][0]): g.wait_ge(T.sem["d%d" % k], 16)
+
+
+def constants(G):
+    iota(G, c("pci", 0, 1), [[0, 1]], 0, 1, False)
+    iota(G, c("CI"), [[1, 136]], 0, 0); iota(G, c("CG"), [[1, 8], [0, 16]], 0, 0); iota(G, c("CR"), [[0, 8], [1, 16]], 0, 0)
+    iota(G, c("S1"), [[0, 8], [1, 17]], -1, 0); iota(G, c("JX"), [[0, 8], [1, 36]], 0, 0); iota(G, c("IDT"), [[2, 1024]], 1, 0)
+    p = c("pci", 0, 1)
+    for k, (x, op) in enumerate(((15, O.bitwise_and), (4, O.arith_shift_right), (7, O.bitwise_and), (3, O.arith_shift_right))): vts(G, c("pci", k + 1, k + 2), p, x, op)
+    vcp(G, c("pcf", 0, 5), c("pci", 0, 5))
+    P, PR, PG, P8, PH = [c("pcf", k, k + 1) for k in range(5)]
+    vts(G, c("pcf", 5, 6), P, 1.0, O.add); vts(G, c("pcf", 6, 7), P, -1.0, O.add)
+    vtt(G, c("pcf", 7, 8), P, PG, O.add); vts(G, c("pcf", 7, 8), c("pcf", 7, 8), 1.0, O.add)
+    ci = c("CI", 0, 128); vts(G, c("If"), ci, P, O.is_equal); vts(G, c("Ib"), ci, P, O.is_equal)
+    for nm, x in (("Ih", 1.0), ("I64", 64.0), ("I296", 296.0), ("I296f", 296.0)): vts(G, c(nm), c("If"), x, O.mult)
+    for nm, x in (("nIb", -1.0), ("m4Ib", -4096.0), ("m64Ib", -64.0), ("m256Ib", -256.0), ("p4Ib", 4096.0)): vts(G, c(nm), c("Ib"), x, O.mult)
+    vts(G, c("PRE"), c("CI", 0, 16), PR, O.is_equal); vts(G, c("PHE"), c("CI", 0, 16), PH, O.is_equal)
+    ha, hb = c("half", 0, 1), c("half", 1, 2); vts(G, ha, PR, 7.5, O.is_le); vts(G, hb, PR, 7.5, O.is_ge)
+    vts(G, c("dA"), c("If"), ha, O.mult); vts(G, c("dB"), c("If"), hb, O.mult)
+    vts(G, c("Blk"), c("CG"), PG, O.is_equal); vts(G, c("EQG"), c("CG"), P8, O.is_equal); vts(G, c("Dm"), c("CR"), PR, O.is_equal)
+    vts(G, c("S01"), c("CR"), 0.0, O.not_equal); vts(G, c("CR0"), c("CR"), 0.0, O.is_equal)
+    vts(G, c("C8"), c("CI", 0, 8), PG, O.is_equal); vcp(G, c("C8h"), c("C8")); vts(G, c("B32"), c("C8"), 32.0, O.mult); vts(G, c("B16"), c("C8"), -16.0, O.mult)
+    vts(G, c("Pick"), c("C8"), c("PRE", 0, 1), O.mult)
+    vts(G, c("PermO"), c("CI"), c("pcf", 7, 8), O.is_equal); vts(G, c("BIGP"), c("PermO"), 262144.0, O.mult)
+    vts(G, c("BIGA"), c("BIGP"), ha, O.mult); vts(G, c("BIGB"), c("BIGP"), hb, O.mult)
+    vts(G, c("SEG"), c("S1"), -1.0, O.is_equal, 4194304.0, O.mult)
+    r = row
+    vts(G, r("T1"), r("S1"), -1.0, O.is_equal, 131073.0, O.mult); vtt(G, r("T1"), r("S1"), r("T1"), O.add); vcp(G, r("crN"), r("T1"))
+    vts(G, r("T3"), r("S1"), 7.5, O.is_ge, 262144.0, O.mult); vtt(G, r("crA"), r("T1"), r("T3"), O.add)
+    vts(G, r("T3"), r("S1"), 7.5, O.is_le, 262144.0, O.mult); vtt(G, r("T1"), r("T1"), r("T3"), O.add)
+    vts(G, r("T3"), r("S1"), -0.5, O.is_le, -262144.0, O.mult); vtt(G, r("crB"), r("T1"), r("T3"), O.add)
+    vset(G, row("one"), 1.0); vset(G, row("m296"), -296.0)
+    vts(G, c("SEGJ"), c("JX"), 0.0, O.is_equal, -4096.015625, O.mult); vts(G, c("SEGJ"), c("SEGJ"), 0.015625, O.add)
+    for j in range(6): vts(G, c("mcol", j, j + 1), PR, float(j), O.add)
+    for j in range(1, 6): vts(G, c("SelJ", 128 * (j - 1), 128 * j), c("Blk"), c("PRE", j, j + 1), O.mult)
+    for h in range(16): vts(G, c("SelT", 128 * h, 128 * h + 128), c("EQG"), c("PHE", h, h + 1), O.mult, 256.0, O.mult)
+    vts(G, c("ShB"), ci, c("pcf", 5, 6), O.is_equal); vtt(G, c("ShB"), c("ShB"), c("S01"), O.mult)
+    vts(G, c("ShA"), ci, c("pcf", 6, 7), O.is_equal); vtt(G, c("G0"), c("Blk"), c("CR0"), O.mult)
+    for p_ in "AB": vset(G, c("SP" + p_), 0.0)
+    vset(G, v("AL2"), 0.0); vset(G, v("EQ"), 0.0); vset(G, c("CT"), 0.0)
+    for t in range(RO): vset(G, v("BL%d" % t), 0.0)
+    vset(G, c("E", 4096, 4112), 0.0)
+    for p_ in "AB": mm(G, c("pk" + p_, 144, 272), c("Ib"), c("Dm"))
+
+
+def angles(G, p, n, P, Vp, hu):
+    t1, t2, t3 = c("t1" + p), c("t2" + p), c("t3" + p)
+    vtt(G, t1, n, P, O.mult); vtt(G, t2, t1, Vp, O.add); vts(G, t3, t2, 4, O.arith_shift_right, 4095, O.bitwise_and)
+    if hu is not None: vcp(G, hu, t3)
+
+
+def first(G, t):
+    sa, sb_ = c("stu", 8 * t, 8 * t + 8), c("sr%d" % t, 8 * t, 8 * t + 8); oa, ob, nc = c("OA%d" % t), c("OB%d" % t), c("NC%d" % t); b = "pnB"
+    gat(G, oa, c("IDT"), sa); gat(G, ob, c("IDT"), sb_); gat(G, c("tn0"), c("NBO"), sa); gat(G, c("tn1"), c("NBO"), sb_)
+    group(G, c(b, 0, 128), [(c("dA"), oa), (c("dB"), ob)]); group(G, c(b, 128, 256), [(c("dA"), c("tn0")), (c("dB"), c("tn1"))])
+    act(G, c("OSC"), c(b, 0, 128)); act(G, nc, c(b, 128, 256))
+    group(G, c(b, 256, 384), [(c("I296f"), c("OSC")), (row("one"), row("m296"))])
+    angles(G, "B", nc, c(b, 0, 128), c(b, 256, 384), c("hu0%d" % t)); vtt(G, c("mk0%d" % t), nc, c(b, 0, 128), O.is_equal)
+
+
+def slot(p, i): return c("po1" + p, 128 * i, 128 * i + 128) if i < 4 else c("po2" + p, 128 * i - 512, 128 * i - 384)
+
+
+def scores(G, p, a, t, xb, mb, ks):
+    gid = ("key", p, a, t); col = lambda k: c("pk" + p, k + 1, 136, 17); mx = lambda k: c(mb, 128 * k, 128 * k + 128)
+    mm(G, c("pk" + p, 0, 136), row("one"), row("crN") if a else row("cr" + p), True, False)
+    for l, r in [(c("mk" + p, 128 * i, 128 * i + 128), c("BIGP")) for i in range(a + 1)] if a else [(c("mk0%d" % t), c("BIG" + p))]:
+        mm(G, c("pk" + p, 0, 136), l, r, False, False, grp=gid)
+    for k in ks: mm(G, col(k), c(xb, k, 2048, 16), c("B16"), False, False, grp=gid)
+    for k in ks[:-1]: mm(G, col(k), mx(k), c("B32"), False, False, grp=gid)
+    mm(G, col(ks[-1]), mx(ks[-1]), c("B32"), False, True)
+
+
+def maxima(G, xb, mb, who):
+    n = 128 // NCH
+    for h in range(0, 128, n):
+        for k in range(16): vtt(G, c(mb, 128 * k + h, 128 * k + h + n), c(xb, 16 * h + k, 16 * (h + n), 16), c("po2" + who(k), 384 + h, 384 + h + n), O.max)
+
+
+def choose(G, p, a, t):
+    key = c("pk" + p, 0, 136); pn = c("pn" + p, 0, 136); R2 = c("R2" + p); RR = c("RR" + p); fin = c("R2" + p, 16, 136, 17)
+    vscan(G, c("RM" + p), c("SEG"), key, O.add, O.min); vtt(G, c("NQ" + p), c("RM" + p), key, O.not_equal)
+    mm(G, pn, c("m4Ib"), c("NQ" + p), False, True)
+    vscan(G, R2, c("NQ" + p), pn, O.mult, O.max)
+    if a < ST - 1:
+        vcp(G, c("SP" + p, 0, 128, 16), fin); vscan(G, RR, c("S01"), c("SP" + p), O.mult, O.add)
+        vtt(G, c("RD" + p), RR, c("pk" + p, 144, 272), O.mult)
+        mm(G, c("pk" + p, 136, 144), c("RD" + p), c("C8h")); vts(G, c("li" + p), c("pk" + p, 136, 144), 0.5, O.mult, -0.5, O.add)
+        mm(G, slot(p, a + 1), RR, c("Ih"))
+        group(G, c("po2" + p, 256, 384), [(RR, c("I296")), (row("one"), row("m296"))])
+    act(G, v("AL2" if p == "A" else "BL%d" % t, ALL, ALL, a + 1), fin)
+
+
+def names(G, p, a, t):
+    pn = c("pn" + p, 0, 136); s0 = c("pn" + p, 0, 136, 17)
+    mm(G, pn, c("n" + p) if a else c("NC%d" % t), c("PermO"), True, False)
+    if a: mm(G, s0, c("If"), c("R2" + p, 16, 136, 17), False, False)
+    else: mm(G, s0, c("O%s%d" % (p, t)), c("Pick"), False, False)
+
+
+def walk(G, t):
+    for p in "AB":
+        mm(G, c("po2" + p, 384, 512), c("Ib"), c("qa") if p == "A" else c("qr%d" % t)); mm(G, slot(p, 0), c("If"), c("O%s%d" % (p, t)))
+    mm(G, c("pnA", 144, 152), c("OA%d" % t), c("Pick")); act(G, v("AL2", ALL, ALL, 0), c("pnA", 144, 152))
+    for p in "AB": names(G, p, 0, t)
+    gather_all(G, "xC", "hu0%d" % t); maxima(G, "xC", "mC", lambda k: "A" if k < 8 else "B")
+    scores(G, "A", 0, t, "xC", "mC", list(range(8))); scores(G, "B", 0, t, "xC", "mC", list(range(8, 16)))
+    for p in "AB": choose(G, p, 0, t)
+    for a in range(1, ST):
+        for p in "AB":
+            vgat(G, c("n" + p), c("NBO"), c("li" + p))
+            angles(G, p, c("n" + p), slot(p, a - 1), c("po2" + p, 256, 384), c("hu" + p))
+            gather_all(G, "x" + p, "hu" + p); names(G, p, a, t)
+            for i in range(a + 1): vtt(G, c("mk" + p, 128 * i, 128 * i + 128), c("n" + p), slot(p, i), O.is_equal)
+            maxima(G, "x" + p, "m" + p, lambda k, p=p: p); scores(G, p, a, t, "x" + p, "m" + p, list(range(16))); choose(G, p, a, t)
+
+
+def rings(G, t):
+    al = lambda a, b: v("AL2", ALL, ALL, slice(a, b)); br = lambda a, b: v("BR%d" % t, ALL, ALL, slice(a, b))
+    for d in range(-5, 6):
+        i0 = max(1, 1 + d) if d else 2; i1 = min(6, 6 + d); n = i1 - i0 + 1; f0 = (i0 - 1) * 6 + i0 - d - 1
+        vtt(G, v("EQ", ALL, ALL, slice(f0, f0 + 7 * (n - 1) + 1, 7)), al(i0, i1 + 1), br(i0 - d, i1 - d + 1), O.is_equal)
+    mm(G, c("pnA", 0, 288), c("Ib"), v("EQ"))
+    vscan(G, c("FJ"), c("SEGJ"), c("pnA", 0, 288), O.add, O.max)
+    vcp(G, c("SPA", 0, 128, 16), c("FJ", 35, 288, 36)); vscan(G, c("RRA"), c("S01"), c("SPA"), O.mult, O.add)
+    y = c("pnB", 0, 128); mm(G, y, c("RRA"), c("I64"))
+    AL1, BL1 = c("po1B", 0, 128), c("po1B", 128, 256); mm(G, AL1, v("AL2"), c("If")); mm(G, BL1, v("BR%d" % t), c("If"))
+    vcp(G, c("BLs"), BL1); brep = [c("po2B", 128 * j, 128 * j + 128) for j in range(4)] + [c("po1B", 256, 384)]
+    for j in range(5): mm(G, brep[j], c("SelJ", 128 * j, 128 * j + 128), c("BLs"))
+    vts(G, c("IR"), y, -1.0 / 6, O.mult, 17.0 + 1.0 / 12, O.add); vts(G, c("TT"), c("IR"), -5.0, O.mult, 106.0, O.add)
+    vtt(G, c("LF"), c("TT"), y, O.subtract); vts(G, c("FN"), y, 63.5, O.is_ge); vtt(G, c("L0"), c("LF"), c("FN"), O.mult)
+    vts(G, c("L1"), c("L0"), -1.0, O.add); vtt(G, c("i0"), c("IR"), c("L1"), O.min)
+    m = lambda j: c("mcol", j, j + 1)
+    vts(G, c("MA"), c("i0"), m(0), O.is_ge); vts(G, c("MA64"), c("i0"), m(0), O.is_ge, 64.0, O.mult)
+    vtt(G, c("Lm"), c("L0"), c("MA64"), O.subtract); vts(G, c("MN"), c("L0"), m(0), O.is_le); vts(G, c("ML"), c("L0"), m(1), O.is_equal)
+    vtt(G, c("PB", 0, 128), c("MA"), AL1, O.mult)
+    for j in range(1, 6):
+        mb = c("MB", 128 * j - 128, 128 * j); vts(G, mb, c("Lm"), m(j), O.is_equal); vtt(G, c("PB", 128 * j, 128 * j + 128), mb, brep[j - 1], O.mult)
+    CP = c("pkB", 0, 128)
+    group(G, CP, [(c("nIb"), c("MN"))] + [(c("Ih"), c("PB", 128 * j, 128 * j + 128)) for j in range(6)])
+    vcp(G, c("CS"), CP); act(G, c("YR", 128 * t, 128 * t + 128), CP, F.Identity, -0.5, 0.5)
+    vtt(G, c("PL"), c("ML"), CP, O.mult); vtt(G, c("PA0"), c("ML"), slot("A", 0), O.mult)
+    BP, AP, VP, NN = [c("pnA", 128 * j, 128 * j + 128) for j in range(4)]
+    group(G, NN, [(c("p4Ib"), c("MN"))]); group(G, VP, [(c("I296"), c("CS")), (row("one"), row("m296"))])
+    group(G, AP, [(c("Ih"), c("PA0")), (c("Ib"), c("ML")), (c("ShA"), c("CS"))]); group(G, BP, [(c("ShB"), c("CS")), (c("G0"), c("PL"))])
+    act(G, c("APs"), AP)
+    angles(G, "A", c("APs"), BP, VP, None); vtt(G, c("HF"), c("t3A"), NN, O.max); vcp(G, c("huA"), c("HF"))
+    gather_all(G, "xA", "huA")
+    vts(G, c("hiB"), c("HF"), 1.0 / 64, O.mult, 129.0 - 63.0 / 128, O.add)
+    LO = c("pkB", 272, 400); group(G, LO, [(c("HF"), c("If")), (c("hiB"), c("m64Ib"))]); vts(G, c("LOT"), LO, 8256.0, O.add)
+    for u in range(64): vts(G, c("OHL", 128 * u, 128 * u + 128), c("LOT"), float(u), O.is_equal)
+    tot = c("pnB", 128, 256); group(G, tot, [(c("Ib"), c("xA", k, 2048, 16)) for k in range(12)])
+    vts(G, c("TH"), tot, c("thf"), O.is_ge); cnt = c("pnB", 256, 384); mm(G, cnt, c("Blk"), c("TH")); vts(G, c("NH"), cnt, 8.5, O.is_le)
+    HI = c("po1B", 384, 512); group(G, HI, [(c("hiB"), c("Ib")), (c("MN"), c("m256Ib")), (c("NH"), c("m256Ib"))]); act(G, c("HIT"), HI, F.Identity, -129.0)
+
+
+def lessen(G, t):
+    for u in range(64):
+        o = c("THH", 128 * u, 128 * u + 128)
+        if u < NTS: act(G, o, c("HIT"), F.Sigmoid, -200.0 * (u - 0.5), 200.0)
+        else: vts(G, o, c("HIT"), float(u), O.is_ge)
+    lo64 = slice(0, 64)
+    for g in range(8): group(G, v("po2A", lo64, slice(g, 512, 8)), [(c("OHL", 16 * g + m, 8192, 128), c("THH", 16 * g + m, 8192, 128)) for m in range(12)])
+    pc = v("po2A", lo64, slice(0, 512)); act(G, v("CT", lo64, slice(0, 512)), pc); vtt(G, v("NM", lo64, ALL), v("CT", lo64, slice(8, 520)), pc, O.is_equal)
+    for b in range(4): mm(G, c("pnA", 64 * b, 64 * b + 64), v("NM", lo64, slice(128 * b, 128 * b + 128)), v("Ib", lo64, slice(0, 64)))
+    act(G, c("NM2"), c("pnA", 0, 256), F.Identity, 0.5, 2.0)
+    for k in range(8):
+        bank = ("po2B", "pnB", "po1A", "pkA", "po1B")[k % 5]; e = c("E", 512 * k, 512 * k + 512); o = c(bank, 0, 512); b = k // 2
+        mm(G, o, c("Ib"), e, True, False); mm(G, o, c("nIb"), c("G4", 512 * k, 512 * k + 512), False, False)
+        for h in range(8):
+            s = 128 * ((k % 2) * 8 + h); mm(G, c(bank, 64 * h, 64 * h + 64), c("SelT", s, s + 128), c("NM2", 64 * b, 64 * b + 64), False, h == 7)
+        vtt(G, e, e, o, O.min)
+        if t == RO - 1 and k % 2:
+            a = 512 * (k - 1); dma(G, lambda g, T, a=a: g.sync.dma_start(T.ye[:, a:a + 1024], T.E[:, a:a + 1024]), [c("E", a, a + 1024)], [], 3.5)
+    if t < RO - 1:
+        quarter(G); mm(G, c("pkA", 144, 272), c("Ib"), c("Dm"))
+
+
+def quarter(G):
+    for k in range(8): act(G, c("G4", 512 * k, 512 * k + 512), c("E", 512 * k, 512 * k + 512), F.Identity, 127.625, 0.25)
+
+
+def build(rank, core, topo):
+    G = {"ops": [], "acc": {}, "nd": [0]}; peers = [(rank + 1 + t) % N for t in range(RO)]; asks = [(rank - 1 - t) % N for t in range(RO)]; ne = 8
+
+    def eng(T, dst):
+        m = 0
+        for e in topo.engines(core, T.cores[dst])[:ne]: m |= 1 << e
+        return m
+
+    def did(T, dst):
+        a = topo.addr(T.cores[dst]); return DstId(rid=a[0], pnc=a[1])
+
+    def send3(src, dsts, sem):
+        def fn(g, T):
+            return g.remote_dma_fused([RemoteDMATransfer(dst_ids=[did(T, s) for s in peers], dma_engine_mask=eng(T, peers[0]), remote_sem=T.sem[sem],
+                                                         srcs=[T[src][:]], dsts=[T[d][:] for d in dsts], alu_op=0)], local_sem=T.sem.loc)
+        return fn
+    dma(G, lambda g, T: g.sync.dma_start(T.sti[:], T.st[:]), [], [c("sti")], 2.0)
+    dma(G, lambda g, T: g.sync.dma_start(T.qa[:], T.q[:]), [], [c("qa")], 2.0)
+    dma(G, lambda g, T: g.sync.dma_start(T.nbi[:], T.nb[:]), [], [c("nbi")], 4.0)
+    dma(G, lambda g, T: g.sync.dma_start(T.E[:, 0:4096], T.ang[:]), [], [c("E", 0, 4096)], 8.0)
+    dma(G, lambda g, T: g.sync.dma_start(T.thi[:], T.th[:]), [], [c("thi")], 2.0)
+    vcp(G, c("stu"), c("sti"))
+    s1 = add(G, "G", send3("stu", ["sr0", "sr1", "sr2"], "as0"), [c("stu")], [], 1.0, sem=("loc", 0))
+    s2 = add(G, "G", send3("qa", ["qr0", "qr1", "qr2"], "aq"), [c("qa")], [], 1.0, sem=("loc", 0))
+    for s, nm, sem in ((s1, "sr", "as0"), (s2, "qr", "aq")):
+        i = add(G, "N", None, [], [c(nm + "%d" % t) for t in range(RO)], 3.0, sem=(sem, 3 * ne)); G["ops"][i]["deps"][s] = False
+    constants(G)
+    vts(G, c("NBO"), c("nbi"), 2.0, O.mult, 1.0, O.add); vcp(G, c("thf"), c("thi"))
+    first(G, 0); quarter(G)
+    for t in range(RO):
+        walk(G, t)
+
+        def back(g, T, t=t):
+            a = topo.addr(T.cores[asks[t]])
+            return g.remote_dma(T["BR%d" % t][:], T["BL%d" % t][:], T.sem["ar%d" % t], T.sem.loc, a[1], a[0], eng(T, asks[t]))
+        s = add(G, "G", back, [v("BL%d" % t)], [], 0.5, sem=("loc", 0))
+        i = add(G, "N", None, [], [v("BR%d" % t)], 2.5, sem=("ar%d" % t, ne)); G["ops"][i]["deps"][s] = False
+        if t < RO - 1: first(G, t + 1)
+        rings(G, t); lessen(G, t)
+    dma(G, lambda g, T: g.sync.dma_start(T.yr[:], ap(T, c("YR"))), [c("YR")], [], 3.0)
+    return G, ne
+
+
+def rank_program(g, core, T, topo):
+    rank = T.rank_of(core)
+    if rank is None: return
+    G, ne = build(rank, core, topo); emit(G, schedule(G), g, T)
+    g.wait_ge(T.sem.loc, ne * (2 + RO))

@@ -1,13 +1,14 @@
 from concourse.bass import DstId, RemoteDMATransfer
 from concourse.mybir import AluOpType as O, ActivationFunctionType as F
 
-N, RO, ST, NCH = 4, 3, 6, 2
-NTS = 19
+N, RO, ST = 4, 3, 6
+CHUNKS = (0, 48, 96, 128)
+RCHUNKS = (0, 64, 128)
 SCRATCH, SHAPE, WIDE, PLACE = {}, {}, {}, {}
-SEMAPHORES = ["sv", "ss", "sp", "sg", "as0", "aq", "ar0", "ar1", "ar2", "loc"] + ["d%d" % i for i in range(16)]
+SEMAPHORES = ["sv", "ss", "sp", "sg", "as0", "aq", "ar0", "ar1", "ar2", "loc"] + ["d%d" % i for i in range(20)]
 QSEM = {"V": "sv", "S": "ss", "P": "sp", "G": "sg"}
 POOL = {"float32": "poolf", "bfloat16": "poolb", "float16": "poolh", "int32": "pooli", "uint16": "poolu"}
-APART = "stu sr0 sr1 sr2 qa qr0 qr1 qr2 sti thi".split()
+APART = "stu sr0 sr1 sr2 qa qr0 qr1 qr2 sti thi CH0 CH1 CH2 BL0 BL1 BL2 YR".split()
 
 
 def sb(name, shape, dtype="float32"):
@@ -16,29 +17,30 @@ def sb(name, shape, dtype="float32"):
 
 def many(dtype, cols, names):
     for n in names.split():
-        if cols > 768 or n in APART: sb(n, [128, cols], dtype); continue
+        if cols > 816 or n in APART: sb(n, [128, cols], dtype); continue
         pool = SCRATCH.setdefault(POOL[dtype], ("sbuf", [128, 0], dtype)); PLACE[n] = (POOL[dtype], pool[1][1]); SHAPE[n] = [128, cols]; WIDE[n] = dtype in ("float32", "int32")
         pool[1][1] += -(-cols // 32) * 32
 
 
-many("int32", 1024, "nbi"); many("float32", 1024, "NBO IDT"); many("bfloat16", 4112, "E"); many("bfloat16", 4096, "G4")
+many("int32", 1024, "nbi"); many("float32", 1024, "NB IDT"); many("bfloat16", 4112, "E"); many("float16", 4096, "L16")
 many("bfloat16", 128, "qa qr0 qr1 qr2"); many("int32", 24, "sti"); many("uint16", 24, "stu sr0 sr1 sr2"); many("int32", 1, "thi"); many("float32", 1, "thf")
-many("int32", 8, "pci"); many("float32", 8, "pcf C8 Pick mcol"); many("float16", 8, "C8h"); many("bfloat16", 8, "B32 B16")
-many("float32", 136, "CI S1 PermO SEG T1 T3"); many("bfloat16", 136, "BIGP BIGA BIGB crN crA crB"); many("float32", 128, "CG CR If I296f dA dB"); many("float32", 288, "JX SEGJ")
-many("float16", 128, "Ih I64 I296 ShB ShA G0"); many("bfloat16", 128, "one m296 Ib nIb m4Ib m64Ib m256Ib p4Ib Blk EQG Dm S01 CR0")
-many("float32", 16, "PHE PRE"); many("float32", 2, "half"); many("float16", 640, "SelJ"); many("bfloat16", 2048, "SelT")
-many("bfloat16", 2048, "xC mC"); many("float32", 128, "tn0 tn1 OSC")
-sb("AL2", [128, 8, 16]); sb("EQ", [128, 8, 36], "bfloat16"); many("float32", 288, "FJ"); many("float16", 128, "BLs PL PA0 CS"); many("int32", 128, "IR")
-many("float32", 128, "TT LF APs HF"); many("bfloat16", 128, "FN L0 L1 i0 MA MA64 Lm MN ML hiB TH NH LOT HIT"); many("bfloat16", 640, "MB"); many("float16", 768, "PB")
-many("bfloat16", 8192, "OHL THH"); many("float32", 520, "CT"); many("bfloat16", 512, "NM"); many("bfloat16", 256, "NM2"); many("float32", 384, "YR")
+many("int32", 4, "pci"); many("float32", 12, "pcf"); many("float32", 136, "CI S1 GC TK"); many("float32", 128, "CR"); many("float32", 16, "G16"); many("float32", 272, "SEG")
+many("bfloat16", 128, "Ib I4 I592 dA dB dA4 dB4 Dm S01 one"); many("float16", 128, "I2050 dA26 dB26"); many("float16", 256, "cq")
+many("bfloat16", 272, "Perm BIGP WN"); many("bfloat16", 136, "nPerm"); many("bfloat16", 816, "cr"); many("bfloat16", 16, "BX BM"); many("bfloat16", 8, "C8 Pick")
+many("bfloat16", 288, "Zb DC BlkC DC2"); many("float16", 288, "Zh DJ"); many("float32", 128, "Zf Dmf"); many("float32", 16, "R1 R2 col")
+many("bfloat16", 128, "CN CQ1 CV1a CV1b CV2 SA SA592 SB4 S06 PZ PI PD AR I16 m4I p4I nI"); many("float16", 128, "CQ2 SB2050"); many("bfloat16", 640, "BRL")
+many("float32", 96, "Cmpf"); many("bfloat16", 96, "Cmp Cmp64 Cmp256"); many("bfloat16", 2048, "SelT")
+many("float16", 128, "CT SPJ RRJ Y1 Y2 NS tnA tnB"); many("float16", 288, "EQ"); many("float32", 288, "FJ"); many("bfloat16", 128, "OH dead hiB TH Zs r1 r2"); many("float32", 128, "HF")
+many("bfloat16", 192, "LOT"); many("bfloat16", 288, "HI0 HIT"); many("bfloat16", 6144, "OHL"); many("bfloat16", 3168, "THH0 THH1"); many("float16", 264, "CN0 CN1")
+many("bfloat16", 256, "NM"); many("bfloat16", 640, "ZL"); many("float16", 768, "PB"); many("float32", 384, "YR")
 for _p in "AB":
-    for _d, _c, _l in (("float32", 128, "n t1"), ("int32", 128, "t2 t3"), ("uint16", 128, "hu"), ("bfloat16", 2048, "x m"), ("bfloat16", 768, "mk"), ("float32", 136, "RM R2"),
-                       ("bfloat16", 136, "NQ"), ("float16", 128, "SP RR RD"), ("uint16", 8, "li")):
+    for _d, _c, _l in (("float16", 128, "n wr SP RR0 RR1 RD"), ("float32", 128, "t1"), ("int32", 128, "t2 t3"), ("uint16", 128, "hu"), ("bfloat16", 2048, "x m"), ("bfloat16", 768, "mk"),
+                       ("float32", 272, "RM"), ("uint16", 8, "li")):
         many(_d, _c, " ".join(n + _p for n in _l.split()))
-    for _n in ("k", "n", "o1", "o2"): SCRATCH["p" + _n + _p] = ("psum", [128, 512], "float32")
+    for _n in ("k", "w", "o1", "o2"): SCRATCH["p" + _n + _p] = ("psum", [128, 512], "float32")
 for _t in range(RO):
-    many("uint16", 128, "hu0%d" % _t); many("bfloat16", 128, "mk0%d" % _t); many("float32", 128, "NC%d OA%d OB%d" % (_t, _t, _t))
-    sb("BL%d" % _t, [128, 8, 16]); sb("BR%d" % _t, [128, 8, 16])
+    many("uint16", 128, "hu0%d" % _t); many("bfloat16", 128, "mk0%d" % _t); many("float16", 128, "NC%d wr0%d OA%d OB%d" % (_t, _t, _t, _t))
+    many("float16", 104, "CH%d" % _t); many("float16", 48, "BL%d" % _t)
 SHAPE.update({k: s[1] for k, s in SCRATCH.items()})
 PSUM = {k for k, s in SCRATCH.items() if s[0] == "psum"}
 WIDE.update({k: s[2] in ("float32", "int32") for k, s in SCRATCH.items()})
@@ -47,12 +49,9 @@ WIDE.update({k: s[2] in ("float32", "int32") for k, s in SCRATCH.items()})
 def v(name, *idx):
     sh = SHAPE[name]; reg = []; n = 1; full = list(idx) + [slice(None)] * (len(sh) - len(idx)); off = PLACE[name][1] if name in PLACE else 0
     for i, (ix, d) in enumerate(zip(full, sh)):
-        if isinstance(ix, slice):
-            a, b, s = ix.indices(d); k = len(range(a, b, s)); reg.append((a, a + (k - 1) * s + 1, s))
-            if i: n *= k
-            if i == 1: full[i] = slice(a + off, a + off + (k - 1) * s + 1, s)
-        else:
-            reg.append((ix, ix + 1, 1))
+        a, b, s = ix.indices(d); k = len(range(a, b, s)); reg.append((a, a + (k - 1) * s + 1, s))
+        if i: n *= k
+        if i == 1: full[i] = slice(a + off, a + off + (k - 1) * s + 1, s)
     return (name, tuple(full), tuple(reg), n)
 
 
@@ -62,7 +61,7 @@ ALL = slice(None)
 def c(name, a=None, b=None, s=None): return v(name, ALL, slice(a, b, s))
 
 
-def row(name): return v(name, slice(0, 1), ALL)
+def pc(name, p0, p1, a=None, b=None, s=None): return v(name, slice(p0, p1), slice(a, b, s))
 
 
 def ap(T, w): return T[PLACE[w[0]][0] if w[0] in PLACE else w[0]][w[1]]
@@ -71,33 +70,38 @@ def ap(T, w): return T[PLACE[w[0]][0] if w[0] in PLACE else w[0]][w[1]]
 def overlap(r, q):
     for (a, b, s), (d, e, u) in zip(r, q):
         if a >= e or d >= b: return False
-        if s == u and s > 1 and (a - d) % s: return False
+        if s > 1 and u > 1 and (s % u == 0 or u % s == 0) and (a - d) % min(s, u): return False
     return True
 
 
-def covers(r, q): return all(s == 1 and a <= d and b >= e for (a, b, s), (d, e, u) in zip(r, q))
+def covers(r, q): return all(s == 1 and a <= d and b >= e for (a, b, s), (d, e, u) in zip(r, q)) or r == q
 
 
-def add(G, q, fn, R, W, dur, grp=None, sem=None):
+def add(G, q, fn, R, W, dur, grp=None, sem=None, gn=0):
     i = len(G["ops"]); deps = {}
     for w, isw in [(x, False) for x in R] + [(x, True) for x in W]:
         name, reg = w[0], w[2]; keep = []
+        if name in PSUM:
+            who, was, now = G["acc"].get(name, (q, [], []))
+            if who != q: was, now = [j for j, g2 in now], []
+            for j in was: deps[j] = True
+            if q == "P":
+                for j, g2 in now:
+                    if j != i and (grp is None or grp != g2): deps.setdefault(j, False)
+                if grp is None: now = []
+            G["acc"][name] = (q, was, now + [(i, grp)]); continue
         for e in G["acc"].get(name, ()):
             j, r2, w2, g2 = e
             if j == i: keep.append(e); continue
-            same = G["ops"][j]["q"] == q and q in QSEM; ov = overlap(reg, r2); hit = None
-            if name in PSUM and not same: hit = True
-            elif name in PSUM and q == "P":
-                if grp is None or grp != g2: hit = False
-            elif ov and (isw or w2): hit = True
-            if hit is not None: deps[j] = deps.get(j, False) or hit
-            if not (isw and ov and covers(reg, r2) and grp is None): keep.append(e)
+            ov = overlap(reg, r2)
+            if ov and (isw or w2): deps[j] = True
+            if not (isw and ov and covers(reg, r2)): keep.append(e)
         keep.append((i, reg, isw, grp)); G["acc"][name] = keep
-    G["ops"].append({"q": q, "fn": fn, "deps": deps, "dur": dur, "sem": sem, "to": W[0][0] if W else ""})
+    G["ops"].append({"q": q, "fn": fn, "deps": deps, "dur": dur, "sem": sem, "to": W[0][0] if W else "", "gn": gn, "late": G["late"][0]})
     return i
 
 
-VC = 0.00083
+VC, GR, PC = 0.00083, 1.56, 0.00042
 
 
 def vcost(n, f): return max(64, n * f) * VC
@@ -106,16 +110,21 @@ def vcost(n, f): return max(64, n * f) * VC
 def two(*ws): return all(not WIDE[w[0]] for w in ws)
 
 
+def num(T, x): return ap(T, x) if isinstance(x, tuple) else x
+
+
+def cols(*xs): return [x for x in xs if isinstance(x, tuple)]
+
+
 def vtt(G, o, a, b, op):
     add(G, "V", lambda g, T: g.vector.tensor_tensor(ap(T, o), ap(T, a), ap(T, b), op), [a, b], [o], vcost(o[3], 1 if (a[0] in PSUM or b[0] in PSUM) else 2))
 
 
 def vts(G, o, a, s1, op0, s2=None, op1=None):
     def fn(g, T):
-        x = ap(T, s1) if isinstance(s1, tuple) else s1
-        if op1 is None: return g.vector.tensor_scalar(ap(T, o), ap(T, a), x, None, op0)
-        return g.vector.tensor_scalar(ap(T, o), ap(T, a), x, s2, op0, op1)
-    add(G, "V", fn, [a] + ([s1] if isinstance(s1, tuple) else []), [o], vcost(o[3], 0.5 if two(o, a) else 1))
+        if op1 is None: return g.vector.tensor_scalar(ap(T, o), ap(T, a), num(T, s1), None, op0)
+        return g.vector.tensor_scalar(ap(T, o), ap(T, a), num(T, s1), num(T, s2), op0, op1)
+    add(G, "V", fn, [a] + cols(s1, s2), [o], vcost(o[3], 0.5 if two(o, a) else 1))
 
 
 def vcp(G, o, a): add(G, "V", lambda g, T: g.vector.tensor_copy(ap(T, o), ap(T, a)), [a], [o], vcost(o[3], 0.5 if two(o, a) else 1))
@@ -125,28 +134,23 @@ def vscan(G, o, a, b, op0, op1):
     add(G, "V", lambda g, T: g.vector.tensor_tensor_scan(ap(T, o), ap(T, a), ap(T, b), 0.0, op0, op1), [a, b], [o], vcost(o[3], 0.5 if two(o, a, b) else 1))
 
 
-def vset(G, o, x): add(G, "V", lambda g, T: g.vector.memset(ap(T, o), x), [], [o], vcost(o[3], 1))
+def vset(G, o, x): add(G, "V", lambda g, T: g.vector.memset(ap(T, o), x), [], [o], vcost(o[3], 0.5 if two(o) else 1))
 
 
 def vgat(G, o, w, off):
-    add(G, "V", lambda g, T: g.vector.tensor_copy(ap(T, o), ap(T, w).indirect(ap(T, off))), [w, off], [o], o[3] * VC * 1.5 + 0.05)
+    add(G, "V", lambda g, T: g.vector.tensor_copy(ap(T, o), ap(T, w).indirect(ap(T, off))), [w, off], [o], o[3] * VC * GR + 0.05, gn=o[3])
 
 
 def act(G, o, a, func=F.Copy, bias=0.0, scale=1.0):
-    add(G, "S", lambda g, T: g.scalar.activation(ap(T, o), ap(T, a), func, bias=bias, scale=scale), [a], [o], o[3] * VC + 0.02)
+    return add(G, "S", lambda g, T: g.scalar.activation(ap(T, o), ap(T, a), func, bias=num(T, bias), scale=scale), [a] + cols(bias), [o], max(64, o[3]) * VC + 0.02)
 
 
 def gat(G, o, w, off):
-    add(G, "S", lambda g, T: g.scalar.activation(ap(T, o), ap(T, w).indirect(ap(T, off)), F.Copy), [w, off], [o], o[3] * VC * 1.5 + 0.065)
-
-
-def gather_all(G, x, hu):
-    n = 128 // NCH
-    for h in range(NCH): gat(G, c(x, 16 * n * h, 16 * n * (h + 1)), c("E"), c(hu, n * h, n * (h + 1)))
+    return add(G, "S", lambda g, T: g.scalar.activation(ap(T, o), ap(T, w).indirect(ap(T, off)), F.Copy), [w, off], [o], o[3] * VC * GR + 0.065, gn=o[3])
 
 
 def mm(G, o, l, r, start=True, stop=True, grp=None):
-    add(G, "P", lambda g, T: g.tensor.matmul(ap(T, o), ap(T, l), ap(T, r), start, stop), [l, r], [o], max(min(64, l[3]), r[3]) * (4 if WIDE[l[0]] else 1) * 0.0005, grp=grp)
+    add(G, "P", lambda g, T: g.tensor.matmul(ap(T, o), ap(T, l), ap(T, r), start, stop), [l, r], [o], max(min(64, l[3]), r[3]) * (4 if WIDE[l[0]] else 1) * PC, grp=grp)
 
 
 def group(G, o, terms):
@@ -160,11 +164,15 @@ def iota(G, o, pat, base, cm, small=True):
     add(G, "G", fn, [], [o], 0.13 + o[3] * 2 * VC)
 
 
+def sel(G, o, a, pat, op, fill, base, cm=1):
+    add(G, "G", lambda g, T: g.affine_select(ap(T, o), ap(T, a), pat, op, float(fill), base, cm), [a], [o], 0.17 + o[3] * 2 * VC)
+
+
 def dma(G, fn, R, W, dur):
     k = "d%d" % G["nd"][0]; G["nd"][0] += 1; add(G, "Y", fn, R, W, dur, sem=(k, 16))
 
 
-LATER = {"mA": 2.0, "mB": 2.0, "mC": 2.0, "mkA": 2.0, "mkB": 2.0}
+LATER = {"mA": 2.0, "mB": 2.0, "mkA": 2.0, "mkB": 2.0, "wrA": 2.0, "wrB": 2.0}
 
 
 def schedule(G):
@@ -176,7 +184,7 @@ def schedule(G):
     def lat(d, i): return 0.0 if not ops[i]["deps"][d] else (0.06 if ops[d]["q"] == ops[i]["q"] else 0.1)
     far = [0.0] * n; pr = [0.0] * n
     for i in range(n - 1, -1, -1):
-        far[i] = ops[i]["dur"] + max([far[s] + lat(i, s) for s in succ[i]] + [0.0]); pr[i] = far[i] - LATER.get(ops[i]["to"], 0.0)
+        far[i] = ops[i]["dur"] + max([far[s] + lat(i, s) for s in succ[i]] + [0.0]); pr[i] = far[i] - LATER.get(ops[i]["to"], 0.0) - ops[i]["late"]
     free = {q: 0.0 for q in "VSPGYN"}; ready = {q: [] for q in free}; rt = [0.0] * n; order = []
     for i in range(n):
         if not need[i]: ready[ops[i]["q"]].append(i)
@@ -221,187 +229,229 @@ def emit(G, order, g, T):
     for k in range(G["nd"][0]): g.wait_ge(T.sem["d%d" % k], 16)
 
 
-def constants(G):
+def walk_constants(G):
     iota(G, c("pci", 0, 1), [[0, 1]], 0, 1, False)
-    iota(G, c("CI"), [[1, 136]], 0, 0); iota(G, c("CG"), [[1, 8], [0, 16]], 0, 0); iota(G, c("CR"), [[0, 8], [1, 16]], 0, 0)
-    iota(G, c("S1"), [[0, 8], [1, 17]], -1, 0); iota(G, c("JX"), [[0, 8], [1, 36]], 0, 0); iota(G, c("IDT"), [[2, 1024]], 1, 0)
-    p = c("pci", 0, 1)
-    for k, (x, op) in enumerate(((15, O.bitwise_and), (4, O.arith_shift_right), (7, O.bitwise_and), (3, O.arith_shift_right))): vts(G, c("pci", k + 1, k + 2), p, x, op)
-    vcp(G, c("pcf", 0, 5), c("pci", 0, 5))
-    P, PR, PG, P8, PH = [c("pcf", k, k + 1) for k in range(5)]
-    vts(G, c("pcf", 5, 6), P, 1.0, O.add); vts(G, c("pcf", 6, 7), P, -1.0, O.add)
-    vtt(G, c("pcf", 7, 8), P, PG, O.add); vts(G, c("pcf", 7, 8), c("pcf", 7, 8), 1.0, O.add)
-    ci = c("CI", 0, 128); vts(G, c("If"), ci, P, O.is_equal); vts(G, c("Ib"), ci, P, O.is_equal)
-    for nm, x in (("Ih", 1.0), ("I64", 64.0), ("I296", 296.0), ("I296f", 296.0)): vts(G, c(nm), c("If"), x, O.mult)
-    for nm, x in (("nIb", -1.0), ("m4Ib", -4096.0), ("m64Ib", -64.0), ("m256Ib", -256.0), ("p4Ib", 4096.0)): vts(G, c(nm), c("Ib"), x, O.mult)
-    vts(G, c("PRE"), c("CI", 0, 16), PR, O.is_equal); vts(G, c("PHE"), c("CI", 0, 16), PH, O.is_equal)
-    ha, hb = c("half", 0, 1), c("half", 1, 2); vts(G, ha, PR, 7.5, O.is_le); vts(G, hb, PR, 7.5, O.is_ge)
-    vts(G, c("dA"), c("If"), ha, O.mult); vts(G, c("dB"), c("If"), hb, O.mult)
-    vts(G, c("Blk"), c("CG"), PG, O.is_equal); vts(G, c("EQG"), c("CG"), P8, O.is_equal); vts(G, c("Dm"), c("CR"), PR, O.is_equal)
-    vts(G, c("S01"), c("CR"), 0.0, O.not_equal); vts(G, c("CR0"), c("CR"), 0.0, O.is_equal)
-    vts(G, c("C8"), c("CI", 0, 8), PG, O.is_equal); vcp(G, c("C8h"), c("C8")); vts(G, c("B32"), c("C8"), 32.0, O.mult); vts(G, c("B16"), c("C8"), -16.0, O.mult)
-    vts(G, c("Pick"), c("C8"), c("PRE", 0, 1), O.mult)
-    vts(G, c("PermO"), c("CI"), c("pcf", 7, 8), O.is_equal); vts(G, c("BIGP"), c("PermO"), 262144.0, O.mult)
-    vts(G, c("BIGA"), c("BIGP"), ha, O.mult); vts(G, c("BIGB"), c("BIGP"), hb, O.mult)
-    vts(G, c("SEG"), c("S1"), -1.0, O.is_equal, 4194304.0, O.mult)
-    r = row
-    vts(G, r("T1"), r("S1"), -1.0, O.is_equal, 131073.0, O.mult); vtt(G, r("T1"), r("S1"), r("T1"), O.add); vcp(G, r("crN"), r("T1"))
-    vts(G, r("T3"), r("S1"), 7.5, O.is_ge, 262144.0, O.mult); vtt(G, r("crA"), r("T1"), r("T3"), O.add)
-    vts(G, r("T3"), r("S1"), 7.5, O.is_le, 262144.0, O.mult); vtt(G, r("T1"), r("T1"), r("T3"), O.add)
-    vts(G, r("T3"), r("S1"), -0.5, O.is_le, -262144.0, O.mult); vtt(G, r("crB"), r("T1"), r("T3"), O.add)
-    vset(G, row("one"), 1.0); vset(G, row("m296"), -296.0)
-    vts(G, c("SEGJ"), c("JX"), 0.0, O.is_equal, -4096.015625, O.mult); vts(G, c("SEGJ"), c("SEGJ"), 0.015625, O.add)
-    for j in range(6): vts(G, c("mcol", j, j + 1), PR, float(j), O.add)
-    for j in range(1, 6): vts(G, c("SelJ", 128 * (j - 1), 128 * j), c("Blk"), c("PRE", j, j + 1), O.mult)
-    for h in range(16): vts(G, c("SelT", 128 * h, 128 * h + 128), c("EQG"), c("PHE", h, h + 1), O.mult, 256.0, O.mult)
-    vts(G, c("ShB"), ci, c("pcf", 5, 6), O.is_equal); vtt(G, c("ShB"), c("ShB"), c("S01"), O.mult)
-    vts(G, c("ShA"), ci, c("pcf", 6, 7), O.is_equal); vtt(G, c("G0"), c("Blk"), c("CR0"), O.mult)
-    for p_ in "AB": vset(G, c("SP" + p_), 0.0)
-    vset(G, v("AL2"), 0.0); vset(G, v("EQ"), 0.0); vset(G, c("CT"), 0.0)
-    for t in range(RO): vset(G, v("BL%d" % t), 0.0)
+    iota(G, c("CI"), [[1, 136]], 0, 0); iota(G, c("IDT"), [[1, 1024]], -512, 0); iota(G, c("G16"), [[0, 2], [1, 8]], 0, 0)
+    iota(G, c("CR"), [[0, 8], [1, 16]], 0, 0); iota(G, c("S1"), [[0, 8], [1, 17]], -1, 0); iota(G, c("GC"), [[1, 8], [0, 17]], 0, 0)
+    p = c("pci", 0, 1); vts(G, c("pci", 1, 2), p, 15, O.bitwise_and); vts(G, c("pci", 2, 3), p, 4, O.arith_shift_right); vcp(G, c("pcf", 0, 3), c("pci", 0, 3))
+    P, PR, PG, SL, ha, hb, R0, k1, k2, k3, k4 = [c("pcf", k, k + 1) for k in range(11)]
+    vts(G, SL, P, PG, O.add, 1.0, O.add); vts(G, ha, PR, 7.5, O.is_le); vts(G, hb, PR, 7.5, O.is_ge); vts(G, R0, PR, 0.0, O.is_equal)
+    vts(G, c("Ib"), c("CI", 0, 128), P, O.is_equal)
+    for nm, x in (("I4", 4.0), ("I592", 592.0), ("I2050", 2050.0)): vts(G, c(nm), c("Ib"), x, O.mult)
+    for h, col in (("A", ha), ("B", hb)):
+        for nm, x in (("", 1.0), ("4", 4.0), ("26", 2642.0)): vts(G, c("d" + h + nm), c("Ib"), col, O.mult, x, O.mult)
+    vset(G, pc("one", 0, 2), 1.0)
+    vset(G, pc("cq", 0, 2, 0, 128), 0.0); vset(G, pc("cq", 0, 2, 128, 256), 1.0); vset(G, pc("cq", 0, 1, 0, 128), 2050.0); vset(G, pc("cq", 0, 1, 128, 256), 43008.0)
+    vts(G, c("Dm"), c("CR"), PR, O.is_equal); vts(G, c("S01"), c("CR"), 0.0, O.not_equal)
+    vts(G, c("C8"), c("G16", 0, 8), PG, O.is_equal); vts(G, c("Pick"), c("C8"), R0, O.mult)
+    vts(G, c("BX"), c("G16"), PG, O.is_equal, -8192.0, O.mult); vts(G, c("BM"), c("G16"), PG, O.is_equal, 16384.0, O.mult)
+    for h in (0, 136):
+        vts(G, c("Perm", h, h + 136), c("CI"), SL, O.is_equal); vts(G, c("WN", h, h + 136), c("GC"), PG, O.is_equal, -8192.0, O.mult)
+        vts(G, c("SEG", h, h + 136), c("S1"), -1.0, O.is_equal, 2.0 ** 30, O.mult)
+    vset(G, c("WN", 0, 272, 17), 0.0); vts(G, c("BIGP"), c("Perm"), 2.0 ** 26, O.mult); vts(G, c("nPerm"), c("Perm", 0, 136), -1.0, O.mult)
+    vts(G, k1, P, 512.0, O.mult); vts(G, k2, P, -1.0, O.add, 2.0 ** 24, O.mult); vts(G, k3, P, -1.0, O.add, -2.0 ** 27, O.mult)
+    vts(G, k4, P, -16899584.0, O.mult, 2.0 ** 24, O.add)
+    r = lambda w: pc(w[0], 0, 2, w[2][1][0], w[2][1][1])
+    vts(G, r(c("cr", 0, 136)), r(c("S1")), r(k1), O.mult, r(k2), O.add)
+    for at, op in ((272, O.is_ge), (544, O.is_le)):
+        vts(G, r(c("TK")), r(c("S1")), 7.5, op, r(k3), O.mult); vtt(G, r(c("cr", at, at + 136)), r(c("cr", 0, 136)), r(c("TK")), O.add)
+    for at in (0, 272, 544): vcp(G, r(c("cr", at + 136, at + 272)), r(c("cr", at, at + 136)))
+    vts(G, pc("cr", 0, 2, 0, 816, 17), r(c("S1", 0, 48)), 0.0, O.mult, r(k4), O.add)
+    for p_ in "AB": vset(G, c("SP" + p_), 0.0); mm(G, c("pk" + p_, 288, 416), c("Ib"), c("Dm"))
     vset(G, c("E", 4096, 4112), 0.0)
-    for p_ in "AB": mm(G, c("pk" + p_, 144, 272), c("Ib"), c("Dm"))
 
 
-def angles(G, p, n, P, Vp, hu):
+def ring_constants(G):
+    ne, ge = O.not_equal, O.is_ge
+    vset(G, c("Zb"), 0.0); vset(G, c("Zh"), 0.0); vset(G, c("Zf"), 0.0); vset(G, c("SPJ"), 0.0); vcp(G, c("Dmf"), c("Dm"))
+    for k in "01": vset(G, c("CN" + k, 260, 264), 0.0)
+    Z = lambda w: c("Zf" if WIDE[w[0]] else ("Zh" if PLACE.get(w[0], ("",))[0] == "poolh" else "Zb"), 0, w[3])
+
+    def put(w, items, fresh=True):
+        for pat, base, x in items: sel(G, w, Z(w) if fresh else w, pat, ne, x, base); fresh = False
+    diag = lambda d, x: ([[-1, 8], [-8, 16]], -8 * d, x)
+    rows = lambda r, x: ([[-16, 8], [0, 16]], -r, x)
+    rcol = [[0, 8], [1, 16]]
+    put(c("DC"), [([[-1, 8], [-8, 6], [0, 6]], -56, 1), ([[-1, 8], [0, 6], [8, 6]], -40, -1)])
+    sel(G, c("DJ"), c("Zh"), [[0, 288]], O.is_gt, 1, 0, 0); sel(G, c("DJ"), c("DJ"), [[0, 48], [1, 6]], ne, 3, 0, 0); sel(G, c("DJ"), c("DJ"), [[0, 8], [1, 36]], ge, -60000, -2, 0)
+    sel(G, c("S06"), c("S01"), rcol, ne, 0, -6, 0)
+    q = lambda nm, a, b: pc(nm, 0, 16, a, b); one = [[0, 1]]
+    iota(G, q("R1", 0, 2), [[0, 2]], 8296, -8); sel(G, q("R1", 0, 2), q("R1", 0, 2), [[0, 2]], ge, 0, -6); iota(G, q("R1", 2, 3), one, 1, 0)
+    for k, x in ((1, -8000), (2, -1)):
+        for r in (6, 12): sel(G, q("R1", k, k + 1), q("R1", k, k + 1), one, ne, x, -r)
+    sel(G, q("R1", 1, 3), q("R1", 1, 3), [[0, 2]], ge, 0, 12, -1)
+    iota(G, q("R1", 3, 4), one, -8200, 0); sel(G, q("R1", 3, 4), q("R1", 3, 4), one, ge, 0, -6)
+    iota(G, q("R1", 4, 9), [[-1, 5]], 11, -1); iota(G, q("R1", 9, 10), one, 7, -1); iota(G, q("R1", 10, 11), one, -6, 1)
+    iota(G, q("R2", 0, 2), [[0, 2]], 0, 1); sel(G, q("R2", 0, 2), q("R2", 0, 2), [[0, 2]], ge, 0, 5, -1)
+    put(c("CN"), [diag(-1, 1)]); sel(G, c("CV1a"), c("CN"), rcol, ge, 0, -7, 0); sel(G, c("CN"), c("CN"), rcol, ne, 0, -12, 0)
+    put(c("CV1b"), [diag(1, 1)]); sel(G, c("CV1b"), c("CV1b"), [[0, 8], [-1, 16]], ge, 0, 5, 0); put(c("CV2"), [diag(0, 1)])
+    put(c("CQ1"), [diag(1, 4)]); put(c("CQ2"), [diag(0, 592)]); sel(G, c("CQ2"), c("CQ2"), rcol, ne, 0, -12, 0); put(c("CQ2"), [diag(1, 2050)], False)
+    for nm, x, lo, hi in (("SA", 1, 6, 15), ("SB4", 4, 0, 5), ("SB2050", 2050, 0, 5), ("SA592", 592, 6, 15)):
+        w = c(nm); sel(G, w, Z(w), rcol, ne, x, -12, 0); sel(G, w, w, [[-16, 8], [0, 16]], ge, 0, -lo); sel(G, w, w, [[16, 8], [0, 16]], ge, 0, hi, -1)
+    for nm, x in (("p4I", 4096), ("nI", -1), ("I16", 16), ("m4I", -4096)): put(c(nm), [([[-1, 128]], 0, x)])
+    for nm, x in (("Cmpf", 1), ("Cmp64", -64), ("Cmp", 1), ("Cmp256", -256)): put(c(nm), [([[-16, 8], [-1, 12]], -1, x)])
+    for k in range(2):
+        w = c("BlkC", 144 * k, 144 * k + 144); up = [[0, 3], [16, 4], [0, 12]]; dn = [[0, 3], [-16, 4], [0, 12]]
+        sel(G, w, Z(w), up, ge, 128, 64 * k - 1, -1); sel(G, w, w, up, ge, 0, 64 * k + 15, -1)
+        put(c("DC2", 144 * k, 144 * k + 144), [(dn, -64 * k - 6, -8192), (dn, -64 * k - 14, -1088)])
+    for h in range(16): put(c("SelT", 128 * h, 128 * h + 128), [([[-64, 2], [-1, 4], [0, 16]], -4 * h, 256)])
+    put(c("PI"), [rows(6, -0.125)]); put(c("PZ"), [rows(6, -0.125), rows(0, -1)]); put(c("PD"), [rows(6, -4096)]); put(c("AR"), [diag(6, 1)])
+    for l in range(1, 6): put(c("BRL", 128 * l - 128, 128 * l), [([[-1, 8], [0, 16]], -8 * (6 - l), 1)])
+
+
+def angles(G, p, n, Q1, Q2):
     t1, t2, t3 = c("t1" + p), c("t2" + p), c("t3" + p)
-    vtt(G, t1, n, P, O.mult); vtt(G, t2, t1, Vp, O.add); vts(G, t3, t2, 4, O.arith_shift_right, 4095, O.bitwise_and)
-    if hu is not None: vcp(G, hu, t3)
+    vtt(G, t1, n, Q1, O.mult); vtt(G, t2, t1, Q2, O.add); vts(G, t3, t2, 4, O.arith_shift_right, 4095, O.bitwise_and)
 
 
-def first(G, t):
-    sa, sb_ = c("stu", 8 * t, 8 * t + 8), c("sr%d" % t, 8 * t, 8 * t + 8); oa, ob, nc = c("OA%d" % t), c("OB%d" % t), c("NC%d" % t); b = "pnB"
-    gat(G, oa, c("IDT"), sa); gat(G, ob, c("IDT"), sb_); gat(G, c("tn0"), c("NBO"), sa); gat(G, c("tn1"), c("NBO"), sb_)
-    group(G, c(b, 0, 128), [(c("dA"), oa), (c("dB"), ob)]); group(G, c(b, 128, 256), [(c("dA"), c("tn0")), (c("dB"), c("tn1"))])
-    act(G, c("OSC"), c(b, 0, 128)); act(G, nc, c(b, 128, 256))
-    group(G, c(b, 256, 384), [(c("I296f"), c("OSC")), (row("one"), row("m296"))])
-    angles(G, "B", nc, c(b, 0, 128), c(b, 256, 384), c("hu0%d" % t)); vtt(G, c("mk0%d" % t), nc, c(b, 0, 128), O.is_equal)
+def first(G, t, gather):
+    sa, sb_ = c("stu", 8 * t, 8 * t + 8), c("sr%d" % t, 8 * t, 8 * t + 8); oa, ob, nc = c("OA%d" % t), c("OB%d" % t), c("NC%d" % t); b = "pwB"
+    gather(G, oa, c("IDT"), sa); gather(G, c("tnA"), c("NB"), sa); gather(G, ob, c("IDT"), sb_); gather(G, c("tnB"), c("NB"), sb_)
+    group(G, c(b, 0, 128), [(c("dA"), c("tnA")), (c("dB"), c("tnB"))])
+    mm(G, c(b, 256, 512), pc("one", 0, 2), pc("cq", 0, 2), True, False)
+    for h, o in (("A", oa), ("B", ob)): mm(G, c(b, 256, 384), c("d%s4" % h), o, False, False); mm(G, c(b, 384, 512), c("d%s26" % h), o, False, h == "B")
+    group(G, c(b, 128, 256), [(c("dA"), oa), (c("dB"), ob)])
+    vcp(G, nc, c(b, 0, 128)); angles(G, "B", nc, c(b, 256, 384), c(b, 384, 512)); vcp(G, c("hu0%d" % t), c("t3B"))
+    vtt(G, c("mk0%d" % t), nc, c(b, 128, 256), O.is_equal); vts(G, c("wr0%d" % t), nc, 0.0, O.max)
 
 
 def slot(p, i): return c("po1" + p, 128 * i, 128 * i + 128) if i < 4 else c("po2" + p, 128 * i - 512, 128 * i - 384)
 
 
+def records(G, x, m, hu, W):
+    last = None
+    for a, b in zip(CHUNKS, CHUNKS[1:]):
+        last = gat(G, c(x, 16 * a, 16 * b), c("E"), c(hu, a, b))
+        for r in range(4): vtt(G, c(m, 16 * a + r, 16 * b, 4), c(x, 16 * a + r, 16 * b, 4), c(W, 4 * a, 4 * b), O.max)
+    return last
+
+
 def scores(G, p, a, t, xb, mb, ks):
-    gid = ("key", p, a, t); col = lambda k: c("pk" + p, k + 1, 136, 17); mx = lambda k: c(mb, 128 * k, 128 * k + 128)
-    mm(G, c("pk" + p, 0, 136), row("one"), row("crN") if a else row("cr" + p), True, False)
-    for l, r in [(c("mk" + p, 128 * i, 128 * i + 128), c("BIGP")) for i in range(a + 1)] if a else [(c("mk0%d" % t), c("BIG" + p))]:
-        mm(G, c("pk" + p, 0, 136), l, r, False, False, grp=gid)
-    for k in ks: mm(G, col(k), c(xb, k, 2048, 16), c("B16"), False, False, grp=gid)
-    for k in ks[:-1]: mm(G, col(k), mx(k), c("B32"), False, False, grp=gid)
-    mm(G, col(ks[-1]), mx(ks[-1]), c("B32"), False, True)
-
-
-def maxima(G, xb, mb, who):
-    n = 128 // NCH
-    for h in range(0, 128, n):
-        for k in range(16): vtt(G, c(mb, 128 * k + h, 128 * k + h + n), c(xb, 16 * h + k, 16 * (h + n), 16), c("po2" + who(k), 384 + h, 384 + h + n), O.max)
+    gid = ("key", p, a, t); key = c("pk" + p, 0, 272); col = lambda k: c("pk" + p, k + 1, 272, 17); at = 0 if a else (272 if p == "A" else 544)
+    mm(G, key, pc("one", 0, 2), pc("cr", 0, 2, at, at + 272), True, False)
+    mm(G, key, c("qa" if p == "A" else "qr%d" % t), c("WN"), False, False, grp=gid)
+    if a: mm(G, c("pk" + p, 0, 136, 17), c("Ib"), c("SP" + p, 0, 128, 16), False, False, grp=gid)
+    else: mm(G, c("pk" + p, 0, 136, 17), c("O%s%d" % (p, t)), c("Pick"), False, False, grp=gid)
+    for l in [c("mk" + p, 128 * i, 128 * i + 128) for i in range(a + 1)] if a else [c("mk0%d" % t)]: mm(G, key, l, c("BIGP"), False, False, grp=gid)
+    for k in ks: mm(G, col(k), c(xb, k, 2048, 16), c("BX"), False, False, grp=gid)
+    for k in sorted(ks, key=lambda k: k % 4): mm(G, col(k), c(mb, k, 2048, 16), c("BM"), False, False, grp=gid)
+    mm(G, key, c("wr" + p) if a else c("wr0%d" % t), c("Perm"), False, False)
+    mm(G, c("pk" + p, 136, 272), c("n" + p) if a else c("NC%d" % t), c("nPerm"), False, True)
 
 
 def choose(G, p, a, t):
-    key = c("pk" + p, 0, 136); pn = c("pn" + p, 0, 136); R2 = c("R2" + p); RR = c("RR" + p); fin = c("R2" + p, 16, 136, 17)
-    vscan(G, c("RM" + p), c("SEG"), key, O.add, O.min); vtt(G, c("NQ" + p), c("RM" + p), key, O.not_equal)
-    mm(G, pn, c("m4Ib"), c("NQ" + p), False, True)
-    vscan(G, R2, c("NQ" + p), pn, O.mult, O.max)
-    if a < ST - 1:
-        vcp(G, c("SP" + p, 0, 128, 16), fin); vscan(G, RR, c("S01"), c("SP" + p), O.mult, O.add)
-        vtt(G, c("RD" + p), RR, c("pk" + p, 144, 272), O.mult)
-        mm(G, c("pk" + p, 136, 144), c("RD" + p), c("C8h")); vts(G, c("li" + p), c("pk" + p, 136, 144), 0.5, O.mult, -0.5, O.add)
-        mm(G, slot(p, a + 1), RR, c("Ih"))
-        group(G, c("po2" + p, 256, 384), [(RR, c("I296")), (row("one"), row("m296"))])
-    act(G, v("AL2" if p == "A" else "BL%d" % t, ALL, ALL, a + 1), fin)
-
-
-def names(G, p, a, t):
-    pn = c("pn" + p, 0, 136); s0 = c("pn" + p, 0, 136, 17)
-    mm(G, pn, c("n" + p) if a else c("NC%d" % t), c("PermO"), True, False)
-    if a: mm(G, s0, c("If"), c("R2" + p, 16, 136, 17), False, False)
-    else: mm(G, s0, c("O%s%d" % (p, t)), c("Pick"), False, False)
+    RM = "RM" + p; RR = c("RR%d%s" % (a % 2, p)); sp = c("SP" + p, 0, 128, 16)
+    path = c("CH%d" % t, 56 + 8 * a, 64 + 8 * a) if p == "A" else c("BL%d" % t, 40 - 8 * a, 48 - 8 * a)
+    vscan(G, c(RM), c("SEG"), c("pk" + p, 0, 272), O.add, O.min)
+    vtt(G, sp if a < ST - 1 else path, c(RM, 16, 136, 17), c(RM, 152, 272, 17), O.subtract)
+    if a == ST - 1: return
+    vscan(G, RR, c("S01"), c("SP" + p), O.mult, O.add); vtt(G, c("RD" + p), RR, c("pk" + p, 288, 416), O.mult)
+    mm(G, c("pk" + p, 272, 280), c("RD" + p), c("C8")); vts(G, c("li" + p), c("pk" + p, 272, 280), 512.0, O.add)
+    Q1, Q2 = c("po2" + p, 256, 384), c("po2" + p, 384, 512); was = c("RR%d%s" % ((a - 1) % 2, p)) if a else c("O%s%d" % (p, t))
+    mm(G, c("po2" + p, 256, 512), pc("one", 0, 2), pc("cq", 0, 2), True, False)
+    for o, i in ((Q1, c("I4")), (Q2, c("I2050"))):
+        if a: mm(G, o, was, i, False, False)
+        else: mm(G, o, i, was, False, False)
+    mm(G, Q2, RR, c("I592"), False, True); mm(G, slot(p, a + 1), RR, c("Ib"))
+    act(G, path, sp)
 
 
 def walk(G, t):
-    for p in "AB":
-        mm(G, c("po2" + p, 384, 512), c("Ib"), c("qa") if p == "A" else c("qr%d" % t)); mm(G, slot(p, 0), c("If"), c("O%s%d" % (p, t)))
-    mm(G, c("pnA", 144, 152), c("OA%d" % t), c("Pick")); act(G, v("AL2", ALL, ALL, 0), c("pnA", 144, 152))
-    for p in "AB": names(G, p, 0, t)
-    gather_all(G, "xC", "hu0%d" % t); maxima(G, "xC", "mC", lambda k: "A" if k < 8 else "B")
-    scores(G, "A", 0, t, "xC", "mC", list(range(8))); scores(G, "B", 0, t, "xC", "mC", list(range(8, 16)))
-    for p in "AB": choose(G, p, 0, t)
+    qs = {"A": c("qa"), "B": c("qr%d" % t)}
+    for r in range(4): mm(G, c("po2A", r, 512, 4), c("Ib"), qs["A" if r < 2 else "B"])
+    last = records(G, "xA", "mA", "hu0%d" % t, "po2A")
+    for p in "BA":
+        mm(G, slot(p, 0), c("Ib"), c("O%s%d" % (p, t)))
+        for r in range(4): mm(G, c("pw" + p, r, 512, 4), c("Ib"), qs[p])
+    mm(G, c("pkA", 272, 280), c("OA%d" % t), c("Pick")); act(G, c("CH%d" % t, 48, 56), c("pkA", 272, 280))
+    scores(G, "B", 0, t, "xA", "mA", list(range(8, 16))); scores(G, "A", 0, t, "xA", "mA", list(range(8)))
+    for p in "BA": choose(G, p, 0, t)
     for a in range(1, ST):
-        for p in "AB":
-            vgat(G, c("n" + p), c("NBO"), c("li" + p))
-            angles(G, p, c("n" + p), slot(p, a - 1), c("po2" + p, 256, 384), c("hu" + p))
-            gather_all(G, "x" + p, "hu" + p); names(G, p, a, t)
-            for i in range(a + 1): vtt(G, c("mk" + p, 128 * i, 128 * i + 128), c("n" + p), slot(p, i), O.is_equal)
-            maxima(G, "x" + p, "m" + p, lambda k, p=p: p); scores(G, p, a, t, "x" + p, "m" + p, list(range(16))); choose(G, p, a, t)
+        for p in "BA":
+            n = c("n" + p); gat(G, n, c("NB"), c("li" + p))
+            angles(G, p, n, c("po2" + p, 256, 384), c("po2" + p, 384, 512)); vcp(G, c("hu" + p), c("t3" + p))
+            vts(G, c("wr" + p), n, 0.0, O.max)
+            for i in range(a + 1): vtt(G, c("mk" + p, 128 * i, 128 * i + 128), n, slot(p, i), O.is_equal)
+            last = records(G, "x" + p, "m" + p, "hu" + p, "pw" + p); scores(G, p, a, t, "x" + p, "m" + p, list(range(16))); choose(G, p, a, t)
+    return last
 
 
 def rings(G, t):
-    al = lambda a, b: v("AL2", ALL, ALL, slice(a, b)); br = lambda a, b: v("BR%d" % t, ALL, ALL, slice(a, b))
-    for d in range(-5, 6):
-        i0 = max(1, 1 + d) if d else 2; i1 = min(6, 6 + d); n = i1 - i0 + 1; f0 = (i0 - 1) * 6 + i0 - d - 1
-        vtt(G, v("EQ", ALL, ALL, slice(f0, f0 + 7 * (n - 1) + 1, 7)), al(i0, i1 + 1), br(i0 - d, i1 - d + 1), O.is_equal)
-    mm(G, c("pnA", 0, 288), c("Ib"), v("EQ"))
-    vscan(G, c("FJ"), c("SEGJ"), c("pnA", 0, 288), O.add, O.max)
-    vcp(G, c("SPA", 0, 128, 16), c("FJ", 35, 288, 36)); vscan(G, c("RRA"), c("S01"), c("SPA"), O.mult, O.add)
-    y = c("pnB", 0, 128); mm(G, y, c("RRA"), c("I64"))
-    AL1, BL1 = c("po1B", 0, 128), c("po1B", 128, 256); mm(G, AL1, v("AL2"), c("If")); mm(G, BL1, v("BR%d" % t), c("If"))
-    vcp(G, c("BLs"), BL1); brep = [c("po2B", 128 * j, 128 * j + 128) for j in range(4)] + [c("po1B", 256, 384)]
-    for j in range(5): mm(G, brep[j], c("SelJ", 128 * j, 128 * j + 128), c("BLs"))
-    vts(G, c("IR"), y, -1.0 / 6, O.mult, 17.0 + 1.0 / 12, O.add); vts(G, c("TT"), c("IR"), -5.0, O.mult, 106.0, O.add)
-    vtt(G, c("LF"), c("TT"), y, O.subtract); vts(G, c("FN"), y, 63.5, O.is_ge); vtt(G, c("L0"), c("LF"), c("FN"), O.mult)
-    vts(G, c("L1"), c("L0"), -1.0, O.add); vtt(G, c("i0"), c("IR"), c("L1"), O.min)
-    m = lambda j: c("mcol", j, j + 1)
-    vts(G, c("MA"), c("i0"), m(0), O.is_ge); vts(G, c("MA64"), c("i0"), m(0), O.is_ge, 64.0, O.mult)
-    vtt(G, c("Lm"), c("L0"), c("MA64"), O.subtract); vts(G, c("MN"), c("L0"), m(0), O.is_le); vts(G, c("ML"), c("L0"), m(1), O.is_equal)
-    vtt(G, c("PB", 0, 128), c("MA"), AL1, O.mult)
-    for j in range(1, 6):
-        mb = c("MB", 128 * j - 128, 128 * j); vts(G, mb, c("Lm"), m(j), O.is_equal); vtt(G, c("PB", 128 * j, 128 * j + 128), mb, brep[j - 1], O.mult)
-    CP = c("pkB", 0, 128)
-    group(G, CP, [(c("nIb"), c("MN"))] + [(c("Ih"), c("PB", 128 * j, 128 * j + 128)) for j in range(6)])
-    vcp(G, c("CS"), CP); act(G, c("YR", 128 * t, 128 * t + 128), CP, F.Identity, -0.5, 0.5)
-    vtt(G, c("PL"), c("ML"), CP, O.mult); vtt(G, c("PA0"), c("ML"), slot("A", 0), O.mult)
-    BP, AP, VP, NN = [c("pnA", 128 * j, 128 * j + 128) for j in range(4)]
-    group(G, NN, [(c("p4Ib"), c("MN"))]); group(G, VP, [(c("I296"), c("CS")), (row("one"), row("m296"))])
-    group(G, AP, [(c("Ih"), c("PA0")), (c("Ib"), c("ML")), (c("ShA"), c("CS"))]); group(G, BP, [(c("ShB"), c("CS")), (c("G0"), c("PL"))])
-    act(G, c("APs"), AP)
-    angles(G, "A", c("APs"), BP, VP, None); vtt(G, c("HF"), c("t3A"), NN, O.max); vcp(G, c("huA"), c("HF"))
-    gather_all(G, "xA", "huA")
+    CH = "CH%d" % t; ct = pc("CT", 0, 104); col = lambda k: c("col", k, k + 1)
+    if t == 0:
+        mm(G, c("po1B", 0, 11), pc("Dmf", 0, 16), pc("R1", 0, 16, 0, 11), True, False); mm(G, c("po1B", 0, 2), pc("Dmf", 0, 16), pc("R2", 0, 16, 0, 2), False, True)
+        vcp(G, c("col", 0, 11), c("po1B", 0, 11))
+    mm(G, pc("po2B", 0, 96, 320, 448), c(CH, 0, 96), c("Ib")); vcp(G, pc("CT", 0, 96), pc("po2B", 0, 96, 320, 448))
+    mm(G, c("pkB", 0, 288), pc("CT", 0, 96), pc("DC", 0, 96), True, False)
+    for j in range(6): mm(G, c("pkB", 30 + j, 288, 36), c("Ib"), c(CH, 96, 104), False, j == 5)
+    vts(G, c("EQ"), c("pkB", 0, 288), 0.0, O.is_equal, 8200.0, O.mult); vscan(G, c("FJ"), c("DJ"), c("EQ"), O.add, O.max)
+    mm(G, pc("po2B", 96, 104, 320, 448), c(CH, 96, 104), c("Ib")); vcp(G, pc("CT", 96, 104), pc("po2B", 96, 104, 320, 448))
+    end = c("FJ", 35, 288, 36); vts(G, c("SPJ", 6, 128, 16), end, -2.5, O.add); vtt(G, c("SPJ", 0, 128, 16), end, c("SPJ", 6, 128, 16), O.subtract)
+    vscan(G, c("RRJ"), c("S06"), c("SPJ"), O.mult, O.add); Z = c("pkA", 0, 128); mm(G, Z, c("RRJ"), c("Ib"))
+    V1, V2, NN = [c("po1A", 128 * k, 128 * k + 128) for k in range(3)]; NP = c("po1B", 0, 128); Q1, Q2 = c("po2A", 0, 128), c("po2A", 128, 256); k104 = lambda nm: pc(nm, 0, 104)
+    group(G, V1, [(k104("CV1a"), ct), (k104("CV1b"), ct)]); mm(G, V2, k104("CV2"), ct); mm(G, NP, k104("CN"), ct, True, False)
+    mm(G, c("po2A", 0, 256), pc("one", 0, 2), pc("cq", 0, 2), True, False); mm(G, Q1, k104("CQ1"), ct, False, False); mm(G, Q2, k104("CQ2"), ct, False, False)
+    vts(G, c("OH"), Z, col(0), O.is_equal); vtt(G, c("Y1"), c("OH"), V1, O.mult); vtt(G, c("Y2"), c("OH"), V2, O.mult)
+    vts(G, c("dead"), Z, col(2), O.mult, col(1), O.is_ge)
+    mm(G, NP, c("SA"), c("Y1"), False, True); mm(G, Q1, c("SB4"), c("Y1"), False, False); mm(G, Q2, c("SB2050"), c("Y1"), False, False); mm(G, Q2, c("SA592"), c("Y2"), False, True)
+    mm(G, NN, c("p4I"), c("dead")); act(G, c("Zs"), Z, F.Identity, col(3))
+    vcp(G, c("NS"), NP); angles(G, "A", c("NS"), Q1, Q2); vtt(G, c("HF"), c("t3A"), NN, O.max); vcp(G, c("huA"), c("HF"))
     vts(G, c("hiB"), c("HF"), 1.0 / 64, O.mult, 129.0 - 63.0 / 128, O.add)
-    LO = c("pkB", 272, 400); group(G, LO, [(c("HF"), c("If")), (c("hiB"), c("m64Ib"))]); vts(G, c("LOT"), LO, 8256.0, O.add)
-    for u in range(64): vts(G, c("OHL", 128 * u, 128 * u + 128), c("LOT"), float(u), O.is_equal)
-    tot = c("pnB", 128, 256); group(G, tot, [(c("Ib"), c("xA", k, 2048, 16)) for k in range(12)])
-    vts(G, c("TH"), tot, c("thf"), O.is_ge); cnt = c("pnB", 256, 384); mm(G, cnt, c("Blk"), c("TH")); vts(G, c("NH"), cnt, 8.5, O.is_le)
-    HI = c("po1B", 384, 512); group(G, HI, [(c("hiB"), c("Ib")), (c("MN"), c("m256Ib")), (c("NH"), c("m256Ib"))]); act(G, c("HIT"), HI, F.Identity, -129.0)
+    LO, HI = c("po2B", 0, 96), c("po2B", 96, 192); group(G, LO, [(c("HF"), c("Cmpf")), (c("hiB"), c("Cmp64"))]); group(G, HI, [(c("hiB"), c("Cmp")), (c("dead"), c("Cmp256"))])
+    for d in range(2): vts(G, c("LOT", 96 * d, 96 * d + 96), LO, 8256.0 - d, O.add)
+    for a, b in zip(RCHUNKS, RCHUNKS[1:]): gat(G, c("xA", 16 * a, 16 * b), c("E"), c("huA", a, b))
+    for k in range(2):
+        for d in range(3): act(G, c("HI0", 144 * k + 48 * d, 144 * k + 48 * d + 48), c("po2B", 96 + 48 * k, 144 + 48 * k), F.Identity, -129.0 - d)
+    for u in range(0, 64, 2): vts(G, c("OHL", 96 * u, 96 * u + 192), c("LOT"), float(u), O.is_equal)
+    for a, b in zip(RCHUNKS, RCHUNKS[1:]): group(G, c("po1B", 128 + a, 128 + b), [(c("Ib"), c("xA", 16 * a + r, 16 * b, 16)) for r in range(1, 13)])
+    mm(G, c("pwB", 0, 288), c("dead"), c("DC2"), True, False)
+    vts(G, c("TH"), c("po1B", 128, 256), c("thf"), O.is_ge); mm(G, c("pwB", 0, 288), c("TH"), c("BlkC"), False, True)
+    for k in range(2): vtt(G, c("HIT", 144 * k, 144 * k + 144), c("HI0", 144 * k, 144 * k + 144), c("pwB", 144 * k, 144 * k + 144), O.min)
 
 
-def lessen(G, t):
-    for u in range(64):
-        o = c("THH", 128 * u, 128 * u + 128)
-        if u < NTS: act(G, o, c("HIT"), F.Sigmoid, -200.0 * (u - 0.5), 200.0)
-        else: vts(G, o, c("HIT"), float(u), O.is_ge)
-    lo64 = slice(0, 64)
-    for g in range(8): group(G, v("po2A", lo64, slice(g, 512, 8)), [(c("OHL", 16 * g + m, 8192, 128), c("THH", 16 * g + m, 8192, 128)) for m in range(12)])
-    pc = v("po2A", lo64, slice(0, 512)); act(G, v("CT", lo64, slice(0, 512)), pc); vtt(G, v("NM", lo64, ALL), v("CT", lo64, slice(8, 520)), pc, O.is_equal)
-    for b in range(4): mm(G, c("pnA", 64 * b, 64 * b + 64), v("NM", lo64, slice(128 * b, 128 * b + 128)), v("Ib", lo64, slice(0, 64)))
-    act(G, c("NM2"), c("pnA", 0, 256), F.Identity, 0.5, 2.0)
+def lessen(G, t, after):
     for k in range(8):
-        bank = ("po2B", "pnB", "po1A", "pkA", "po1B")[k % 5]; e = c("E", 512 * k, 512 * k + 512); o = c(bank, 0, 512); b = k // 2
-        mm(G, o, c("Ib"), e, True, False); mm(G, o, c("nIb"), c("G4", 512 * k, 512 * k + 512), False, False)
+        i = act(G, c("L16", 512 * k, 512 * k + 512), c("E", 512 * k, 512 * k + 512), F.Identity, 1024.375, 0.75); G["ops"][i]["deps"].setdefault(after, False)
+    for k, bank in enumerate(("pwA", "pkB")):
+        hit = c("HIT", 144 * k, 144 * k + 144); th = "THH%d" % k; cn = "CN%d" % k
+        for i in range(22):
+            o = c(th, 144 * i, 144 * i + 144)
+            if i < 6: act(G, o, hit, F.Sign, 1.5 - 3 * i)
+            else: vts(G, o, hit, float(3 * i - 2), O.is_ge)
+        for gl in range(4):
+            group(G, pc(bank, 0, 64, gl, 260, 4), [(c("OHL", 48 * k + 12 * gl + s, 6144, 96), c(th, 48 + 12 * gl + s, 3168, 48)) for s in range(12)])
+        act(G, pc(cn, 0, 64, 0, 260), pc(bank, 0, 64, 0, 260))
+        for b in range(4):
+            a = 4 * (16 * b + (1 if b else 0))
+            group(G, pc("pkA", 64 * k, 64 * k + 64, 64 * b, 64 * b + 64), [(pc(cn, 0, 64, a, a + 64), pc("Ib", 0, 64, 0, 64)), (pc(cn, 0, 64, a + 4, a + 68), pc("nI", 0, 64, 0, 64))])
+    vts(G, c("NM"), c("pkA", 0, 256), 0.0, O.is_equal, 4.0, O.subtract)
+    for k in range(8):
+        bank = ("po1A", "po2A", "po2B", "po1B")[k % 4]; e = c("E", 512 * k, 512 * k + 512); o = c(bank, 0, 512); b = k // 2
+        mm(G, o, c("Ib"), c("L16", 512 * k, 512 * k + 512), True, False)
         for h in range(8):
-            s = 128 * ((k % 2) * 8 + h); mm(G, c(bank, 64 * h, 64 * h + 64), c("SelT", s, s + 128), c("NM2", 64 * b, 64 * b + 64), False, h == 7)
+            s = 128 * ((k % 2) * 8 + h); mm(G, c(bank, 64 * h, 64 * h + 64), c("SelT", s, s + 128), c("NM", 64 * b, 64 * b + 64), False, h == 7)
         vtt(G, e, e, o, O.min)
         if t == RO - 1 and k % 2:
-            a = 512 * (k - 1); dma(G, lambda g, T, a=a: g.sync.dma_start(T.ye[:, a:a + 1024], T.E[:, a:a + 1024]), [c("E", a, a + 1024)], [], 3.5)
-    if t < RO - 1:
-        quarter(G); mm(G, c("pkA", 144, 272), c("Ib"), c("Dm"))
+            a = 512 * (k - 1); dma(G, lambda g, T, a=a: g.sync.dma_start(T.ye[:, a:a + 1024], T.E[:, a:a + 1024]), [c("E", a, a + 1024)], [], 2.5)
 
 
-def quarter(G):
-    for k in range(8): act(G, c("G4", 512 * k, 512 * k + 512), c("E", 512 * k, 512 * k + 512), F.Identity, 127.625, 0.25)
+def ring_atoms(G, t):
+    ct = pc("CT", 0, 104); col = lambda k: c("col", k, k + 1); PL, PI = c("pwB", 0, 128), c("pwB", 128, 256)
+    mm(G, PI, c("PI"), c("Zs")); act(G, c("r1"), PI, F.Relu, col(9)); act(G, c("r2"), PI, F.Relu, col(10), -1.0)
+    group(G, PL, [(c("PZ"), c("Zs")), (c("I16"), c("r1"))])
+    for l in range(5): act(G, c("ZL", 128 * l, 128 * l + 128), PL, F.Abs, col(4 + l))
+    group(G, c("pwB", 256, 384), [(pc("AR", 0, 104), ct), (c("m4I"), c("r2")), (c("PD"), c("dead"))])
+    for l in range(5):
+        o = c("pwA", 128 * l, 128 * l + 128) if l < 4 else c("pwB", 384, 512)
+        group(G, o, [(pc("BRL", 0, 104, 128 * l, 128 * l + 128), ct), (c("m4I"), c("ZL", 128 * l, 128 * l + 128))])
+    act(G, c("PB", 0, 256), c("pwB", 256, 512), F.Relu, 513.0); act(G, c("PB", 256, 768), c("pwA"), F.Relu, 513.0)
+    group(G, c("pkB", 0, 128), [(c("Ib"), c("PB", 128 * k, 128 * k + 128)) for k in range(6)])
+    y = c("YR", 128 * t, 128 * t + 128); act(G, y, c("pkB", 0, 128), F.Identity, -1.0)
+    dma(G, lambda g, T: g.sync.dma_start(T.yr[:, 128 * t:128 * t + 128], ap(T, y)), [y], [], 2.0)
 
 
 def build(rank, core, topo):
-    G = {"ops": [], "acc": {}, "nd": [0]}; peers = [(rank + 1 + t) % N for t in range(RO)]; asks = [(rank - 1 - t) % N for t in range(RO)]; ne = 8
+    G = {"ops": [], "acc": {}, "nd": [0], "late": [0.0]}; peers = [(rank + 1 + t) % N for t in range(RO)]; asks = [(rank - 1 - t) % N for t in range(RO)]; ne = 8
 
     def eng(T, dst):
         m = 0
@@ -418,28 +468,27 @@ def build(rank, core, topo):
         return fn
     dma(G, lambda g, T: g.sync.dma_start(T.sti[:], T.st[:]), [], [c("sti")], 2.0)
     dma(G, lambda g, T: g.sync.dma_start(T.qa[:], T.q[:]), [], [c("qa")], 2.0)
-    dma(G, lambda g, T: g.sync.dma_start(T.nbi[:], T.nb[:]), [], [c("nbi")], 4.0)
-    dma(G, lambda g, T: g.sync.dma_start(T.E[:, 0:4096], T.ang[:]), [], [c("E", 0, 4096)], 8.0)
+    dma(G, lambda g, T: g.sync.dma_start(T.nbi[:], T.nb[:]), [], [c("nbi")], 3.5)
+    dma(G, lambda g, T: g.sync.dma_start(T.E[:, 0:4096], T.ang[:]), [], [c("E", 0, 4096)], 6.0)
     dma(G, lambda g, T: g.sync.dma_start(T.thi[:], T.th[:]), [], [c("thi")], 2.0)
     vcp(G, c("stu"), c("sti"))
-    s1 = add(G, "G", send3("stu", ["sr0", "sr1", "sr2"], "as0"), [c("stu")], [], 1.0, sem=("loc", 0))
-    s2 = add(G, "G", send3("qa", ["qr0", "qr1", "qr2"], "aq"), [c("qa")], [], 1.0, sem=("loc", 0))
+    s1 = add(G, "G", send3("stu", ["sr0", "sr1", "sr2"], "as0"), [c("stu")], [], 0.5, sem=("loc", 0))
+    s2 = add(G, "G", send3("qa", ["qr0", "qr1", "qr2"], "aq"), [c("qa")], [], 0.5, sem=("loc", 0))
     for s, nm, sem in ((s1, "sr", "as0"), (s2, "qr", "aq")):
         i = add(G, "N", None, [], [c(nm + "%d" % t) for t in range(RO)], 3.0, sem=(sem, 3 * ne)); G["ops"][i]["deps"][s] = False
-    constants(G)
-    vts(G, c("NBO"), c("nbi"), 2.0, O.mult, 1.0, O.add); vcp(G, c("thf"), c("thi"))
-    first(G, 0); quarter(G)
+    walk_constants(G)
+    vts(G, c("NB"), c("nbi"), -512.0, O.add); vcp(G, c("thf"), c("thi"))
+    first(G, 0, gat); ring_constants(G)
     for t in range(RO):
-        walk(G, t)
+        last = walk(G, t)
 
         def back(g, T, t=t):
             a = topo.addr(T.cores[asks[t]])
-            return g.remote_dma(T["BR%d" % t][:], T["BL%d" % t][:], T.sem["ar%d" % t], T.sem.loc, a[1], a[0], eng(T, asks[t]))
-        s = add(G, "G", back, [v("BL%d" % t)], [], 0.5, sem=("loc", 0))
-        i = add(G, "N", None, [], [v("BR%d" % t)], 2.5, sem=("ar%d" % t, ne)); G["ops"][i]["deps"][s] = False
-        if t < RO - 1: first(G, t + 1)
-        rings(G, t); lessen(G, t)
-    dma(G, lambda g, T: g.sync.dma_start(T.yr[:], ap(T, c("YR"))), [c("YR")], [], 3.0)
+            return g.remote_dma(T["CH%d" % t][:, 0:48], T["BL%d" % t][:], T.sem["ar%d" % t], T.sem.loc, a[1], a[0], eng(T, asks[t]))
+        s = add(G, "G", back, [c("BL%d" % t)], [], 0.5, sem=("loc", 0))
+        i = add(G, "N", None, [], [c("CH%d" % t, 0, 48)], 2.0, sem=("ar%d" % t, ne)); G["ops"][i]["deps"][s] = False
+        if t < RO - 1: first(G, t + 1, vgat)
+        rings(G, t); lessen(G, t, last); ring_atoms(G, t)
     return G, ne
 
 

@@ -3,6 +3,7 @@ from concourse.mybir import AluOpType as O, ActivationFunctionType as F
 
 N, RO, ST = 4, 3, 6
 CHUNKS = (0, 48, 96, 128)
+MCHUNKS = (0, 32, 64, 96); NM_ = 96
 RCHUNKS = (0, 64, 128)
 SCRATCH, SHAPE, WIDE, PLACE = {}, {}, {}, {}
 SEMAPHORES = ["sv", "ss", "sp", "sg", "as0", "aq", "ar0", "ar1", "ar2", "loc"] + ["d%d" % i for i in range(20)]
@@ -25,16 +26,16 @@ def many(dtype, cols, names):
 many("int32", 1024, "nbi"); many("float32", 1024, "NB IDT"); many("bfloat16", 4112, "E"); many("float16", 4096, "L16")
 many("bfloat16", 128, "qa qr0 qr1 qr2"); many("int32", 24, "sti"); many("uint16", 24, "stu sr0 sr1 sr2"); many("int32", 1, "thi"); many("float32", 1, "thf")
 many("int32", 4, "pci"); many("float32", 12, "pcf"); many("float32", 136, "CI S1 GC TK"); many("float32", 128, "CR"); many("float32", 16, "G16"); many("float32", 272, "SEG")
-many("bfloat16", 128, "Ib I4 I592 dA dB dA4 dB4 Dm S01 one"); many("float16", 128, "I2050 dA26 dB26"); many("float16", 256, "cq")
-many("bfloat16", 272, "Perm BIGP WN"); many("bfloat16", 136, "nPerm"); many("bfloat16", 816, "cr"); many("bfloat16", 16, "BX BM"); many("bfloat16", 8, "C8 Pick")
-many("bfloat16", 288, "Zb DC BlkC DC2"); many("float16", 288, "Zh DJ"); many("float32", 128, "Zf Dmf"); many("float32", 16, "R1 R2 col")
-many("bfloat16", 128, "CN CQ1 CV1a CV1b CV2 SA SA592 SB4 S06 PZ PI PD AR I16 m4I p4I nI"); many("float16", 128, "CQ2 SB2050"); many("bfloat16", 640, "BRL")
-many("float32", 96, "Cmpf"); many("bfloat16", 96, "Cmp Cmp64 Cmp256"); many("bfloat16", 2048, "SelT")
-many("float16", 128, "CT SPJ RRJ Y1 Y2 NS tnA tnB"); many("float16", 288, "EQ"); many("float32", 288, "FJ"); many("bfloat16", 128, "OH dead hiB TH Zs r1 r2"); many("float32", 128, "HF")
-many("bfloat16", 192, "LOT"); many("bfloat16", 288, "HI0 HIT"); many("bfloat16", 6144, "OHL"); many("bfloat16", 3168, "THH0 THH1"); many("float16", 264, "CN0 CN1")
+many("bfloat16", 128, "Ib I4 I592 dA dB dA4 dB4 Dm S01 TR nI one W4A W4B"); many("float16", 128, "I2050 dA26 dB26"); many("float16", 256, "cq")
+many("bfloat16", 272, "Perm BIGP WN"); many("bfloat16", 136, "nPerm"); many("bfloat16", 816, "cr"); many("bfloat16", 16, "BX BM BA"); many("bfloat16", 8, "C8 nC8 Pick")
+many("bfloat16", 288, "Zb DC"); many("bfloat16", 576, "BlkC DC2 Cmp6 Cmq6 DH6"); many("float16", 288, "Zh DJ"); many("float32", 128, "Zf Dmf"); many("float32", 16, "R1 R2 col")
+many("bfloat16", 128, "CN CQ1 CV1a CV1b CV2 SA SA592 SB4 S06 PZ PI PD AR I16 m4I p4I"); many("float16", 128, "CQ2 SB2050"); many("bfloat16", 640, "BRL")
+many("float32", 96, "Cmpf"); many("bfloat16", 96, "Cmp64"); many("bfloat16", 2048, "SelT")
+many("float16", 128, "CT SPJ RRJ Y1 Y2 NS tnA tnB"); many("float16", 288, "EQ"); many("float32", 288, "FJ"); many("bfloat16", 128, "OH dead hiB hqB TH Zs r1 r2"); many("float32", 128, "HF")
+many("bfloat16", 384, "LOT"); many("bfloat16", 576, "HI0 HIT"); many("bfloat16", 6144, "OHL"); many("bfloat16", 3168, "THH0 THH1"); many("float16", 264, "CN0 CN1")
 many("bfloat16", 256, "NM"); many("bfloat16", 640, "ZL"); many("float16", 768, "PB"); many("float32", 384, "YR")
 for _p in "AB":
-    for _d, _c, _l in (("float16", 128, "n wr SP RR0 RR1 RD"), ("float32", 128, "t1"), ("int32", 128, "t2 t3"), ("uint16", 128, "hu"), ("bfloat16", 2048, "x m"), ("bfloat16", 768, "mk"),
+    for _d, _c, _l in (("float16", 128, "n wr RR1 RR2 RR3 RR4 RR5"), ("float16", 144, "SP RT"), ("float32", 128, "t1 Q1"), ("int32", 128, "t2 t3"), ("uint16", 128, "hu"), ("bfloat16", 2048, "x m"), ("bfloat16", 768, "mk"),
                        ("float32", 272, "RM"), ("uint16", 8, "li")):
         many(_d, _c, " ".join(n + _p for n in _l.split()))
     for _n in ("k", "w", "o1", "o2"): SCRATCH["p" + _n + _p] = ("psum", [128, 512], "float32")
@@ -141,6 +142,10 @@ def vgat(G, o, w, off):
     add(G, "V", lambda g, T: g.vector.tensor_copy(ap(T, o), ap(T, w).indirect(ap(T, off))), [w, off], [o], o[3] * VC * GR + 0.05, gn=o[3])
 
 
+def vgop(G, o, w, off, b, op):
+    add(G, "V", lambda g, T: g.vector.tensor_tensor(ap(T, o), ap(T, w).indirect(ap(T, off)), ap(T, b), op), [w, off, b], [o], o[3] * VC * GR + 0.05, gn=o[3])
+
+
 def act(G, o, a, func=F.Copy, bias=0.0, scale=1.0):
     return add(G, "S", lambda g, T: g.scalar.activation(ap(T, o), ap(T, a), func, bias=num(T, bias), scale=scale), [a] + cols(bias), [o], max(64, o[3]) * VC + 0.02)
 
@@ -172,7 +177,8 @@ def dma(G, fn, R, W, dur):
     k = "d%d" % G["nd"][0]; G["nd"][0] += 1; add(G, "Y", fn, R, W, dur, sem=(k, 16))
 
 
-LATER = {"mA": 2.0, "mB": 2.0, "mkA": 2.0, "mkB": 2.0, "wrA": 2.0, "wrB": 2.0}
+PASSES = 3; SAME, CROSS = 0.15, 0.25
+LATER = {"Vm": 2.0, "Vmk": 2.0, "Swr": 2.0}
 
 
 def schedule(G):
@@ -181,10 +187,10 @@ def schedule(G):
         need[i] = len(o["deps"])
         for d in o["deps"]: succ[d].append(i)
 
-    def lat(d, i): return 0.0 if not ops[i]["deps"][d] else (0.06 if ops[d]["q"] == ops[i]["q"] else 0.1)
+    def lat(d, i): return 0.0 if not ops[i]["deps"][d] else (SAME if ops[d]["q"] == ops[i]["q"] else CROSS)
     far = [0.0] * n; pr = [0.0] * n
     for i in range(n - 1, -1, -1):
-        far[i] = ops[i]["dur"] + max([far[s] + lat(i, s) for s in succ[i]] + [0.0]); pr[i] = far[i] - LATER.get(ops[i]["to"], 0.0) - ops[i]["late"]
+        far[i] = ops[i]["dur"] + max([far[s] + lat(i, s) for s in succ[i]] + [0.0]); pr[i] = far[i] - LATER.get(ops[i]["q"] + ops[i]["to"][:-1], 0.0)
     free = {q: 0.0 for q in "VSPGYN"}; ready = {q: [] for q in free}; rt = [0.0] * n; order = []
     for i in range(n):
         if not need[i]: ready[ops[i]["q"]].append(i)
@@ -200,7 +206,29 @@ def schedule(G):
             rt[s] = max(rt[s], end + lat(i, s)); need[s] -= 1
             if not need[s]: ready[ops[s]["q"]].append(s)
         ops[i]["t"] = (t0, end)
-    return order
+    pred = [list(o["deps"]) for o in ops]; dur = [o["dur"] for o in ops]
+
+    def place(seq, before, gap):
+        at = [0.0] * n; busy = {q: ([], []) for q in QSEM}
+        for i in seq:
+            t0 = max([at[d] + dur[d] + gap(d, i) for d in before[i]] + [0.0])
+            if ops[i]["q"] in busy:
+                a, b = busy[ops[i]["q"]]; lo, hi = 0, len(b)
+                while lo < hi:
+                    mid = (lo + hi) // 2
+                    if b[mid] <= t0 + 1e-9: lo = mid + 1
+                    else: hi = mid
+                while lo < len(a) and a[lo] < t0 + dur[i] - 1e-9: t0 = max(t0, b[lo]); lo += 1
+                a.insert(lo, t0); b.insert(lo, t0 + dur[i])
+            at[i] = t0
+        return at
+    at = [o["t"][0] for o in ops]; best = (max(at[i] + dur[i] for i in range(n)), at)
+    for _ in range(PASSES):
+        back = place(sorted(range(n), key=lambda i: -at[i] - dur[i]), succ, lambda d, i: lat(i, d))
+        at = place(sorted(range(n), key=lambda i: -back[i] - dur[i]), pred, lat); end = max(at[i] + dur[i] for i in range(n))
+        if end < best[0]: best = (end, at)
+    for i in range(n): ops[i]["t"] = (best[1][i], best[1][i] + dur[i])
+    return sorted(range(n), key=lambda i: (best[1][i], i))
 
 
 def emit(G, order, g, T):
@@ -237,14 +265,14 @@ def walk_constants(G):
     P, PR, PG, SL, ha, hb, R0, k1, k2, k3, k4 = [c("pcf", k, k + 1) for k in range(11)]
     vts(G, SL, P, PG, O.add, 1.0, O.add); vts(G, ha, PR, 7.5, O.is_le); vts(G, hb, PR, 7.5, O.is_ge); vts(G, R0, PR, 0.0, O.is_equal)
     vts(G, c("Ib"), c("CI", 0, 128), P, O.is_equal)
-    for nm, x in (("I4", 4.0), ("I592", 592.0), ("I2050", 2050.0)): vts(G, c(nm), c("Ib"), x, O.mult)
+    for nm, x in (("I4", 4.0), ("I592", 592.0), ("I2050", 2050.0), ("nI", -1.0)): vts(G, c(nm), c("Ib"), x, O.mult)
     for h, col in (("A", ha), ("B", hb)):
         for nm, x in (("", 1.0), ("4", 4.0), ("26", 2642.0)): vts(G, c("d" + h + nm), c("Ib"), col, O.mult, x, O.mult)
     vset(G, pc("one", 0, 2), 1.0)
     vset(G, pc("cq", 0, 2, 0, 128), 0.0); vset(G, pc("cq", 0, 2, 128, 256), 1.0); vset(G, pc("cq", 0, 1, 0, 128), 2050.0); vset(G, pc("cq", 0, 1, 128, 256), 43008.0)
-    vts(G, c("Dm"), c("CR"), PR, O.is_equal); vts(G, c("S01"), c("CR"), 0.0, O.not_equal)
-    vts(G, c("C8"), c("G16", 0, 8), PG, O.is_equal); vts(G, c("Pick"), c("C8"), R0, O.mult)
-    vts(G, c("BX"), c("G16"), PG, O.is_equal, -8192.0, O.mult); vts(G, c("BM"), c("G16"), PG, O.is_equal, 16384.0, O.mult)
+    vts(G, c("Dm"), c("CR"), PR, O.is_equal); vts(G, c("S01"), c("CR"), 0.0, O.not_equal); vts(G, c("TR"), c("CR"), PR, O.is_le); vset(G, c("TR", 0, 128, 16), 0.0)
+    vts(G, c("C8"), c("G16", 0, 8), PG, O.is_equal); vts(G, c("Pick"), c("C8"), R0, O.mult); vts(G, c("nC8"), c("C8"), -1.0, O.mult)
+    vts(G, c("BX"), c("G16"), PG, O.is_equal, -8192.0, O.mult); vts(G, c("BM"), c("BX"), -2.0, O.mult); vts(G, c("BA"), c("BX"), -1.0, O.mult)
     for h in (0, 136):
         vts(G, c("Perm", h, h + 136), c("CI"), SL, O.is_equal); vts(G, c("WN", h, h + 136), c("GC"), PG, O.is_equal, -8192.0, O.mult)
         vts(G, c("SEG", h, h + 136), c("S1"), -1.0, O.is_equal, 2.0 ** 30, O.mult)
@@ -257,7 +285,7 @@ def walk_constants(G):
         vts(G, r(c("TK")), r(c("S1")), 7.5, op, r(k3), O.mult); vtt(G, r(c("cr", at, at + 136)), r(c("cr", 0, 136)), r(c("TK")), O.add)
     for at in (0, 272, 544): vcp(G, r(c("cr", at + 136, at + 272)), r(c("cr", at, at + 136)))
     vts(G, pc("cr", 0, 2, 0, 816, 17), r(c("S1", 0, 48)), 0.0, O.mult, r(k4), O.add)
-    for p_ in "AB": vset(G, c("SP" + p_), 0.0); mm(G, c("pk" + p_, 288, 416), c("Ib"), c("Dm"))
+    for p_ in "AB": vset(G, c("SP" + p_), 0.0); vset(G, c("RT" + p_, 128, 144), 0.0)
     vset(G, c("E", 4096, 4112), 0.0)
 
 
@@ -288,12 +316,13 @@ def ring_constants(G):
     put(c("CQ1"), [diag(1, 4)]); put(c("CQ2"), [diag(0, 592)]); sel(G, c("CQ2"), c("CQ2"), rcol, ne, 0, -12, 0); put(c("CQ2"), [diag(1, 2050)], False)
     for nm, x, lo, hi in (("SA", 1, 6, 15), ("SB4", 4, 0, 5), ("SB2050", 2050, 0, 5), ("SA592", 592, 6, 15)):
         w = c(nm); sel(G, w, Z(w), rcol, ne, x, -12, 0); sel(G, w, w, [[-16, 8], [0, 16]], ge, 0, -lo); sel(G, w, w, [[16, 8], [0, 16]], ge, 0, hi, -1)
-    for nm, x in (("p4I", 4096), ("nI", -1), ("I16", 16), ("m4I", -4096)): put(c(nm), [([[-1, 128]], 0, x)])
-    for nm, x in (("Cmpf", 1), ("Cmp64", -64), ("Cmp", 1), ("Cmp256", -256)): put(c(nm), [([[-16, 8], [-1, 12]], -1, x)])
+    for nm, x in (("p4I", 4096), ("I16", 16), ("m4I", -4096)): put(c(nm), [([[-1, 128]], 0, x)])
+    for nm, x in (("Cmpf", 1), ("Cmp64", -64)): put(c(nm), [([[-16, 8], [-1, 12]], -1, x)])
     for k in range(2):
-        w = c("BlkC", 144 * k, 144 * k + 144); up = [[0, 3], [16, 4], [0, 12]]; dn = [[0, 3], [-16, 4], [0, 12]]
+        part = lambda nm: c(nm, 288 * k, 288 * k + 288); w = part("BlkC"); up = [[0, 6], [16, 4], [0, 12]]; dn = [[0, 6], [-16, 4], [0, 12]]; dg = [[0, 6], [-16, 4], [-1, 12]]
         sel(G, w, Z(w), up, ge, 128, 64 * k - 1, -1); sel(G, w, w, up, ge, 0, 64 * k + 15, -1)
-        put(c("DC2", 144 * k, 144 * k + 144), [(dn, -64 * k - 6, -8192), (dn, -64 * k - 14, -1088)])
+        put(part("DC2"), [(dn, -64 * k - 6, -8192), (dn, -64 * k - 14, -1088)]); put(part("Cmp6"), [(dg, -64 * k - 1, 16)]); put(part("Cmq6"), [(dg, -64 * k - 1, -63)])
+        w = part("DH6"); iota(G, w, [[-1, 6], [0, 48]], 47, 0); sel(G, w, w, dn, O.is_equal, 0, -64 * k - 14); put(w, [(dn, -64 * k - 13, 6016), (dg, -64 * k - 1, -256)], False)
     for h in range(16): put(c("SelT", 128 * h, 128 * h + 128), [([[-64, 2], [-1, 4], [0, 16]], -4 * h, 256)])
     put(c("PI"), [rows(6, -0.125)]); put(c("PZ"), [rows(6, -0.125), rows(0, -1)]); put(c("PD"), [rows(6, -4096)]); put(c("AR"), [diag(6, 1)])
     for l in range(1, 6): put(c("BRL", 128 * l - 128, 128 * l), [([[-1, 8], [0, 16]], -8 * (6 - l), 1)])
@@ -315,64 +344,83 @@ def first(G, t, gather):
     vtt(G, c("mk0%d" % t), nc, c(b, 128, 256), O.is_equal); vts(G, c("wr0%d" % t), nc, 0.0, O.max)
 
 
-def slot(p, i): return c("po1" + p, 128 * i, 128 * i + 128) if i < 4 else c("po2" + p, 128 * i - 512, 128 * i - 384)
+def maxima(G, x, m, W, a, b):
+    for r in range(4): vtt(G, c(m, 16 * a + r, 16 * b, 4), c(x, 16 * a + r, 16 * b, 4), c(W, 4 * a, 4 * b), O.max)
 
 
-def records(G, x, m, hu, W):
-    last = None
-    for a, b in zip(CHUNKS, CHUNKS[1:]):
-        last = gat(G, c(x, 16 * a, 16 * b), c("E"), c(hu, a, b))
-        for r in range(4): vtt(G, c(m, 16 * a + r, 16 * b, 4), c(x, 16 * a + r, 16 * b, 4), c(W, 4 * a, 4 * b), O.max)
+def records(G, p):
+    x, m, hu, d = "x" + p, "m" + p, "hu" + p, "po1" + p; a = 16 * NM_
+    gat(G, c(x, a, 2048), c("E"), c(hu, NM_, 128))
+    mm(G, c(d), c("Ib"), c(x, a, 2048), True, False)
+    for r in range(4): mm(G, c(d, r, 512, 4), c("nI"), c("W4" + p), False, r == 3)
+    act(G, c(m, a, 2048), c(d), F.Abs, 0.0, 0.5)
+    for a, b in zip(MCHUNKS, MCHUNKS[1:]):
+        if a == 0: vgat(G, c(x, 16 * a, 16 * b), c("E"), c(hu, a, b))
+        else: last = gat(G, c(x, 16 * a, 16 * b), c("E"), c(hu, a, b))
+        maxima(G, x, m, "pw" + p, a, b)
     return last
 
 
-def scores(G, p, a, t, xb, mb, ks):
-    gid = ("key", p, a, t); key = c("pk" + p, 0, 272); col = lambda k: c("pk" + p, k + 1, 272, 17); at = 0 if a else (272 if p == "A" else 544)
+def scores(G, p, a, t, xb, mb, ks, n):
+    gid = ("key", p, a, t); pk = "pk" + p; key = c(pk, 0, 272); col = lambda k, p0, p1: pc(pk, p0, p1, k + 1, 272, 17); at = 0 if a else (272 if p == "A" else 544)
     mm(G, key, pc("one", 0, 2), pc("cr", 0, 2, at, at + 272), True, False)
-    mm(G, key, c("qa" if p == "A" else "qr%d" % t), c("WN"), False, False, grp=gid)
-    if a: mm(G, c("pk" + p, 0, 136, 17), c("Ib"), c("SP" + p, 0, 128, 16), False, False, grp=gid)
-    else: mm(G, c("pk" + p, 0, 136, 17), c("O%s%d" % (p, t)), c("Pick"), False, False, grp=gid)
+    mm(G, pc(pk, 0, n, 0, 272), c("qa" if p == "A" else "qr%d" % t, 0, n), c("WN"), False, False, grp=gid)
+    if a: mm(G, c(pk, 0, 136, 17), c("Ib"), c("SP" + p, 0, 128, 16), False, False, grp=gid)
+    else: mm(G, c(pk, 0, 136, 17), c("O%s%d" % (p, t)), c("Pick"), False, False, grp=gid)
     for l in [c("mk" + p, 128 * i, 128 * i + 128) for i in range(a + 1)] if a else [c("mk0%d" % t)]: mm(G, key, l, c("BIGP"), False, False, grp=gid)
-    for k in ks: mm(G, col(k), c(xb, k, 2048, 16), c("BX"), False, False, grp=gid)
-    for k in sorted(ks, key=lambda k: k % 4): mm(G, col(k), c(mb, k, 2048, 16), c("BM"), False, False, grp=gid)
+    for k in ks: mm(G, col(k, 0, n), c(xb, k, 16 * n, 16), c("BX"), False, False, grp=gid)
+    for k in sorted(ks, key=lambda k: k % 4): mm(G, col(k, 0, 128), c(mb, k, 2048, 16), c("BM"), False, False, grp=gid)
     mm(G, key, c("wr" + p) if a else c("wr0%d" % t), c("Perm"), False, False)
-    mm(G, c("pk" + p, 136, 272), c("n" + p) if a else c("NC%d" % t), c("nPerm"), False, True)
+    mm(G, c(pk, 136, 272), c("n" + p) if a else c("NC%d" % t), c("nPerm"), False, True)
+
+
+def atom(G, o, p, i, t, x, start, stop):
+    if i: mm(G, o, c("RR%d%s" % (i, p)), c(x), start, stop)
+    else: mm(G, o, c(x), c("O%s%d" % (p, t)), start, stop)
 
 
 def choose(G, p, a, t):
-    RM = "RM" + p; RR = c("RR%d%s" % (a % 2, p)); sp = c("SP" + p, 0, 128, 16)
+    RM = "RM" + p; SP = "SP" + p; RT = "RT" + p; pk = "pk" + p; sp = c(SP, 0, 128, 16)
     path = c("CH%d" % t, 56 + 8 * a, 64 + 8 * a) if p == "A" else c("BL%d" % t, 40 - 8 * a, 48 - 8 * a)
-    vscan(G, c(RM), c("SEG"), c("pk" + p, 0, 272), O.add, O.min)
+    vscan(G, c(RM), c("SEG"), c(pk, 0, 272), O.add, O.min)
     vtt(G, sp if a < ST - 1 else path, c(RM, 16, 136, 17), c(RM, 152, 272, 17), O.subtract)
     if a == ST - 1: return
-    vscan(G, RR, c("S01"), c("SP" + p), O.mult, O.add); vtt(G, c("RD" + p), RR, c("pk" + p, 288, 416), O.mult)
-    mm(G, c("pk" + p, 272, 280), c("RD" + p), c("C8")); vts(G, c("li" + p), c("pk" + p, 272, 280), 512.0, O.add)
-    Q1, Q2 = c("po2" + p, 256, 384), c("po2" + p, 384, 512); was = c("RR%d%s" % ((a - 1) % 2, p)) if a else c("O%s%d" % (p, t))
-    mm(G, c("po2" + p, 256, 512), pc("one", 0, 2), pc("cq", 0, 2), True, False)
-    for o, i in ((Q1, c("I4")), (Q2, c("I2050"))):
-        if a: mm(G, o, was, i, False, False)
-        else: mm(G, o, i, was, False, False)
-    mm(G, Q2, RR, c("I592"), False, True); mm(G, slot(p, a + 1), RR, c("Ib"))
+    vscan(G, c(RT, 0, 128), c("TR"), c(SP, 0, 128), O.mult, O.add); vscan(G, c("RR%d%s" % (a + 1, p)), c("S01"), c(SP, 0, 128), O.mult, O.add)
+    li = c("po1" + p, 0, 8); group(G, li, [(c(SP, 1, 129), c("C8")), (c(RT, 0, 128), c("C8")), (c(RT, 1, 129), c("nC8"))]); vts(G, c("li" + p), li, 512.0, O.add)
+    Q2 = c(pk, 128, 256); mm(G, Q2, pc("one", 0, 2), pc("cq", 0, 2, 128, 256), True, False)
+    atom(G, Q2, p, a, t, "I2050", False, False); atom(G, Q2, p, a + 1, t, "I592", False, True); atom(G, slot(p, a + 1), p, a + 1, t, "Ib", True, True)
     act(G, path, sp)
 
 
+def slot(p, i): return c("po2" + p, 128 * i, 128 * i + 128) if i < 4 else (c("pw" + p, 384, 512) if i == 4 else c("pk" + p, 288, 416))
+
+
+def front(G, p, a, t):
+    n = c("n" + p); q1, li = c("Q1" + p), c("li" + p)
+    vgop(G, c("t1" + p), c("NB"), li, q1, O.mult); gat(G, n, c("NB"), li)
+    vtt(G, c("t2" + p), c("t1" + p), c("pk" + p, 128, 256), O.add); vts(G, c("t3" + p), c("t2" + p), 4, O.arith_shift_right, 4095, O.bitwise_and); vcp(G, c("hu" + p), c("t3" + p)); act(G, c("wr" + p), n, F.Relu)
+    for i in range(a, -1, -1): vtt(G, c("mk" + p, 128 * i, 128 * i + 128), n, slot(p, i), O.is_equal)
+    last = records(G, p)
+    if a < ST - 1: act(G, q1, slot(p, a), F.Identity, 2050.0, 4.0)
+    scores(G, p, a, t, "x" + p, "m" + p, list(range(16)), NM_)
+    return last
+
+
 def walk(G, t):
-    qs = {"A": c("qa"), "B": c("qr%d" % t)}
-    for r in range(4): mm(G, c("po2A", r, 512, 4), c("Ib"), qs["A" if r < 2 else "B"])
-    last = records(G, "xA", "mA", "hu0%d" % t, "po2A")
+    qs = {"A": "qa", "B": "qr%d" % t}
+    for r in range(4): mm(G, c("po1A", r, 512, 4), c("Ib"), c(qs["A" if r < 2 else "B"]))
+    for a, b in zip(CHUNKS, CHUNKS[1:]):
+        (vgat if b == 128 else gat)(G, c("xA", 16 * a, 16 * b), c("E"), c("hu0%d" % t, a, b)); maxima(G, "xA", "mA", "po1A", a, b)
     for p in "BA":
-        mm(G, slot(p, 0), c("Ib"), c("O%s%d" % (p, t)))
-        for r in range(4): mm(G, c("pw" + p, r, 512, 4), c("Ib"), qs[p])
+        atom(G, slot(p, 0), p, 0, t, "Ib", True, True); act(G, c("Q1" + p), c("O%s%d" % (p, t)), F.Identity, 2050.0, 4.0)
+        for r in range(4):
+            mm(G, c("pw" + p, r, 4 * NM_, 4), c("Ib"), c(qs[p], 0, NM_))
+            if p == "B" or t == 0: sel(G, c("W4" + p, r, 128, 4), c(qs[p], NM_, 128), [[0, 128 - NM_]], O.is_ge, 0, 0, 0)
     mm(G, c("pkA", 272, 280), c("OA%d" % t), c("Pick")); act(G, c("CH%d" % t, 48, 56), c("pkA", 272, 280))
-    scores(G, "B", 0, t, "xA", "mA", list(range(8, 16))); scores(G, "A", 0, t, "xA", "mA", list(range(8)))
-    for p in "BA": choose(G, p, 0, t)
+    scores(G, "B", 0, t, "xA", "mA", list(range(8, 16)), 128); scores(G, "A", 0, t, "xA", "mA", list(range(8)), 128)
     for a in range(1, ST):
-        for p in "BA":
-            n = c("n" + p); gat(G, n, c("NB"), c("li" + p))
-            angles(G, p, n, c("po2" + p, 256, 384), c("po2" + p, 384, 512)); vcp(G, c("hu" + p), c("t3" + p))
-            vts(G, c("wr" + p), n, 0.0, O.max)
-            for i in range(a + 1): vtt(G, c("mk" + p, 128 * i, 128 * i + 128), n, slot(p, i), O.is_equal)
-            last = records(G, "x" + p, "m" + p, "hu" + p, "pw" + p); scores(G, p, a, t, "x" + p, "m" + p, list(range(16))); choose(G, p, a, t)
+        for p in "BA": choose(G, p, a - 1, t); last = front(G, p, a, t)
+    for p in "BA": choose(G, p, ST - 1, t)
     return last
 
 
@@ -381,11 +429,11 @@ def rings(G, t):
     if t == 0:
         mm(G, c("po1B", 0, 11), pc("Dmf", 0, 16), pc("R1", 0, 16, 0, 11), True, False); mm(G, c("po1B", 0, 2), pc("Dmf", 0, 16), pc("R2", 0, 16, 0, 2), False, True)
         vcp(G, c("col", 0, 11), c("po1B", 0, 11))
-    mm(G, pc("po2B", 0, 96, 320, 448), c(CH, 0, 96), c("Ib")); vcp(G, pc("CT", 0, 96), pc("po2B", 0, 96, 320, 448))
+    mm(G, pc("po2B", 0, 96, 384, 512), c(CH, 0, 96), c("Ib")); vcp(G, pc("CT", 0, 96), pc("po2B", 0, 96, 384, 512))
     mm(G, c("pkB", 0, 288), pc("CT", 0, 96), pc("DC", 0, 96), True, False)
     for j in range(6): mm(G, c("pkB", 30 + j, 288, 36), c("Ib"), c(CH, 96, 104), False, j == 5)
     vts(G, c("EQ"), c("pkB", 0, 288), 0.0, O.is_equal, 8200.0, O.mult); vscan(G, c("FJ"), c("DJ"), c("EQ"), O.add, O.max)
-    mm(G, pc("po2B", 96, 104, 320, 448), c(CH, 96, 104), c("Ib")); vcp(G, pc("CT", 96, 104), pc("po2B", 96, 104, 320, 448))
+    mm(G, pc("po2B", 96, 104, 384, 512), c(CH, 96, 104), c("Ib")); vcp(G, pc("CT", 96, 104), pc("po2B", 96, 104, 384, 512))
     end = c("FJ", 35, 288, 36); vts(G, c("SPJ", 6, 128, 16), end, -2.5, O.add); vtt(G, c("SPJ", 0, 128, 16), end, c("SPJ", 6, 128, 16), O.subtract)
     vscan(G, c("RRJ"), c("S06"), c("SPJ"), O.mult, O.add); Z = c("pkA", 0, 128); mm(G, Z, c("RRJ"), c("Ib"))
     V1, V2, NN = [c("po1A", 128 * k, 128 * k + 128) for k in range(3)]; NP = c("po1B", 0, 128); Q1, Q2 = c("po2A", 0, 128), c("po2A", 128, 256); k104 = lambda nm: pc(nm, 0, 104)
@@ -397,39 +445,45 @@ def rings(G, t):
     mm(G, NN, c("p4I"), c("dead")); act(G, c("Zs"), Z, F.Identity, col(3))
     vcp(G, c("NS"), NP); angles(G, "A", c("NS"), Q1, Q2); vtt(G, c("HF"), c("t3A"), NN, O.max); vcp(G, c("huA"), c("HF"))
     vts(G, c("hiB"), c("HF"), 1.0 / 64, O.mult, 129.0 - 63.0 / 128, O.add)
-    LO, HI = c("po2B", 0, 96), c("po2B", 96, 192); group(G, LO, [(c("HF"), c("Cmpf")), (c("hiB"), c("Cmp64"))]); group(G, HI, [(c("hiB"), c("Cmp")), (c("dead"), c("Cmp256"))])
+    LO = c("po2B", 0, 96); group(G, LO, [(c("HF"), c("Cmpf")), (c("hiB"), c("Cmp64"))])
     for d in range(2): vts(G, c("LOT", 96 * d, 96 * d + 96), LO, 8256.0 - d, O.add)
+    vts(G, c("LOT", 192, 384), c("LOT", 0, 192), -2.0, O.add)
     for a, b in zip(RCHUNKS, RCHUNKS[1:]): gat(G, c("xA", 16 * a, 16 * b), c("E"), c("huA", a, b))
-    for k in range(2):
-        for d in range(3): act(G, c("HI0", 144 * k + 48 * d, 144 * k + 48 * d + 48), c("po2B", 96 + 48 * k, 144 + 48 * k), F.Identity, -129.0 - d)
-    for u in range(0, 64, 2): vts(G, c("OHL", 96 * u, 96 * u + 192), c("LOT"), float(u), O.is_equal)
+    part = lambda nm, k: c(nm, 288 * k, 288 * k + 288); cnt = (c("pwB", 0, 288), c("po2B", 96, 384))
+    vts(G, c("hqB"), c("HF"), 1.0 / 256, O.mult, 129.0 - 255.0 / 512, O.add)
+    for k, bank in enumerate(("pwA", "pkB")):
+        group(G, c(bank, 0, 288), [(c("dead"), part("DH6", k)), (c("hiB"), part("Cmp6", k)), (c("hqB"), part("Cmq6", k))]); act(G, part("HI0", k), c(bank, 0, 288))
+    for u in range(0, 64, 4): vts(G, c("OHL", 96 * u, 96 * u + 384), c("LOT"), float(u), O.is_equal)
     for a, b in zip(RCHUNKS, RCHUNKS[1:]): group(G, c("po1B", 128 + a, 128 + b), [(c("Ib"), c("xA", 16 * a + r, 16 * b, 16)) for r in range(1, 13)])
-    mm(G, c("pwB", 0, 288), c("dead"), c("DC2"), True, False)
-    vts(G, c("TH"), c("po1B", 128, 256), c("thf"), O.is_ge); mm(G, c("pwB", 0, 288), c("TH"), c("BlkC"), False, True)
-    for k in range(2): vtt(G, c("HIT", 144 * k, 144 * k + 144), c("HI0", 144 * k, 144 * k + 144), c("pwB", 144 * k, 144 * k + 144), O.min)
+    for k in range(2): mm(G, cnt[k], c("dead"), part("DC2", k), True, False)
+    vts(G, c("TH"), c("po1B", 128, 256), c("thf"), O.is_ge)
+    for k in range(2): mm(G, cnt[k], c("TH"), part("BlkC", k), False, True); vtt(G, part("HIT", k), part("HI0", k), cnt[k], O.min)
 
 
 def lessen(G, t, after):
     for k in range(8):
         i = act(G, c("L16", 512 * k, 512 * k + 512), c("E", 512 * k, 512 * k + 512), F.Identity, 1024.375, 0.75); G["ops"][i]["deps"].setdefault(after, False)
     for k, bank in enumerate(("pwA", "pkB")):
-        hit = c("HIT", 144 * k, 144 * k + 144); th = "THH%d" % k; cn = "CN%d" % k
-        for i in range(22):
-            o = c(th, 144 * i, 144 * i + 144)
-            if i < 6: act(G, o, hit, F.Sign, 1.5 - 3 * i)
-            else: vts(G, o, hit, float(3 * i - 2), O.is_ge)
+        hit = c("HIT", 288 * k, 288 * k + 288); th = "THH%d" % k; cn = "CN%d" % k
+        for i in range(11):
+            o = c(th, 288 * i, 288 * i + 288)
+            if i < 3: act(G, o, hit, F.Sign, 1.5 - 6 * i)
+            else: vts(G, o, hit, float(6 * i - 2), O.is_ge)
+        was = len(G["ops"])
         for gl in range(4):
             group(G, pc(bank, 0, 64, gl, 260, 4), [(c("OHL", 48 * k + 12 * gl + s, 6144, 96), c(th, 48 + 12 * gl + s, 3168, 48)) for s in range(12)])
+        if k: G["ops"][was]["deps"].setdefault(done, False)
+        done = len(G["ops"]) - 1
         act(G, pc(cn, 0, 64, 0, 260), pc(bank, 0, 64, 0, 260))
         for b in range(4):
             a = 4 * (16 * b + (1 if b else 0))
             group(G, pc("pkA", 64 * k, 64 * k + 64, 64 * b, 64 * b + 64), [(pc(cn, 0, 64, a, a + 64), pc("Ib", 0, 64, 0, 64)), (pc(cn, 0, 64, a + 4, a + 68), pc("nI", 0, 64, 0, 64))])
     vts(G, c("NM"), c("pkA", 0, 256), 0.0, O.is_equal, 4.0, O.subtract)
     for k in range(8):
-        bank = ("po1A", "po2A", "po2B", "po1B")[k % 4]; e = c("E", 512 * k, 512 * k + 512); o = c(bank, 0, 512); b = k // 2
+        bank = ("po1A", "po2A", "po2B", "po1B")[k % 4]; e = c("E", 512 * k, 512 * k + 512); o = c(bank, 0, 512)
         mm(G, o, c("Ib"), c("L16", 512 * k, 512 * k + 512), True, False)
-        for h in range(8):
-            s = 128 * ((k % 2) * 8 + h); mm(G, c(bank, 64 * h, 64 * h + 64), c("SelT", s, s + 128), c("NM", 64 * b, 64 * b + 64), False, h == 7)
+        for h in range(2): mm(G, c(bank, 256 * h, 256 * h + 256), c("SelT", 256 * k + 128 * h, 256 * k + 128 * h + 128), c("NM"), False, h == 1)
+        if k == 1: G["spread"] = len(G["ops"]) - 1
         vtt(G, e, e, o, O.min)
         if t == RO - 1 and k % 2:
             a = 512 * (k - 1); dma(G, lambda g, T, a=a: g.sync.dma_start(T.ye[:, a:a + 1024], T.E[:, a:a + 1024]), [c("E", a, a + 1024)], [], 2.5)
@@ -443,7 +497,7 @@ def ring_atoms(G, t):
     group(G, c("pwB", 256, 384), [(pc("AR", 0, 104), ct), (c("m4I"), c("r2")), (c("PD"), c("dead"))])
     for l in range(5):
         o = c("pwA", 128 * l, 128 * l + 128) if l < 4 else c("pwB", 384, 512)
-        group(G, o, [(pc("BRL", 0, 104, 128 * l, 128 * l + 128), ct), (c("m4I"), c("ZL", 128 * l, 128 * l + 128))])
+        group(G, o, [(pc("BRL", 0, 104, 128 * l, 128 * l + 128), ct), (c("m4I"), c("ZL", 128 * l, 128 * l + 128))]); G["ops"][-2]["deps"].setdefault(G["spread"], False)
     act(G, c("PB", 0, 256), c("pwB", 256, 512), F.Relu, 513.0); act(G, c("PB", 256, 768), c("pwA"), F.Relu, 513.0)
     group(G, c("pkB", 0, 128), [(c("Ib"), c("PB", 128 * k, 128 * k + 128)) for k in range(6)])
     y = c("YR", 128 * t, 128 * t + 128); act(G, y, c("pkB", 0, 128), F.Identity, -1.0)

@@ -2,67 +2,55 @@ from concourse.bass import DstId, RemoteDMATransfer
 from concourse.mybir import AluOpType as O, ActivationFunctionType as F
 
 N, RO, ST = 4, 3, 6
-CHUNKS = (0, 48, 96, 128)
-MCHUNKS = (0, 32, 64, 96); NM_ = 96
-RCHUNKS = (0, 64, 128)
+CHUNKS = (0, 48, 88, 128)
+MCHUNKS = (0, 32, 64, 80, 96)
+NV, NA = 64, 96
+RCHUNKS = (0, 24, 80, 128)
+NS, KV = 2, 6
 SCRATCH, SHAPE, WIDE, PLACE = {}, {}, {}, {}
-SEMAPHORES = ["sv", "ss", "sp", "sg", "as0", "aq", "ar0", "ar1", "ar2", "loc"] + ["d%d" % i for i in range(20)]
+SEMAPHORES = ["sv", "ss", "sp", "sg", "as0", "as1", "aq0", "aq1", "ar0", "ar1", "ar2", "al0", "al1", "al2", "loc"] + ["d%d" % i for i in range(20)]
 QSEM = {"V": "sv", "S": "ss", "P": "sp", "G": "sg"}
 POOL = {"float32": "poolf", "bfloat16": "poolb", "float16": "poolh", "int32": "pooli", "uint16": "poolu"}
-APART = "stu sr0 sr1 sr2 qa qr0 qr1 qr2 sti thi CH0 CH1 CH2 BL0 BL1 BL2 YR".split()
-
-
-def sb(name, shape, dtype="float32"):
-    SCRATCH[name] = ("sbuf", shape, dtype)
+APART = "stu sr0 sr1 sr2 qa qr0 qr1 qr2 sti thi CH0 CH1 CH2 BL0 BL1 BL2 B60 B61 B62 YR".split()
 
 
 def many(dtype, cols, names):
     for n in names.split():
-        if cols > 816 or n in APART: sb(n, [128, cols], dtype); continue
+        if cols > 816 or n in APART: SCRATCH[n] = ("sbuf", [128, cols], dtype); continue
         pool = SCRATCH.setdefault(POOL[dtype], ("sbuf", [128, 0], dtype)); PLACE[n] = (POOL[dtype], pool[1][1]); SHAPE[n] = [128, cols]; WIDE[n] = dtype in ("float32", "int32")
         pool[1][1] += -(-cols // 32) * 32
 
 
 many("int32", 1024, "nbi"); many("float32", 1024, "NB IDT"); many("bfloat16", 4112, "E"); many("float16", 4096, "L16")
-many("bfloat16", 128, "qa qr0 qr1 qr2"); many("int32", 24, "sti"); many("uint16", 24, "stu sr0 sr1 sr2"); many("int32", 1, "thi"); many("float32", 1, "thf")
-many("int32", 4, "pci"); many("float32", 12, "pcf"); many("float32", 136, "CI S1 GC TK"); many("float32", 128, "CR"); many("float32", 16, "G16"); many("float32", 272, "SEG")
-many("bfloat16", 128, "Ib I4 I592 dA dB dA4 dB4 Dm S01 TR nI one W4A W4B"); many("float16", 128, "I2050 dA26 dB26"); many("float16", 256, "cq")
-many("bfloat16", 272, "Perm BIGP WN"); many("bfloat16", 136, "nPerm"); many("bfloat16", 816, "cr"); many("bfloat16", 16, "BX BM BA"); many("bfloat16", 8, "C8 nC8 Pick")
-many("bfloat16", 288, "Zb DC"); many("bfloat16", 576, "BlkC DC2 Cmp6 Cmq6 DH6"); many("float16", 288, "Zh DJ"); many("float32", 128, "Zf Dmf"); many("float32", 16, "R1 R2 col")
-many("bfloat16", 128, "CN CQ1 CV1a CV1b CV2 SA SA592 SB4 S06 PZ PI PD AR I16 m4I p4I"); many("float16", 128, "CQ2 SB2050"); many("bfloat16", 640, "BRL")
-many("float32", 96, "Cmpf"); many("bfloat16", 96, "Cmp64"); many("bfloat16", 2048, "SelT")
-many("float16", 128, "CT SPJ RRJ Y1 Y2 NS tnA tnB"); many("float16", 288, "EQ"); many("float32", 288, "FJ"); many("bfloat16", 128, "OH dead hiB hqB TH Zs r1 r2"); many("float32", 128, "HF")
-many("bfloat16", 384, "LOT"); many("bfloat16", 576, "HI0 HIT"); many("bfloat16", 6144, "OHL"); many("bfloat16", 3168, "THH0 THH1"); many("float16", 264, "CN0 CN1")
-many("bfloat16", 256, "NM"); many("bfloat16", 640, "ZL"); many("float16", 768, "PB"); many("float32", 384, "YR")
+many("bfloat16", 128, "qa qr0 qr1 qr2"); many("int32", 24, "sti"); many("uint16", 24, "stu"); many("uint16", 8, "sr0 sr1 sr2"); many("int32", 1, "thi"); many("float32", 1, "thf")
+many("uint16", 8, "lW4"); many("int32", 4, "pci"); many("float32", 12, "pcf"); many("float32", 136, "CI S1 GC TK"); many("float32", 128, "CR"); many("float32", 16, "G16"); many("float32", 272, "SEG")
+many("bfloat16", 128, "Ib I592 dA dB dA4 dB4 Dm S01 TR nI one W4A W4B"); many("float16", 128, "I2050 dA26 dB26"); many("float16", 256, "cq")
+many("bfloat16", 272, "Perm BIGP WN"); many("bfloat16", 136, "nPerm"); many("bfloat16", 816, "cr"); many("bfloat16", 16, "BX BM"); many("bfloat16", 8, "C8 nC8 Pick")
+many("bfloat16", 288, "Zb DC"); many("bfloat16", 384, "BlkC DC2 C5 C8x C9 DH"); many("float16", 288, "Zh DJ"); many("float32", 128, "Zf Dmf"); many("float32", 16, "R1 R2 col")
+many("bfloat16", 128, "CN CQ1 CV1a CV1b CV2 SA SA592 SB4 S06 S0n PZ PI PD AR I16 m4I p4I I1k"); many("float16", 128, "CQ2 SB2050"); many("bfloat16", 640, "BRL")
+many("float32", 96, "Cmpf"); many("bfloat16", 96, "Cm5 Cm8 Cm9"); many("bfloat16", 2048, "SelT")
+many("float16", 128, "CT Y1 Y2 NR0 tnA tnB h5B SPY RRY"); many("float16", 288, "EQ"); many("float32", 288, "FJ"); many("bfloat16", 128, "OH dead h8B h9B TH Zs r1 r2 SPJ RRJ"); many("float32", 128, "HF")
+many("bfloat16", 384, "LOT HI0 HIT"); many("bfloat16", 192, "AB0 AB1"); many("bfloat16", 6144, "OHL"); many("bfloat16", 3072, "THH0 THH1")
+many("bfloat16", 256, "NR NM"); many("bfloat16", 640, "ZL"); many("bfloat16", 1024, "DD"); many("float16", 768, "PB"); many("float32", 384, "YR")
 for _p in "AB":
-    for _d, _c, _l in (("float16", 128, "n wr RR1 RR2 RR3 RR4 RR5"), ("float16", 144, "SP RT"), ("float32", 128, "t1 Q1"), ("int32", 128, "t2 t3"), ("uint16", 128, "hu"), ("bfloat16", 2048, "x m"), ("bfloat16", 768, "mk"),
-                       ("float32", 272, "RM"), ("uint16", 8, "li")):
+    for _d, _c, _l in (("float16", 128, "n wr RR1 RR2 RR3 RR4 RR5"), ("float16", 144, "SP RT"), ("float32", 128, "t1 Q1"), ("int32", 128, "t2 t3"), ("uint16", 128, "hu"),
+                       ("bfloat16", 2048, "x m"), ("bfloat16", 768, "mk"), ("float32", 272, "RM"), ("uint16", 8, "li")):
         many(_d, _c, " ".join(n + _p for n in _l.split()))
-    for _n in ("k", "w", "o1", "o2"): SCRATCH["p" + _n + _p] = ("psum", [128, 512], "float32")
+    for _n in "kwds": SCRATCH["p" + _n + _p] = ("psum", [128, 512], "float32")
 for _t in range(RO):
     many("uint16", 128, "hu0%d" % _t); many("bfloat16", 128, "mk0%d" % _t); many("float16", 128, "NC%d wr0%d OA%d OB%d" % (_t, _t, _t, _t))
-    many("float16", 104, "CH%d" % _t); many("float16", 48, "BL%d" % _t)
+    many("float16", 104, "CH%d" % _t); many("float16", 48, "BL%d" % _t); many("float16", 8, "B6%d" % _t)
 SHAPE.update({k: s[1] for k, s in SCRATCH.items()})
 PSUM = {k for k, s in SCRATCH.items() if s[0] == "psum"}
 WIDE.update({k: s[2] in ("float32", "int32") for k, s in SCRATCH.items()})
 
 
-def v(name, *idx):
-    sh = SHAPE[name]; reg = []; n = 1; full = list(idx) + [slice(None)] * (len(sh) - len(idx)); off = PLACE[name][1] if name in PLACE else 0
-    for i, (ix, d) in enumerate(zip(full, sh)):
-        a, b, s = ix.indices(d); k = len(range(a, b, s)); reg.append((a, a + (k - 1) * s + 1, s))
-        if i: n *= k
-        if i == 1: full[i] = slice(a + off, a + off + (k - 1) * s + 1, s)
-    return (name, tuple(full), tuple(reg), n)
+def pc(name, p0, p1, a=None, b=None, s=None):
+    a, b, s = slice(a, b, s).indices(SHAPE[name][1]); k = len(range(a, b, s)); b = a + (k - 1) * s + 1; off = PLACE[name][1] if name in PLACE else 0
+    return (name, (slice(p0, p1), slice(a + off, b + off, s)), ((p0, p1, 1), (a, b, s)), k)
 
 
-ALL = slice(None)
-
-
-def c(name, a=None, b=None, s=None): return v(name, ALL, slice(a, b, s))
-
-
-def pc(name, p0, p1, a=None, b=None, s=None): return v(name, slice(p0, p1), slice(a, b, s))
+def c(name, a=None, b=None, s=None): return pc(name, 0, 128, a, b, s)
 
 
 def ap(T, w): return T[PLACE[w[0]][0] if w[0] in PLACE else w[0]][w[1]]
@@ -92,14 +80,17 @@ def add(G, q, fn, R, W, dur, grp=None, sem=None, gn=0):
                 if grp is None: now = []
             G["acc"][name] = (q, was, now + [(i, grp)]); continue
         for e in G["acc"].get(name, ()):
-            j, r2, w2, g2 = e
+            j, r2, w2 = e
             if j == i: keep.append(e); continue
             ov = overlap(reg, r2)
             if ov and (isw or w2): deps[j] = True
             if not (isw and ov and covers(reg, r2)): keep.append(e)
-        keep.append((i, reg, isw, grp)); G["acc"][name] = keep
-    G["ops"].append({"q": q, "fn": fn, "deps": deps, "dur": dur, "sem": sem, "to": W[0][0] if W else "", "gn": gn, "late": G["late"][0]})
+        keep.append((i, reg, isw)); G["acc"][name] = keep
+    G["ops"].append({"q": q, "fn": fn, "deps": deps, "dur": dur, "sem": sem, "to": W[0][0] if W else "", "gn": gn})
     return i
+
+
+def behind(G, i, j): G["ops"][i]["deps"].setdefault(j, False)
 
 
 VC, GR, PC = 0.00083, 1.56, 0.00042
@@ -135,15 +126,18 @@ def vscan(G, o, a, b, op0, op1):
     add(G, "V", lambda g, T: g.vector.tensor_tensor_scan(ap(T, o), ap(T, a), ap(T, b), 0.0, op0, op1), [a, b], [o], vcost(o[3], 0.5 if two(o, a, b) else 1))
 
 
+def vtr(G, o, a): add(G, "V", lambda g, T: g.vector.transpose(ap(T, o), ap(T, a)), [a], [o], vcost(o[3], 0.5 if two(o, a) else 1))
+
+
 def vset(G, o, x): add(G, "V", lambda g, T: g.vector.memset(ap(T, o), x), [], [o], vcost(o[3], 0.5 if two(o) else 1))
 
 
 def vgat(G, o, w, off):
-    add(G, "V", lambda g, T: g.vector.tensor_copy(ap(T, o), ap(T, w).indirect(ap(T, off))), [w, off], [o], o[3] * VC * GR + 0.05, gn=o[3])
+    return add(G, "V", lambda g, T: g.vector.tensor_copy(ap(T, o), ap(T, w).indirect(ap(T, off))), [w, off], [o], o[3] * VC * GR + 0.05, gn=o[3])
 
 
 def vgop(G, o, w, off, b, op):
-    add(G, "V", lambda g, T: g.vector.tensor_tensor(ap(T, o), ap(T, w).indirect(ap(T, off)), ap(T, b), op), [w, off, b], [o], o[3] * VC * GR + 0.05, gn=o[3])
+    add(G, "V", lambda g, T: g.vector.tensor_tensor(ap(T, o), ap(T, w).indirect(ap(T, off)), ap(T, b), op), [w, off, b], [o], o[3] * VC * 2 + 0.05)
 
 
 def act(G, o, a, func=F.Copy, bias=0.0, scale=1.0):
@@ -155,29 +149,29 @@ def gat(G, o, w, off):
 
 
 def mm(G, o, l, r, start=True, stop=True, grp=None):
-    add(G, "P", lambda g, T: g.tensor.matmul(ap(T, o), ap(T, l), ap(T, r), start, stop), [l, r], [o], max(min(64, l[3]), r[3]) * (4 if WIDE[l[0]] else 1) * PC, grp=grp)
+    return add(G, "P", lambda g, T: g.tensor.matmul(ap(T, o), ap(T, l), ap(T, r), start, stop), [l, r], [o], max(min(64, l[3]), r[3]) * (4 if WIDE[l[0]] else 1) * PC, grp=grp)
 
 
 def group(G, o, terms):
-    for i, (l, r) in enumerate(terms): mm(G, o, l, r, i == 0, i == len(terms) - 1)
+    return [mm(G, o, l, r, i == 0, i == len(terms) - 1) for i, (l, r) in enumerate(terms)]
 
 
 def iota(G, o, pat, base, cm, small=True):
     def fn(g, T):
         if small: return g.iota(ap(T, o), pat, base, cm, allow_small_or_imprecise_dtypes=True)
         return g.iota(ap(T, o), pat, base, cm)
-    add(G, "G", fn, [], [o], 0.13 + o[3] * 2 * VC)
+    add(G, "G", fn, [], [o], 1.25 * (0.13 + o[3] * 2 * VC))
 
 
 def sel(G, o, a, pat, op, fill, base, cm=1):
-    add(G, "G", lambda g, T: g.affine_select(ap(T, o), ap(T, a), pat, op, float(fill), base, cm), [a], [o], 0.17 + o[3] * 2 * VC)
+    add(G, "G", lambda g, T: g.affine_select(ap(T, o), ap(T, a), pat, op, float(fill), base, cm), [a], [o], 1.25 * (0.17 + o[3] * 2 * VC))
 
 
 def dma(G, fn, R, W, dur):
     k = "d%d" % G["nd"][0]; G["nd"][0] += 1; add(G, "Y", fn, R, W, dur, sem=(k, 16))
 
 
-PASSES = 3; SAME, CROSS = 0.15, 0.25
+PASSES = 3; SAME, CROSS = 0.2, 0.27
 LATER = {"Vm": 2.0, "Vmk": 2.0, "Swr": 2.0}
 
 
@@ -191,21 +185,20 @@ def schedule(G):
     far = [0.0] * n; pr = [0.0] * n
     for i in range(n - 1, -1, -1):
         far[i] = ops[i]["dur"] + max([far[s] + lat(i, s) for s in succ[i]] + [0.0]); pr[i] = far[i] - LATER.get(ops[i]["q"] + ops[i]["to"][:-1], 0.0)
-    free = {q: 0.0 for q in "VSPGYN"}; ready = {q: [] for q in free}; rt = [0.0] * n; order = []
+    free = {q: 0.0 for q in "VSPGYN"}; ready = {q: [] for q in free}; rt = [0.0] * n; at = [0.0] * n
     for i in range(n):
         if not need[i]: ready[ops[i]["q"]].append(i)
-    while len(order) < n:
+    for _ in range(n):
         best = None
         for q in free:
             if not ready[q]: continue
             t0 = max(free[q], min(rt[i] for i in ready[q]))
             i = max((j for j in ready[q] if rt[j] <= t0 + 1e-9), key=lambda j: (pr[j], -j))
             if best is None or t0 < best[0]: best = (t0, i)
-        t0, i = best; q = ops[i]["q"]; ready[q].remove(i); order.append(i); end = t0 + ops[i]["dur"]; free[q] = end if q in QSEM else t0 + 0.1
+        t0, i = best; q = ops[i]["q"]; ready[q].remove(i); at[i] = t0; end = t0 + ops[i]["dur"]; free[q] = end if q in QSEM else t0 + 0.1
         for s in succ[i]:
             rt[s] = max(rt[s], end + lat(i, s)); need[s] -= 1
             if not need[s]: ready[ops[s]["q"]].append(s)
-        ops[i]["t"] = (t0, end)
     pred = [list(o["deps"]) for o in ops]; dur = [o["dur"] for o in ops]
 
     def place(seq, before, gap):
@@ -222,7 +215,7 @@ def schedule(G):
                 a.insert(lo, t0); b.insert(lo, t0 + dur[i])
             at[i] = t0
         return at
-    at = [o["t"][0] for o in ops]; best = (max(at[i] + dur[i] for i in range(n)), at)
+    best = (max(at[i] + dur[i] for i in range(n)), at)
     for _ in range(PASSES):
         back = place(sorted(range(n), key=lambda i: -at[i] - dur[i]), succ, lambda d, i: lat(i, d))
         at = place(sorted(range(n), key=lambda i: -back[i] - dur[i]), pred, lat); end = max(at[i] + dur[i] for i in range(n))
@@ -259,20 +252,23 @@ def emit(G, order, g, T):
 
 def walk_constants(G):
     iota(G, c("pci", 0, 1), [[0, 1]], 0, 1, False)
-    iota(G, c("CI"), [[1, 136]], 0, 0); iota(G, c("IDT"), [[1, 1024]], -512, 0); iota(G, c("G16"), [[0, 2], [1, 8]], 0, 0)
+    iota(G, c("CI"), [[1, 136]], 0, 0); iota(G, c("G16"), [[0, 2], [1, 8]], 0, 0)
+    for k in range(8): act(G, c("IDT", 128 * k, 128 * k + 128), c("CI", 0, 128), F.Identity, 128.0 * k - 512)
     iota(G, c("CR"), [[0, 8], [1, 16]], 0, 0); iota(G, c("S1"), [[0, 8], [1, 17]], -1, 0); iota(G, c("GC"), [[1, 8], [0, 17]], 0, 0)
     p = c("pci", 0, 1); vts(G, c("pci", 1, 2), p, 15, O.bitwise_and); vts(G, c("pci", 2, 3), p, 4, O.arith_shift_right); vcp(G, c("pcf", 0, 3), c("pci", 0, 3))
+    vts(G, c("pci", 3, 4), p, 2, O.arith_shift_right, 3, O.bitwise_and); vts(G, c("pcf", 11, 12), c("pci", 3, 4), float(NA), O.add)
+    vts(G, c("lW4"), c("CI", 0, 8), 4.0, O.mult, c("pcf", 11, 12), O.add)
     P, PR, PG, SL, ha, hb, R0, k1, k2, k3, k4 = [c("pcf", k, k + 1) for k in range(11)]
     vts(G, SL, P, PG, O.add, 1.0, O.add); vts(G, ha, PR, 7.5, O.is_le); vts(G, hb, PR, 7.5, O.is_ge); vts(G, R0, PR, 0.0, O.is_equal)
     vts(G, c("Ib"), c("CI", 0, 128), P, O.is_equal)
-    for nm, x in (("I4", 4.0), ("I592", 592.0), ("I2050", 2050.0), ("nI", -1.0)): vts(G, c(nm), c("Ib"), x, O.mult)
+    for nm, x in (("I592", 592.0), ("I2050", 2050.0), ("nI", -1.0)): vts(G, c(nm), c("Ib"), x, O.mult)
     for h, col in (("A", ha), ("B", hb)):
         for nm, x in (("", 1.0), ("4", 4.0), ("26", 2642.0)): vts(G, c("d" + h + nm), c("Ib"), col, O.mult, x, O.mult)
     vset(G, pc("one", 0, 2), 1.0)
     vset(G, pc("cq", 0, 2, 0, 128), 0.0); vset(G, pc("cq", 0, 2, 128, 256), 1.0); vset(G, pc("cq", 0, 1, 0, 128), 2050.0); vset(G, pc("cq", 0, 1, 128, 256), 43008.0)
     vts(G, c("Dm"), c("CR"), PR, O.is_equal); vts(G, c("S01"), c("CR"), 0.0, O.not_equal); vts(G, c("TR"), c("CR"), PR, O.is_le); vset(G, c("TR", 0, 128, 16), 0.0)
     vts(G, c("C8"), c("G16", 0, 8), PG, O.is_equal); vts(G, c("Pick"), c("C8"), R0, O.mult); vts(G, c("nC8"), c("C8"), -1.0, O.mult)
-    vts(G, c("BX"), c("G16"), PG, O.is_equal, -8192.0, O.mult); vts(G, c("BM"), c("BX"), -2.0, O.mult); vts(G, c("BA"), c("BX"), -1.0, O.mult)
+    vts(G, c("BX"), c("G16"), PG, O.is_equal, -8192.0, O.mult); vts(G, c("BM"), c("BX"), -2.0, O.mult)
     for h in (0, 136):
         vts(G, c("Perm", h, h + 136), c("CI"), SL, O.is_equal); vts(G, c("WN", h, h + 136), c("GC"), PG, O.is_equal, -8192.0, O.mult)
         vts(G, c("SEG", h, h + 136), c("S1"), -1.0, O.is_equal, 2.0 ** 30, O.mult)
@@ -291,8 +287,8 @@ def walk_constants(G):
 
 def ring_constants(G):
     ne, ge = O.not_equal, O.is_ge
-    vset(G, c("Zb"), 0.0); vset(G, c("Zh"), 0.0); vset(G, c("Zf"), 0.0); vset(G, c("SPJ"), 0.0); vcp(G, c("Dmf"), c("Dm"))
-    for k in "01": vset(G, c("CN" + k, 260, 264), 0.0)
+    vset(G, c("Zb"), 0.0); vset(G, c("Zh"), 0.0); vset(G, c("Zf"), 0.0); vset(G, c("SPJ"), 0.0); vset(G, c("SPY"), 0.0); vcp(G, c("Dmf"), c("Dm"))
+    for t in range(RO): vset(G, c("CH%d" % t, 0, 8), 0.0)
     Z = lambda w: c("Zf" if WIDE[w[0]] else ("Zh" if PLACE.get(w[0], ("",))[0] == "poolh" else "Zb"), 0, w[3])
 
     def put(w, items, fresh=True):
@@ -301,46 +297,46 @@ def ring_constants(G):
     rows = lambda r, x: ([[-16, 8], [0, 16]], -r, x)
     rcol = [[0, 8], [1, 16]]
     put(c("DC"), [([[-1, 8], [-8, 6], [0, 6]], -56, 1), ([[-1, 8], [0, 6], [8, 6]], -40, -1)])
-    sel(G, c("DJ"), c("Zh"), [[0, 288]], O.is_gt, 1, 0, 0); sel(G, c("DJ"), c("DJ"), [[0, 48], [1, 6]], ne, 3, 0, 0); sel(G, c("DJ"), c("DJ"), [[0, 8], [1, 36]], ge, -60000, -2, 0)
-    sel(G, c("S06"), c("S01"), rcol, ne, 0, -6, 0)
+    sel(G, c("DJ"), c("Zh"), [[0, 288]], O.is_gt, 1 / 1024, 0, 0); sel(G, c("DJ"), c("DJ"), [[0, 48], [1, 6]], ne, 3 / 1024, 0, 0); sel(G, c("DJ"), c("DJ"), [[0, 8], [1, 36]], ge, -4, -2, 0)
+    sel(G, c("S06"), c("S01"), rcol, ne, 0, -6, 0); sel(G, c("S0n"), c("S01"), rcol, ne, -1, -6, 0)
     q = lambda nm, a, b: pc(nm, 0, 16, a, b); one = [[0, 1]]
-    iota(G, q("R1", 0, 2), [[0, 2]], 8296, -8); sel(G, q("R1", 0, 2), q("R1", 0, 2), [[0, 2]], ge, 0, -6); iota(G, q("R1", 2, 3), one, 1, 0)
-    for k, x in ((1, -8000), (2, -1)):
+    iota(G, q("R1", 0, 2), [[0, 2]], 1128, -8); sel(G, q("R1", 0, 2), q("R1", 0, 2), [[0, 2]], ge, 0, -6); iota(G, q("R1", 2, 3), one, 1, 0)
+    for k, x in ((1, -1000), (2, -1)):
         for r in (6, 12): sel(G, q("R1", k, k + 1), q("R1", k, k + 1), one, ne, x, -r)
     sel(G, q("R1", 1, 3), q("R1", 1, 3), [[0, 2]], ge, 0, 12, -1)
-    iota(G, q("R1", 3, 4), one, -8200, 0); sel(G, q("R1", 3, 4), q("R1", 3, 4), one, ge, 0, -6)
+    iota(G, q("R1", 3, 4), one, -1032, 0); sel(G, q("R1", 3, 4), q("R1", 3, 4), one, ge, 8, -6)
     iota(G, q("R1", 4, 9), [[-1, 5]], 11, -1); iota(G, q("R1", 9, 10), one, 7, -1); iota(G, q("R1", 10, 11), one, -6, 1)
-    iota(G, q("R2", 0, 2), [[0, 2]], 0, 1); sel(G, q("R2", 0, 2), q("R2", 0, 2), [[0, 2]], ge, 0, 5, -1)
+    iota(G, q("R2", 0, 2), [[0, 2]], -8, 1); sel(G, q("R2", 0, 2), q("R2", 0, 2), [[0, 2]], ge, 0, 5, -1)
     put(c("CN"), [diag(-1, 1)]); sel(G, c("CV1a"), c("CN"), rcol, ge, 0, -7, 0); sel(G, c("CN"), c("CN"), rcol, ne, 0, -12, 0)
     put(c("CV1b"), [diag(1, 1)]); sel(G, c("CV1b"), c("CV1b"), [[0, 8], [-1, 16]], ge, 0, 5, 0); put(c("CV2"), [diag(0, 1)])
     put(c("CQ1"), [diag(1, 4)]); put(c("CQ2"), [diag(0, 592)]); sel(G, c("CQ2"), c("CQ2"), rcol, ne, 0, -12, 0); put(c("CQ2"), [diag(1, 2050)], False)
-    for nm, x, lo, hi in (("SA", 1, 6, 15), ("SB4", 4, 0, 5), ("SB2050", 2050, 0, 5), ("SA592", 592, 6, 15)):
+    for nm, x, lo, hi in (("SA", 1, 6, 15), ("SB4", 4, 0, 5)):
         w = c(nm); sel(G, w, Z(w), rcol, ne, x, -12, 0); sel(G, w, w, [[-16, 8], [0, 16]], ge, 0, -lo); sel(G, w, w, [[16, 8], [0, 16]], ge, 0, hi, -1)
-    for nm, x in (("p4I", 4096), ("I16", 16), ("m4I", -4096)): put(c(nm), [([[-1, 128]], 0, x)])
-    for nm, x in (("Cmpf", 1), ("Cmp64", -64)): put(c(nm), [([[-16, 8], [-1, 12]], -1, x)])
+    put(c("Cm8"), [([[-16, 8], [-1, 12]], -1, 32)])
     for k in range(2):
-        part = lambda nm: c(nm, 288 * k, 288 * k + 288); w = part("BlkC"); up = [[0, 6], [16, 4], [0, 12]]; dn = [[0, 6], [-16, 4], [0, 12]]; dg = [[0, 6], [-16, 4], [-1, 12]]
+        part = lambda nm: c(nm, 192 * k, 192 * k + 192); w = part("BlkC"); up = [[0, 4], [16, 4], [0, 12]]; dn = [[0, 4], [-16, 4], [0, 12]]; dg = [[0, 4], [-16, 4], [-1, 12]]
         sel(G, w, Z(w), up, ge, 128, 64 * k - 1, -1); sel(G, w, w, up, ge, 0, 64 * k + 15, -1)
-        put(part("DC2"), [(dn, -64 * k - 6, -8192), (dn, -64 * k - 14, -1088)]); put(part("Cmp6"), [(dg, -64 * k - 1, 16)]); put(part("Cmq6"), [(dg, -64 * k - 1, -63)])
-        w = part("DH6"); iota(G, w, [[-1, 6], [0, 48]], 47, 0); sel(G, w, w, dn, O.is_equal, 0, -64 * k - 14); put(w, [(dn, -64 * k - 13, 6016), (dg, -64 * k - 1, -256)], False)
-    for h in range(16): put(c("SelT", 128 * h, 128 * h + 128), [([[-64, 2], [-1, 4], [0, 16]], -4 * h, 256)])
+        put(part("DC2"), [(dn, -64 * k - 6, -8192), (dn, -64 * k - 14, -1088)]); put(part("C9"), [(dg, -64 * k - 1, 1)])
+        w = part("DH"); iota(G, w, [[-1, 4], [0, 48]], -73, 0); sel(G, w, w, dn, O.is_equal, 0, -64 * k - 14); put(w, [(dg, -64 * k - 1, -256)], False)
+    for nm, a, x in (("I1k", "Ib", 1024), ("p4I", "Ib", 4096), ("I16", "Ib", 16), ("m4I", "Ib", -4096), ("SA592", "SA", 592), ("SB2050", "SB4", 512.5),
+                     ("Cmpf", "Cm8", 1 / 32), ("Cm5", "Cm8", -1), ("Cm9", "Cm8", -2), ("C5", "C9", 8), ("C8x", "C9", -64)): act(G, c(nm), c(a), F.Identity, 0.0, float(x))
+    for h in range(16): put(c("SelT", 128 * h, 128 * h + 128), [([[-64, 2], [-1, 4], [0, 16]], -32 * (h % 2) - 4 * (h // 2), 256 if h < 2 * KV else -256)])
     put(c("PI"), [rows(6, -0.125)]); put(c("PZ"), [rows(6, -0.125), rows(0, -1)]); put(c("PD"), [rows(6, -4096)]); put(c("AR"), [diag(6, 1)])
     for l in range(1, 6): put(c("BRL", 128 * l - 128, 128 * l), [([[-1, 8], [0, 16]], -8 * (6 - l), 1)])
 
 
-def angles(G, p, n, Q1, Q2):
-    t1, t2, t3 = c("t1" + p), c("t2" + p), c("t3" + p)
-    vtt(G, t1, n, Q1, O.mult); vtt(G, t2, t1, Q2, O.add); vts(G, t3, t2, 4, O.arith_shift_right, 4095, O.bitwise_and)
+def angles(G, p, Q2):
+    vtt(G, c("t2" + p), c("t1" + p), Q2, O.add); vts(G, c("t3" + p), c("t2" + p), 4, O.arith_shift_right, 4095, O.bitwise_and)
 
 
 def first(G, t, gather):
-    sa, sb_ = c("stu", 8 * t, 8 * t + 8), c("sr%d" % t, 8 * t, 8 * t + 8); oa, ob, nc = c("OA%d" % t), c("OB%d" % t), c("NC%d" % t); b = "pwB"
+    sa, sb_ = c("stu", 8 * t, 8 * t + 8), c("sr%d" % t); oa, ob, nc = c("OA%d" % t), c("OB%d" % t), c("NC%d" % t); b = "pwB"
     gather(G, oa, c("IDT"), sa); gather(G, c("tnA"), c("NB"), sa); gather(G, ob, c("IDT"), sb_); gather(G, c("tnB"), c("NB"), sb_)
     group(G, c(b, 0, 128), [(c("dA"), c("tnA")), (c("dB"), c("tnB"))])
     mm(G, c(b, 256, 512), pc("one", 0, 2), pc("cq", 0, 2), True, False)
     for h, o in (("A", oa), ("B", ob)): mm(G, c(b, 256, 384), c("d%s4" % h), o, False, False); mm(G, c(b, 384, 512), c("d%s26" % h), o, False, h == "B")
     group(G, c(b, 128, 256), [(c("dA"), oa), (c("dB"), ob)])
-    vcp(G, nc, c(b, 0, 128)); angles(G, "B", nc, c(b, 256, 384), c(b, 384, 512)); vcp(G, c("hu0%d" % t), c("t3B"))
+    vcp(G, nc, c(b, 0, 128)); vtt(G, c("t1B"), nc, c(b, 256, 384), O.mult); angles(G, "B", c(b, 384, 512)); vcp(G, c("hu0%d" % t), c("t3B"))
     vtt(G, c("mk0%d" % t), nc, c(b, 128, 256), O.is_equal); vts(G, c("wr0%d" % t), nc, 0.0, O.max)
 
 
@@ -349,27 +345,28 @@ def maxima(G, x, m, W, a, b):
 
 
 def records(G, p):
-    x, m, hu, d = "x" + p, "m" + p, "hu" + p, "po1" + p; a = 16 * NM_
-    gat(G, c(x, a, 2048), c("E"), c(hu, NM_, 128))
+    x, m, hu, d = "x" + p, "m" + p, "hu" + p, "pd" + p; a = 16 * NA
+    gat(G, c(x, a, 2048), c("E"), c(hu, NA, 128))
     mm(G, c(d), c("Ib"), c(x, a, 2048), True, False)
     for r in range(4): mm(G, c(d, r, 512, 4), c("nI"), c("W4" + p), False, r == 3)
     act(G, c(m, a, 2048), c(d), F.Abs, 0.0, 0.5)
     for a, b in zip(MCHUNKS, MCHUNKS[1:]):
-        if a == 0: vgat(G, c(x, 16 * a, 16 * b), c("E"), c(hu, a, b))
+        if a >= NV: vgat(G, c(x, 16 * a, 16 * b), c("E"), c(hu, a, b))
         else: last = gat(G, c(x, 16 * a, 16 * b), c("E"), c(hu, a, b))
         maxima(G, x, m, "pw" + p, a, b)
     return last
 
 
-def scores(G, p, a, t, xb, mb, ks, n):
-    gid = ("key", p, a, t); pk = "pk" + p; key = c(pk, 0, 272); col = lambda k, p0, p1: pc(pk, p0, p1, k + 1, 272, 17); at = 0 if a else (272 if p == "A" else 544)
+def scores(G, p, a, t, xb, mb, ks):
+    gid = ("key", p, a, t); pk = "pk" + p; key = c(pk, 0, 272); col = lambda k, n: pc(pk, 0, n, k + 1, 272, 17); at = 0 if a else (272 if p == "A" else 544)
+    nx = NA if a else 128
     mm(G, key, pc("one", 0, 2), pc("cr", 0, 2, at, at + 272), True, False)
-    mm(G, pc(pk, 0, n, 0, 272), c("qa" if p == "A" else "qr%d" % t, 0, n), c("WN"), False, False, grp=gid)
+    mm(G, pc(pk, 0, nx, 0, 272), c("qa" if p == "A" else "qr%d" % t, 0, nx), c("WN"), False, False, grp=gid)
     if a: mm(G, c(pk, 0, 136, 17), c("Ib"), c("SP" + p, 0, 128, 16), False, False, grp=gid)
     else: mm(G, c(pk, 0, 136, 17), c("O%s%d" % (p, t)), c("Pick"), False, False, grp=gid)
     for l in [c("mk" + p, 128 * i, 128 * i + 128) for i in range(a + 1)] if a else [c("mk0%d" % t)]: mm(G, key, l, c("BIGP"), False, False, grp=gid)
-    for k in ks: mm(G, col(k, 0, n), c(xb, k, 16 * n, 16), c("BX"), False, False, grp=gid)
-    for k in sorted(ks, key=lambda k: k % 4): mm(G, col(k, 0, 128), c(mb, k, 2048, 16), c("BM"), False, False, grp=gid)
+    for k in ks: mm(G, col(k, nx), c(xb, k, 16 * nx, 16), c("BX"), False, False, grp=gid)
+    for k in sorted(ks, key=lambda k: k % 4): mm(G, col(k, 128), c(mb, k, 2048, 16), c("BM"), False, False, grp=gid)
     mm(G, key, c("wr" + p) if a else c("wr0%d" % t), c("Perm"), False, False)
     mm(G, c(pk, 136, 272), c("n" + p) if a else c("NC%d" % t), c("nPerm"), False, True)
 
@@ -379,6 +376,9 @@ def atom(G, o, p, i, t, x, start, stop):
     else: mm(G, o, c(x), c("O%s%d" % (p, t)), start, stop)
 
 
+def slot(p, i): return c("ps" + p, 128 * i, 128 * i + 128) if i < 4 else (c("pw" + p, 384, 512) if i == 4 else c("pk" + p, 288, 416))
+
+
 def choose(G, p, a, t):
     RM = "RM" + p; SP = "SP" + p; RT = "RT" + p; pk = "pk" + p; sp = c(SP, 0, 128, 16)
     path = c("CH%d" % t, 56 + 8 * a, 64 + 8 * a) if p == "A" else c("BL%d" % t, 40 - 8 * a, 48 - 8 * a)
@@ -386,38 +386,33 @@ def choose(G, p, a, t):
     vtt(G, sp if a < ST - 1 else path, c(RM, 16, 136, 17), c(RM, 152, 272, 17), O.subtract)
     if a == ST - 1: return
     vscan(G, c(RT, 0, 128), c("TR"), c(SP, 0, 128), O.mult, O.add); vscan(G, c("RR%d%s" % (a + 1, p)), c("S01"), c(SP, 0, 128), O.mult, O.add)
-    li = c("po1" + p, 0, 8); group(G, li, [(c(SP, 1, 129), c("C8")), (c(RT, 0, 128), c("C8")), (c(RT, 1, 129), c("nC8"))]); vts(G, c("li" + p), li, 512.0, O.add)
+    li = c("pd" + p, 0, 8); group(G, li, [(c(SP, 1, 129), c("C8")), (c(RT, 0, 128), c("C8")), (c(RT, 1, 129), c("nC8"))]); vts(G, c("li" + p), li, 512.0, O.add)
     Q2 = c(pk, 128, 256); mm(G, Q2, pc("one", 0, 2), pc("cq", 0, 2, 128, 256), True, False)
     atom(G, Q2, p, a, t, "I2050", False, False); atom(G, Q2, p, a + 1, t, "I592", False, True); atom(G, slot(p, a + 1), p, a + 1, t, "Ib", True, True)
     act(G, path, sp)
 
 
-def slot(p, i): return c("po2" + p, 128 * i, 128 * i + 128) if i < 4 else (c("pw" + p, 384, 512) if i == 4 else c("pk" + p, 288, 416))
-
-
 def front(G, p, a, t):
     n = c("n" + p); q1, li = c("Q1" + p), c("li" + p)
     vgop(G, c("t1" + p), c("NB"), li, q1, O.mult); gat(G, n, c("NB"), li)
-    vtt(G, c("t2" + p), c("t1" + p), c("pk" + p, 128, 256), O.add); vts(G, c("t3" + p), c("t2" + p), 4, O.arith_shift_right, 4095, O.bitwise_and); vcp(G, c("hu" + p), c("t3" + p)); act(G, c("wr" + p), n, F.Relu)
+    angles(G, p, c("pk" + p, 128, 256)); vcp(G, c("hu" + p), c("t3" + p)); act(G, c("wr" + p), n, F.Relu)
     for i in range(a, -1, -1): vtt(G, c("mk" + p, 128 * i, 128 * i + 128), n, slot(p, i), O.is_equal)
     last = records(G, p)
     if a < ST - 1: act(G, q1, slot(p, a), F.Identity, 2050.0, 4.0)
-    scores(G, p, a, t, "x" + p, "m" + p, list(range(16)), NM_)
+    scores(G, p, a, t, "x" + p, "m" + p, list(range(16)))
     return last
 
 
 def walk(G, t):
     qs = {"A": "qa", "B": "qr%d" % t}
-    for r in range(4): mm(G, c("po1A", r, 512, 4), c("Ib"), c(qs["A" if r < 2 else "B"]))
-    for a, b in zip(CHUNKS, CHUNKS[1:]):
-        (vgat if b == 128 else gat)(G, c("xA", 16 * a, 16 * b), c("E"), c("hu0%d" % t, a, b)); maxima(G, "xA", "mA", "po1A", a, b)
+    for r in range(4): mm(G, c("pdA", r, 512, 4), c("Ib"), c(qs["A" if r < 2 else "B"]))
+    for a, b in zip(CHUNKS, CHUNKS[1:]): (vgat if b == 128 else gat)(G, c("xA", 16 * a, 16 * b), c("E"), c("hu0%d" % t, a, b)); maxima(G, "xA", "mA", "pdA", a, b)
     for p in "BA":
         atom(G, slot(p, 0), p, 0, t, "Ib", True, True); act(G, c("Q1" + p), c("O%s%d" % (p, t)), F.Identity, 2050.0, 4.0)
-        for r in range(4):
-            mm(G, c("pw" + p, r, 4 * NM_, 4), c("Ib"), c(qs[p], 0, NM_))
-            if p == "B" or t == 0: sel(G, c("W4" + p, r, 128, 4), c(qs[p], NM_, 128), [[0, 128 - NM_]], O.is_ge, 0, 0, 0)
+        for r in range(4): mm(G, c("pw" + p, r, 4 * NA, 4), c("Ib"), c(qs[p], 0, NA))
+        if p == "B" or t == 0: gat(G, c("W4" + p), c(qs[p]), c("lW4"))
     mm(G, c("pkA", 272, 280), c("OA%d" % t), c("Pick")); act(G, c("CH%d" % t, 48, 56), c("pkA", 272, 280))
-    scores(G, "B", 0, t, "xA", "mA", list(range(8, 16)), 128); scores(G, "A", 0, t, "xA", "mA", list(range(8)), 128)
+    scores(G, "B", 0, t, "xA", "mA", list(range(8, 16))); scores(G, "A", 0, t, "xA", "mA", list(range(8)))
     for a in range(1, ST):
         for p in "BA": choose(G, p, a - 1, t); last = front(G, p, a, t)
     for p in "BA": choose(G, p, ST - 1, t)
@@ -425,124 +420,117 @@ def walk(G, t):
 
 
 def rings(G, t):
-    CH = "CH%d" % t; ct = pc("CT", 0, 104); col = lambda k: c("col", k, k + 1)
+    CH = "CH%d" % t; b6 = c("B6%d" % t); ct = pc("CT", 0, 104); col = lambda k: c("col", k, k + 1)
     if t == 0:
-        mm(G, c("po1B", 0, 11), pc("Dmf", 0, 16), pc("R1", 0, 16, 0, 11), True, False); mm(G, c("po1B", 0, 2), pc("Dmf", 0, 16), pc("R2", 0, 16, 0, 2), False, True)
-        vcp(G, c("col", 0, 11), c("po1B", 0, 11))
-    mm(G, pc("po2B", 0, 96, 384, 512), c(CH, 0, 96), c("Ib")); vcp(G, pc("CT", 0, 96), pc("po2B", 0, 96, 384, 512))
-    mm(G, c("pkB", 0, 288), pc("CT", 0, 96), pc("DC", 0, 96), True, False)
-    for j in range(6): mm(G, c("pkB", 30 + j, 288, 36), c("Ib"), c(CH, 96, 104), False, j == 5)
-    vts(G, c("EQ"), c("pkB", 0, 288), 0.0, O.is_equal, 8200.0, O.mult); vscan(G, c("FJ"), c("DJ"), c("EQ"), O.add, O.max)
-    mm(G, pc("po2B", 96, 104, 384, 512), c(CH, 96, 104), c("Ib")); vcp(G, pc("CT", 96, 104), pc("po2B", 96, 104, 384, 512))
-    end = c("FJ", 35, 288, 36); vts(G, c("SPJ", 6, 128, 16), end, -2.5, O.add); vtt(G, c("SPJ", 0, 128, 16), end, c("SPJ", 6, 128, 16), O.subtract)
-    vscan(G, c("RRJ"), c("S06"), c("SPJ"), O.mult, O.add); Z = c("pkA", 0, 128); mm(G, Z, c("RRJ"), c("Ib"))
-    V1, V2, NN = [c("po1A", 128 * k, 128 * k + 128) for k in range(3)]; NP = c("po1B", 0, 128); Q1, Q2 = c("po2A", 0, 128), c("po2A", 128, 256); k104 = lambda nm: pc(nm, 0, 104)
+        mm(G, c("pdB", 0, 11), pc("Dmf", 0, 16), pc("R1", 0, 16, 0, 11), True, False); mm(G, c("pdB", 0, 2), pc("Dmf", 0, 16), pc("R2", 0, 16, 0, 2), False, True)
+        vcp(G, c("col", 0, 11), c("pdB", 0, 11))
+    mm(G, pc("psB", 0, 96, 384, 512), c(CH, 0, 96), c("Ib")); vcp(G, pc("CT", 0, 96), pc("psB", 0, 96, 384, 512))
+    mm(G, c("pkB", 0, 288), pc("CT", 0, 96), pc("DC", 0, 96)); vts(G, c("EQ"), c("pkB", 0, 288), 0.0, O.is_equal)
+    for i in range(1, 6): vtt(G, c("EQ", 6 * i - 1, 288, 36), c(CH, 48 + 8 * i, 56 + 8 * i), b6, O.is_equal)
+    for j in range(6): vtt(G, c("EQ", 30 + j, 288, 36), c(CH, 96, 104), c(CH, 40 - 8 * j, 48 - 8 * j) if j < 5 else b6, O.is_equal)
+    vscan(G, c("FJ"), c("DJ"), c("EQ"), O.add, O.max)
+    mm(G, pc("psB", 0, 8, 384, 512), b6, c("Ib")); vcp(G, pc("CT", 0, 8), pc("psB", 0, 8, 384, 512))
+    mm(G, pc("psB", 96, 104, 384, 512), c(CH, 96, 104), c("Ib")); vcp(G, pc("CT", 96, 104), pc("psB", 96, 104, 384, 512))
+    end = c("FJ", 35, 288, 36); vts(G, c("SPJ", 0, 128, 16), end, -1.0, O.mult, -5.5 / 1024, O.add); vcp(G, c("SPY", 0, 128, 16), end)
+    vscan(G, c("RRJ"), c("S0n"), c("SPJ"), O.mult, O.add); vscan(G, c("RRY"), c("S06"), c("SPY"), O.mult, O.add)
+    Z = c("pkA", 0, 128); group(G, Z, [(c("RRJ"), c("I1k")), (c("RRY"), c("I1k"))])
+    V1, V2, NN = [c("pdA", 128 * k, 128 * k + 128) for k in range(3)]; NP = c("pdB", 0, 128); Q1, Q2 = c("psA", 0, 128), c("psA", 128, 256); k104 = lambda nm: pc(nm, 0, 104)
     group(G, V1, [(k104("CV1a"), ct), (k104("CV1b"), ct)]); mm(G, V2, k104("CV2"), ct); mm(G, NP, k104("CN"), ct, True, False)
-    mm(G, c("po2A", 0, 256), pc("one", 0, 2), pc("cq", 0, 2), True, False); mm(G, Q1, k104("CQ1"), ct, False, False); mm(G, Q2, k104("CQ2"), ct, False, False)
+    mm(G, c("psA", 0, 256), pc("one", 0, 2), pc("cq", 0, 2), True, False); mm(G, Q1, k104("CQ1"), ct, False, False); mm(G, Q2, k104("CQ2"), ct, False, False)
     vts(G, c("OH"), Z, col(0), O.is_equal); vtt(G, c("Y1"), c("OH"), V1, O.mult); vtt(G, c("Y2"), c("OH"), V2, O.mult)
     vts(G, c("dead"), Z, col(2), O.mult, col(1), O.is_ge)
     mm(G, NP, c("SA"), c("Y1"), False, True); mm(G, Q1, c("SB4"), c("Y1"), False, False); mm(G, Q2, c("SB2050"), c("Y1"), False, False); mm(G, Q2, c("SA592"), c("Y2"), False, True)
     mm(G, NN, c("p4I"), c("dead")); act(G, c("Zs"), Z, F.Identity, col(3))
-    vcp(G, c("NS"), NP); angles(G, "A", c("NS"), Q1, Q2); vtt(G, c("HF"), c("t3A"), NN, O.max); vcp(G, c("huA"), c("HF"))
-    vts(G, c("hiB"), c("HF"), 1.0 / 64, O.mult, 129.0 - 63.0 / 128, O.add)
-    LO = c("po2B", 0, 96); group(G, LO, [(c("HF"), c("Cmpf")), (c("hiB"), c("Cmp64"))])
-    for d in range(2): vts(G, c("LOT", 96 * d, 96 * d + 96), LO, 8256.0 - d, O.add)
+    vcp(G, c("NR0"), NP); vtt(G, c("t1A"), c("NR0"), Q1, O.mult); angles(G, "A", Q2); vtt(G, c("HF"), c("t3A"), NN, O.max); vcp(G, c("huA"), c("HF"))
+    for nm, d, x in (("h5B", 32, 1025.0), ("h8B", 256, 129.0), ("h9B", 512, 129.0)):
+        vts(G, c(nm), c("HF"), 1.0 / d, O.mult, x - (d - 1.0) / (2 * d), O.add)
+    LO = c("psB", 0, 96); group(G, LO, [(c("HF"), c("Cmpf")), (c("h5B"), c("Cm5")), (c("h8B"), c("Cm8")), (c("h9B"), c("Cm9"))])
+    for d in range(2): vts(G, c("LOT", 96 * d, 96 * d + 96), LO, 36928.0 - d, O.add)
     vts(G, c("LOT", 192, 384), c("LOT", 0, 192), -2.0, O.add)
-    for a, b in zip(RCHUNKS, RCHUNKS[1:]): gat(G, c("xA", 16 * a, 16 * b), c("E"), c("huA", a, b))
-    part = lambda nm, k: c(nm, 288 * k, 288 * k + 288); cnt = (c("pwB", 0, 288), c("po2B", 96, 384))
-    vts(G, c("hqB"), c("HF"), 1.0 / 256, O.mult, 129.0 - 255.0 / 512, O.add)
+    for a, b in zip(RCHUNKS, RCHUNKS[1:]): (gat if a else vgat)(G, c("xA", 16 * a, 16 * b), c("E"), c("huA", a, b))
+    part = lambda nm, k: c(nm, 192 * k, 192 * k + 192); cnt = (c("pwB", 0, 192), c("psB", 96, 288))
     for k, bank in enumerate(("pwA", "pkB")):
-        group(G, c(bank, 0, 288), [(c("dead"), part("DH6", k)), (c("hiB"), part("Cmp6", k)), (c("hqB"), part("Cmq6", k))]); act(G, part("HI0", k), c(bank, 0, 288))
+        group(G, c(bank, 0, 192), [(c("dead"), part("DH", k)), (c("h5B"), part("C5", k)), (c("h8B"), part("C8x", k)), (c("h9B"), part("C9", k))]); act(G, part("HI0", k), c(bank, 0, 192))
     for u in range(0, 64, 4): vts(G, c("OHL", 96 * u, 96 * u + 384), c("LOT"), float(u), O.is_equal)
-    for a, b in zip(RCHUNKS, RCHUNKS[1:]): group(G, c("po1B", 128 + a, 128 + b), [(c("Ib"), c("xA", 16 * a + r, 16 * b, 16)) for r in range(1, 13)])
+    for a, b in zip(RCHUNKS, RCHUNKS[1:]): group(G, c("pdB", 128 + a, 128 + b), [(c("Ib"), c("xA", 16 * a + r, 16 * b, 16)) for r in range(1, 13)])
     for k in range(2): mm(G, cnt[k], c("dead"), part("DC2", k), True, False)
-    vts(G, c("TH"), c("po1B", 128, 256), c("thf"), O.is_ge)
+    vts(G, c("TH"), c("pdB", 128, 256), c("thf"), O.is_ge)
     for k in range(2): mm(G, cnt[k], c("TH"), part("BlkC", k), False, True); vtt(G, part("HIT", k), part("HI0", k), cnt[k], O.min)
+
+
+def ring_atoms(G, t):
+    ct = pc("CT", 0, 104); col = lambda k: c("col", k, k + 1); PL, PI, Y = [c("pkA", a, a + 128) for a in (128, 256, 384)]
+    mm(G, PI, c("PI"), c("Zs")); act(G, c("r1"), PI, F.Relu, col(9)); act(G, c("r2"), PI, F.Relu, col(10), -1.0)
+    group(G, PL, [(c("PZ"), c("Zs")), (c("I16"), c("r1"))])
+    for l in range(5): act(G, c("ZL", 128 * l, 128 * l + 128), PL, F.Abs, col(4 + l))
+    group(G, c("pdA", 0, 128), [(pc("AR", 0, 104), ct), (c("m4I"), c("r2")), (c("PD"), c("dead"))])
+    for l in range(5):
+        o = c("psA", 128 * l, 128 * l + 128) if l < 4 else c("pdA", 128, 256)
+        group(G, o, [(pc("BRL", 0, 104, 128 * l, 128 * l + 128), ct), (c("m4I"), c("ZL", 128 * l, 128 * l + 128))])
+    act(G, c("PB", 0, 256), c("pdA", 0, 256), F.Relu, 513.0); act(G, c("PB", 256, 768), c("psA"), F.Relu, 513.0)
+    group(G, Y, [(c("Ib"), c("PB", 128 * k, 128 * k + 128)) for k in range(6)])
+    y = c("YR", 128 * t, 128 * t + 128); act(G, y, Y, F.Identity, -1.0)
+    dma(G, lambda g, T: g.sync.dma_start(T.yr[:, 128 * t:128 * t + 128], ap(T, y)), [y], [], 2.0)
 
 
 def lessen(G, t, after):
     for k in range(8):
-        i = act(G, c("L16", 512 * k, 512 * k + 512), c("E", 512 * k, 512 * k + 512), F.Identity, 1024.375, 0.75); G["ops"][i]["deps"].setdefault(after, False)
+        behind(G, act(G, c("L16", 512 * k, 512 * k + 512), c("E", 512 * k, 512 * k + 512), F.Identity, *((1024.375, 0.75) if k < KV else (1023.625, 0.25))), after)
     for k, bank in enumerate(("pwA", "pkB")):
-        hit = c("HIT", 288 * k, 288 * k + 288); th = "THH%d" % k; cn = "CN%d" % k
-        for i in range(11):
-            o = c(th, 288 * i, 288 * i + 288)
-            if i < 3: act(G, o, hit, F.Sign, 1.5 - 6 * i)
-            else: vts(G, o, hit, float(6 * i - 2), O.is_ge)
-        was = len(G["ops"])
+        hit = c("HIT", 192 * k, 192 * k + 192); th = "THH%d" % k; half = lambda nm: pc(nm, 64 * k, 64 * k + 64, 0, 256)
+        for i in range(16):
+            o = c(th, 192 * i, 192 * i + 192)
+            if i < NS: act(G, c("AB%d" % (i % 2)), hit, F.Abs, -4.0 * i); act(G, o, c("AB%d" % (i % 2)), F.Relu, 1.0, -1.0)
+            else: vts(G, o, hit, 4.0 * i, O.is_equal)
         for gl in range(4):
-            group(G, pc(bank, 0, 64, gl, 260, 4), [(c("OHL", 48 * k + 12 * gl + s, 6144, 96), c(th, 48 + 12 * gl + s, 3168, 48)) for s in range(12)])
-        if k: G["ops"][was]["deps"].setdefault(done, False)
-        done = len(G["ops"]) - 1
-        act(G, pc(cn, 0, 64, 0, 260), pc(bank, 0, 64, 0, 260))
-        for b in range(4):
-            a = 4 * (16 * b + (1 if b else 0))
-            group(G, pc("pkA", 64 * k, 64 * k + 64, 64 * b, 64 * b + 64), [(pc(cn, 0, 64, a, a + 64), pc("Ib", 0, 64, 0, 64)), (pc(cn, 0, 64, a + 4, a + 68), pc("nI", 0, 64, 0, 64))])
-    vts(G, c("NM"), c("pkA", 0, 256), 0.0, O.is_equal, 4.0, O.subtract)
-    for k in range(8):
-        bank = ("po1A", "po2A", "po2B", "po1B")[k % 4]; e = c("E", 512 * k, 512 * k + 512); o = c(bank, 0, 512)
+            ms = group(G, pc(bank, 64 * k, 64 * k + 64, gl, 256, 4), [(c("OHL", 48 * k + 12 * gl + s, 6144, 96), c(th, 12 * gl + s, 3072, 48)) for s in range(12)])
+            if k and not gl: behind(G, ms[0], done)
+        done = ms[-1]
+        vts(G, half("NR"), half(bank), 0.0, O.is_equal, 4.0, O.subtract); vtr(G, half("NM"), half("NR"))
+    for k in (0, 6, 7, 1, 2, 3, 4, 5):
+        bank = ("pdA", "psA", "psB", "pdB")[k % 4] if k < KV else ("pkA", "pwA")[k % 2]; e = c("E", 512 * k, 512 * k + 512); o = c(bank, 0, 512)
         mm(G, o, c("Ib"), c("L16", 512 * k, 512 * k + 512), True, False)
         for h in range(2): mm(G, c(bank, 256 * h, 256 * h + 256), c("SelT", 256 * k + 128 * h, 256 * k + 128 * h + 128), c("NM"), False, h == 1)
-        if k == 1: G["spread"] = len(G["ops"]) - 1
-        vtt(G, e, e, o, O.min)
-        if t == RO - 1 and k % 2:
-            a = 512 * (k - 1); dma(G, lambda g, T, a=a: g.sync.dma_start(T.ye[:, a:a + 1024], T.E[:, a:a + 1024]), [c("E", a, a + 1024)], [], 2.5)
-
-
-def ring_atoms(G, t):
-    ct = pc("CT", 0, 104); col = lambda k: c("col", k, k + 1); PL, PI = c("pwB", 0, 128), c("pwB", 128, 256)
-    mm(G, PI, c("PI"), c("Zs")); act(G, c("r1"), PI, F.Relu, col(9)); act(G, c("r2"), PI, F.Relu, col(10), -1.0)
-    group(G, PL, [(c("PZ"), c("Zs")), (c("I16"), c("r1"))])
-    for l in range(5): act(G, c("ZL", 128 * l, 128 * l + 128), PL, F.Abs, col(4 + l))
-    group(G, c("pwB", 256, 384), [(pc("AR", 0, 104), ct), (c("m4I"), c("r2")), (c("PD"), c("dead"))])
-    for l in range(5):
-        o = c("pwA", 128 * l, 128 * l + 128) if l < 4 else c("pwB", 384, 512)
-        group(G, o, [(pc("BRL", 0, 104, 128 * l, 128 * l + 128), ct), (c("m4I"), c("ZL", 128 * l, 128 * l + 128))]); G["ops"][-2]["deps"].setdefault(G["spread"], False)
-    act(G, c("PB", 0, 256), c("pwB", 256, 512), F.Relu, 513.0); act(G, c("PB", 256, 768), c("pwA"), F.Relu, 513.0)
-    group(G, c("pkB", 0, 128), [(c("Ib"), c("PB", 128 * k, 128 * k + 128)) for k in range(6)])
-    y = c("YR", 128 * t, 128 * t + 128); act(G, y, c("pkB", 0, 128), F.Identity, -1.0)
-    dma(G, lambda g, T: g.sync.dma_start(T.yr[:, 128 * t:128 * t + 128], ap(T, y)), [y], [], 2.0)
+        if k < KV: vtt(G, e, e, o, O.min)
+        else:
+            d = c("DD", 512 * (k % 2), 512 * (k % 2) + 512); act(G, d, o, F.Relu, -2048.0); o = c(("pwB", "pkB")[k % 2]); group(G, o, [(c("Ib"), e), (c("nI"), d)]); act(G, e, o)
+        if t == RO - 1 and (k % 2 or k == KV - 2):
+            a, b = 512 * (k if k in (KV - 2, KV - 1) else k - 1), 512 * k + 512
+            dma(G, lambda g, T, a=a, b=b: g.sync.dma_start(T.ye[:, a:b], T.E[:, a:b]), [c("E", a, b)], [], 1.5 + (b - a) / 1024)
 
 
 def build(rank, core, topo):
-    G = {"ops": [], "acc": {}, "nd": [0], "late": [0.0]}; peers = [(rank + 1 + t) % N for t in range(RO)]; asks = [(rank - 1 - t) % N for t in range(RO)]; ne = 8
+    G = {"ops": [], "acc": {}, "nd": [0]}; peers = [(rank + 1 + t) % N for t in range(RO)]; asks = [(rank - 1 - t) % N for t in range(RO)]; ne = 8
 
-    def eng(T, dst):
-        m = 0
-        for e in topo.engines(core, T.cores[dst])[:ne]: m |= 1 << e
-        return m
-
-    def did(T, dst):
-        a = topo.addr(T.cores[dst]); return DstId(rid=a[0], pnc=a[1])
-
-    def send3(src, dsts, sem):
-        def fn(g, T):
-            return g.remote_dma_fused([RemoteDMATransfer(dst_ids=[did(T, s) for s in peers], dma_engine_mask=eng(T, peers[0]), remote_sem=T.sem[sem],
-                                                         srcs=[T[src][:]], dsts=[T[d][:] for d in dsts], alu_op=0)], local_sem=T.sem.loc)
+    def send(src, dst, to):
+        def fn(g, T, sem):
+            a = topo.addr(T.cores[to]); m = 0
+            for e in topo.engines(core, T.cores[to])[:ne]: m |= 1 << e
+            return g.remote_dma(ap(T, dst), ap(T, src), T.sem[sem], T.sem.loc, a[1], a[0], m)
         return fn
-    dma(G, lambda g, T: g.sync.dma_start(T.sti[:], T.st[:]), [], [c("sti")], 2.0)
-    dma(G, lambda g, T: g.sync.dma_start(T.qa[:], T.q[:]), [], [c("qa")], 2.0)
-    dma(G, lambda g, T: g.sync.dma_start(T.nbi[:], T.nb[:]), [], [c("nbi")], 3.5)
-    dma(G, lambda g, T: g.sync.dma_start(T.E[:, 0:4096], T.ang[:]), [], [c("E", 0, 4096)], 6.0)
+
+    def exchange(sem, moves, dur):
+        sent = [add(G, "G", lambda g, T, fn=send(*m): fn(g, T, sem), [m[0]], [], 1.0, sem=("loc", 0)) for m in moves]
+        i = add(G, "N", None, [], [m[1] for m in moves], dur, sem=(sem, ne * len(moves)))
+        for s in sent: behind(G, i, s)
+    dma(G, lambda g, T: g.sync.dma_start(T.sti[:], T.st[:]), [], [c("sti")], 1.5)
+    dma(G, lambda g, T: g.sync.dma_start(T.qa[:], T.q[:]), [], [c("qa")], 1.6)
+    dma(G, lambda g, T: g.sync.dma_start(T.nbi[:], T.nb[:]), [], [c("nbi")], 2.5)
+    dma(G, lambda g, T: g.sync.dma_start(T.E[:, 0:4096], T.ang[:]), [], [c("E", 0, 4096)], 4.5)
     dma(G, lambda g, T: g.sync.dma_start(T.thi[:], T.th[:]), [], [c("thi")], 2.0)
     vcp(G, c("stu"), c("sti"))
-    s1 = add(G, "G", send3("stu", ["sr0", "sr1", "sr2"], "as0"), [c("stu")], [], 0.5, sem=("loc", 0))
-    s2 = add(G, "G", send3("qa", ["qr0", "qr1", "qr2"], "aq"), [c("qa")], [], 0.5, sem=("loc", 0))
-    for s, nm, sem in ((s1, "sr", "as0"), (s2, "qr", "aq")):
-        i = add(G, "N", None, [], [c(nm + "%d" % t) for t in range(RO)], 3.0, sem=(sem, 3 * ne)); G["ops"][i]["deps"][s] = False
+    for k, ts in enumerate(([0], [1, 2])):
+        exchange("as%d" % k, [(c("stu", 8 * t, 8 * t + 8), c("sr%d" % t), peers[t]) for t in ts], 6.0 if k else 1.2)
+        exchange("aq%d" % k, [(c("qa"), c("qr%d" % t), peers[t]) for t in ts], 6.0 if k else 1.2)
     walk_constants(G)
     vts(G, c("NB"), c("nbi"), -512.0, O.add); vcp(G, c("thf"), c("thi"))
     first(G, 0, gat); ring_constants(G)
     for t in range(RO):
         last = walk(G, t)
-
-        def back(g, T, t=t):
-            a = topo.addr(T.cores[asks[t]])
-            return g.remote_dma(T["CH%d" % t][:, 0:48], T["BL%d" % t][:], T.sem["ar%d" % t], T.sem.loc, a[1], a[0], eng(T, asks[t]))
-        s = add(G, "G", back, [c("BL%d" % t)], [], 0.5, sem=("loc", 0))
-        i = add(G, "N", None, [], [c("CH%d" % t, 0, 48)], 2.0, sem=("ar%d" % t, ne)); G["ops"][i]["deps"][s] = False
+        exchange("ar%d" % t, [(c("BL%d" % t, 8, 48), c("CH%d" % t, 8, 48), asks[t])], 4.5)
+        exchange("al%d" % t, [(c("BL%d" % t, 0, 8), c("B6%d" % t), asks[t])], 2.5)
         if t < RO - 1: first(G, t + 1, vgat)
-        rings(G, t); lessen(G, t, last); ring_atoms(G, t)
+        rings(G, t); ring_atoms(G, t); lessen(G, t, last)
     return G, ne
 
 
@@ -550,4 +538,4 @@ def rank_program(g, core, T, topo):
     rank = T.rank_of(core)
     if rank is None: return
     G, ne = build(rank, core, topo); emit(G, schedule(G), g, T)
-    g.wait_ge(T.sem.loc, ne * (2 + RO))
+    g.wait_ge(T.sem.loc, ne * 4 * RO)

@@ -2,12 +2,14 @@ from concourse.bass import DstId, RemoteDMATransfer
 from concourse.mybir import AluOpType as O, ActivationFunctionType as F
 
 N, RO, ST = 4, 3, 6
-CHUNKS = (0, 48, 88, 128)
+CHUNKS = {"B": (0, 48, 88, 128), "A": (0, 32, 64)}
 MCHUNKS = (0, 32, 64, 80, 96)
 NV, NA = 64, 96
 RCHUNKS = (0, 24, 80, 128)
+TURN = 2688
 NS, KV = 2, 6
-SCRATCH, SHAPE, WIDE, PLACE = {}, {}, {}, {}
+BANKS = ("pwB", "pkB", "pdB", "psB", "pdA", "psA", "pkA", "pwA"); EIGHTHS = (0, 6, 1, 7, 2, 3, 4, 5)
+SCRATCH, SHAPE, WIDE, PLACE, ORDER = {}, {}, {}, {}, {}
 SEMAPHORES = ["sv", "ss", "sp", "sg", "as0", "as1", "aq0", "aq1", "ar0", "ar1", "ar2", "al0", "al1", "al2", "loc"] + ["d%d" % i for i in range(20)]
 QSEM = {"V": "sv", "S": "ss", "P": "sp", "G": "sg"}
 POOL = {"float32": "poolf", "bfloat16": "poolb", "float16": "poolh", "int32": "pooli", "uint16": "poolu"}
@@ -21,16 +23,17 @@ def many(dtype, cols, names):
         pool[1][1] += -(-cols // 32) * 32
 
 
-many("int32", 1024, "nbi"); many("float32", 1024, "NB IDT"); many("bfloat16", 4112, "E"); many("float16", 4096, "L16")
+many("int32", 1024, "nbi"); many("float32", 1024, "NB IDT"); many("bfloat16", 4112, "E"); many("int32", 512 * KV, "L"); many("float16", 4096 - 512 * KV, "D16")
 many("bfloat16", 128, "qa qr0 qr1 qr2"); many("int32", 24, "sti"); many("uint16", 24, "stu"); many("uint16", 8, "sr0 sr1 sr2"); many("int32", 1, "thi"); many("float32", 1, "thf")
-many("uint16", 8, "lW4"); many("int32", 4, "pci"); many("float32", 12, "pcf"); many("float32", 136, "CI S1 GC TK"); many("float32", 128, "CR"); many("float32", 16, "G16"); many("float32", 272, "SEG")
-many("bfloat16", 128, "Ib I592 dA dB dA4 dB4 Dm S01 TR nI one W4A W4B"); many("float16", 128, "I2050 dA26 dB26"); many("float16", 256, "cq")
-many("bfloat16", 272, "Perm BIGP WN"); many("bfloat16", 136, "nPerm"); many("bfloat16", 816, "cr"); many("bfloat16", 16, "BX BM"); many("bfloat16", 8, "C8 nC8 Pick")
-many("bfloat16", 288, "Zb DC"); many("bfloat16", 384, "BlkC DC2 C5 C8x C9 DH"); many("float16", 288, "Zh DJ"); many("float32", 128, "Zf Dmf"); many("float32", 16, "R1 R2 col")
-many("bfloat16", 128, "CN CQ1 CV1a CV1b CV2 SA SA592 SB4 S06 S0n PZ PI PD AR I16 m4I p4I I1k"); many("float16", 128, "CQ2 SB2050"); many("bfloat16", 640, "BRL")
+many("uint16", 8, "lW4"); many("int32", 4, "pci"); many("float32", 12, "pcf"); many("float32", 136, "CI S1 GC"); many("float32", 128, "CR"); many("float32", 16, "G16"); many("float32", 272, "SEG")
+many("bfloat16", 128, "Sdn Sup Ib I592 dA dB dA4 dB4 S01 TR nI one W4A W4B"); many("float16", 128, "I2050 dA26 dB26"); many("float16", 256, "cq")
+many("bfloat16", 272, "Perm BIGP WN"); many("bfloat16", 136, "nPerm"); many("bfloat16", 544, "cr"); many("float16", 128, "qwA qwB"); many("bfloat16", 16, "BX BM"); many("bfloat16", 8, "C8 nC8 Pick")
+many("bfloat16", 288, "Zb DC PU PQ1"); many("bfloat16", 384, "BlkC DC2 C5 C8x C9 DH"); many("float16", 288, "Zh DJ PQ2"); many("float32", 8, "col"); many("float16", 576, "cp")
+many("bfloat16", 128, "CN CQ1 one1 MI MJ PZ PI PD PN AR I4 I16 m4I p4I"); many("float16", 128, "CQ2"); many("bfloat16", 640, "BRL")
 many("float32", 96, "Cmpf"); many("bfloat16", 96, "Cm5 Cm8 Cm9"); many("bfloat16", 2048, "SelT")
-many("float16", 128, "CT Y1 Y2 NR0 tnA tnB h5B SPY RRY"); many("float16", 288, "EQ"); many("float32", 288, "FJ"); many("bfloat16", 128, "OH dead h8B h9B TH Zs r1 r2 SPJ RRJ"); many("float32", 128, "HF")
-many("bfloat16", 384, "LOT HI0 HIT"); many("bfloat16", 192, "AB0 AB1"); many("bfloat16", 6144, "OHL"); many("bfloat16", 3072, "THH0 THH1")
+many("float16", 128, "CT N0 tnA tnB h5B SPJ RRJ TB HQ"); many("float16", 144, "TA"); many("float16", 288, "FJ"); many("float16", 289, "h4"); many("float16", 416, "UN"); many("bfloat16", 288, "NE NA")
+many("float32", 288, "h1 HS"); many("int32", 288, "h2 h3"); many("bfloat16", 128, "dead h8B h9B TH Zs r1 r2 SPI RRI"); many("float32", 128, "H0 HF Q20")
+many("bfloat16", 384, "LOT HI0 HIT"); many("bfloat16", 384 * NS, "AB"); many("bfloat16", 6144, "OHL"); many("bfloat16", 3072, "THH0 THH1")
 many("bfloat16", 256, "NR NM"); many("bfloat16", 640, "ZL"); many("bfloat16", 1024, "DD"); many("float16", 768, "PB"); many("float32", 384, "YR")
 for _p in "AB":
     for _d, _c, _l in (("float16", 128, "n wr RR1 RR2 RR3 RR4 RR5"), ("float16", 144, "SP RT"), ("float32", 128, "t1 Q1"), ("int32", 128, "t2 t3"), ("uint16", 128, "hu"),
@@ -38,8 +41,8 @@ for _p in "AB":
         many(_d, _c, " ".join(n + _p for n in _l.split()))
     for _n in "kwds": SCRATCH["p" + _n + _p] = ("psum", [128, 512], "float32")
 for _t in range(RO):
-    many("uint16", 128, "hu0%d" % _t); many("bfloat16", 128, "mk0%d" % _t); many("float16", 128, "NC%d wr0%d OA%d OB%d" % (_t, _t, _t, _t))
-    many("float16", 104, "CH%d" % _t); many("float16", 48, "BL%d" % _t); many("float16", 8, "B6%d" % _t)
+    many("uint16", 128, "hu0%d" % _t); many("bfloat16", 128, "mk0%d" % _t); many("float16", 128, "wr0%d OA%d OB%d" % (_t, _t, _t)); many("float16", 384, "NC%d" % _t)
+    many("float16", 96, "CH%d" % _t); many("float16", 48, "BL%d" % _t); many("float16", 8, "B6%d" % _t)
 SHAPE.update({k: s[1] for k, s in SCRATCH.items()})
 PSUM = {k for k, s in SCRATCH.items() if s[0] == "psum"}
 WIDE.update({k: s[2] in ("float32", "int32") for k, s in SCRATCH.items()})
@@ -109,17 +112,17 @@ def cols(*xs): return [x for x in xs if isinstance(x, tuple)]
 
 
 def vtt(G, o, a, b, op):
-    add(G, "V", lambda g, T: g.vector.tensor_tensor(ap(T, o), ap(T, a), ap(T, b), op), [a, b], [o], vcost(o[3], 1 if (a[0] in PSUM or b[0] in PSUM) else 2))
+    return add(G, "V", lambda g, T: g.vector.tensor_tensor(ap(T, o), ap(T, a), ap(T, b), op), [a, b], [o], vcost(o[3], 1 if (a[0] in PSUM or b[0] in PSUM) else 2))
 
 
 def vts(G, o, a, s1, op0, s2=None, op1=None):
     def fn(g, T):
         if op1 is None: return g.vector.tensor_scalar(ap(T, o), ap(T, a), num(T, s1), None, op0)
         return g.vector.tensor_scalar(ap(T, o), ap(T, a), num(T, s1), num(T, s2), op0, op1)
-    add(G, "V", fn, [a] + cols(s1, s2), [o], vcost(o[3], 0.5 if two(o, a) else 1))
+    return add(G, "V", fn, [a] + cols(s1, s2), [o], vcost(o[3], 0.5 if two(o, a) else 1))
 
 
-def vcp(G, o, a): add(G, "V", lambda g, T: g.vector.tensor_copy(ap(T, o), ap(T, a)), [a], [o], vcost(o[3], 0.5 if two(o, a) else 1))
+def vcp(G, o, a): return add(G, "V", lambda g, T: g.vector.tensor_copy(ap(T, o), ap(T, a)), [a], [o], vcost(o[3], 0.5 if two(o, a) else 1))
 
 
 def vscan(G, o, a, b, op0, op1):
@@ -144,8 +147,8 @@ def act(G, o, a, func=F.Copy, bias=0.0, scale=1.0):
     return add(G, "S", lambda g, T: g.scalar.activation(ap(T, o), ap(T, a), func, bias=num(T, bias), scale=scale), [a] + cols(bias), [o], max(64, o[3]) * VC + 0.02)
 
 
-def gat(G, o, w, off):
-    return add(G, "S", lambda g, T: g.scalar.activation(ap(T, o), ap(T, w).indirect(ap(T, off)), F.Copy), [w, off], [o], o[3] * VC * GR + 0.065, gn=o[3])
+def gat(G, o, w, off, bias=0.0):
+    return add(G, "S", lambda g, T: g.scalar.activation(ap(T, o), ap(T, w).indirect(ap(T, off)), F.Identity if bias else F.Copy, bias=bias), [w, off], [o], o[3] * VC * GR + 0.065, gn=o[3])
 
 
 def mm(G, o, l, r, start=True, stop=True, grp=None):
@@ -160,19 +163,23 @@ def iota(G, o, pat, base, cm, small=True):
     def fn(g, T):
         if small: return g.iota(ap(T, o), pat, base, cm, allow_small_or_imprecise_dtypes=True)
         return g.iota(ap(T, o), pat, base, cm)
-    add(G, "G", fn, [], [o], 1.25 * (0.13 + o[3] * 2 * VC))
+    i = add(G, "G", fn, [], [o], 1.25 * (0.13 + o[3] * 2 * VC))
+    if "sent" in G: behind(G, i, G["sent"])
+    G["sent"] = i
 
 
 def sel(G, o, a, pat, op, fill, base, cm=1):
-    add(G, "G", lambda g, T: g.affine_select(ap(T, o), ap(T, a), pat, op, float(fill), base, cm), [a], [o], 1.25 * (0.17 + o[3] * 2 * VC))
+    behind(G, add(G, "G", lambda g, T: g.affine_select(ap(T, o), ap(T, a), pat, op, float(fill), base, cm), [a], [o], 1.25 * (0.17 + o[3] * 2 * VC)), G["sent"])
 
 
 def dma(G, fn, R, W, dur):
     k = "d%d" % G["nd"][0]; G["nd"][0] += 1; add(G, "Y", fn, R, W, dur, sem=(k, 16))
 
 
-PASSES = 3; SAME, CROSS = 0.2, 0.27
-LATER = {"Vm": 2.0, "Vmk": 2.0, "Swr": 2.0}
+PASSES = 3; SAME, CROSS, ISSUE = 0.2, 0.27, 1.5
+LATER = {"Vm": 2.0, "Vmk": 3.0, "Swr": 2.0, "Vx": 0.5}
+PACES = ((1.0, 1.0, 1.5, 0.2, 0.27, 0.7), (1.3, 1.3, 1.2, 0.1, 0.15, 1.5), (1.3, 1.3, 1.9, 0.15, 0.2, 0.7), (1.15, 1.9, 1.3, 0.15, 0.2, 1.0))
+TRIES, REACH, AHEAD = 2000, 6, 600
 
 
 def schedule(G):
@@ -220,8 +227,52 @@ def schedule(G):
         back = place(sorted(range(n), key=lambda i: -at[i] - dur[i]), succ, lambda d, i: lat(i, d))
         at = place(sorted(range(n), key=lambda i: -back[i] - dur[i]), pred, lat); end = max(at[i] + dur[i] for i in range(n))
         if end < best[0]: best = (end, at)
-    for i in range(n): ops[i]["t"] = (best[1][i], best[1][i] + dur[i])
-    return sorted(range(n), key=lambda i: (best[1][i], i))
+    return polish(ops, sorted(range(n), key=lambda i: (best[1][i], i)))
+
+
+def polish(ops, order):
+    n = len(ops); q = [o["q"] for o in ops]; deps = [set(o["deps"]) for o in ops]; S = range(len(PACES))
+    dur = [[(o["dur"] + o["gn"] * VC * (gr - GR)) * (far if o["sem"] else (fp if o["q"] == "P" else f)) for o in ops] for f, fp, gr, a, b, far in PACES]
+    wait = [[[(j, (a if q[j] == q[i] else b) if w else 0.0) for j, w in o["deps"].items() if w or q[i] == "N"] for i, o in enumerate(ops)] for f, fp, gr, a, b, far in PACES]
+    end, free, why = [[[x] * n for s in S] for x in (0.0, 0.0, None)]
+
+    def run(s, lo, hi, E, Fr, W):
+        last = {}
+        for x in order[max(0, lo - 900):lo]: last[q[x]] = x
+        for i in order[lo:hi]:
+            y = last.get(q[i]) if q[i] != "N" else None; t = 0.0 if y is None else Fr[y]
+            for j, w in wait[s][i]:
+                if E[j] + w > t: t = E[j] + w; y = j
+            E[i] = t + dur[s][i]; Fr[i] = t + 0.1 if q[i] == "Y" else E[i]; W[i] = y; last[q[i]] = i
+        return far(hi, E)
+
+    def far(hi, E):
+        last = {q[x]: E[x] for x in order[max(0, hi - 60):hi]}
+        return max(last.values()) + sum(last.get(k, 0.0) for k in "VSP") / 12
+    norm = [run(s, 0, n, end[s], free[s], why[s]) for s in S]; tried = set(); left = TRIES; gained = True
+    while gained and left > 0:
+        gained = False; pairs = set(); pos = {x: k for k, x in enumerate(order)}
+        for s in S:
+            j = max(range(n), key=lambda x: end[s][x])
+            while why[s][j] is not None:
+                i = why[s][j]
+                if q[i] == q[j] and q[j] in QSEM and i not in deps[j]: pairs.add((pos[j], i, j))
+                j = i
+        for _, i, j in sorted(pairs):
+            for ahead in (True, False):
+                a, b = pos[i], pos[j]
+                if (i, j, ahead) in tried or a > b or left <= 0: continue
+                tried.add((i, j, ahead)); old = order[a:b + 1]; move = {j if ahead else i}
+                for x in (old[-2::-1] if ahead else old[1:]):
+                    if (any(x in deps[z] for z in move) if ahead else deps[x] & move): move.add(x)
+                if (i in move and j in move) or len(move) > REACH or (ahead and sum(q[x] == q[j] for x in move) > 1): continue
+                hi = min(n, b + AHEAD); was = sum(far(hi, end[s]) / norm[s] for s in S); left -= 1
+                order[a:b + 1] = [x for x in old if (x in move) == ahead] + [x for x in old if (x in move) != ahead]
+                if sum(run(s, a, hi, list(end[s]), list(free[s]), {}) / norm[s] for s in S) < was - 1e-6:
+                    for s in S: run(s, a, n, end[s], free[s], why[s])
+                    pos.update({x: a + k for k, x in enumerate(order[a:b + 1])}); gained = True; break
+                order[a:b + 1] = old
+    return order
 
 
 def emit(G, order, g, T):
@@ -264,84 +315,93 @@ def walk_constants(G):
     for nm, x in (("I592", 592.0), ("I2050", 2050.0), ("nI", -1.0)): vts(G, c(nm), c("Ib"), x, O.mult)
     for h, col in (("A", ha), ("B", hb)):
         for nm, x in (("", 1.0), ("4", 4.0), ("26", 2642.0)): vts(G, c("d" + h + nm), c("Ib"), col, O.mult, x, O.mult)
-    vset(G, pc("one", 0, 2), 1.0)
-    vset(G, pc("cq", 0, 2, 0, 128), 0.0); vset(G, pc("cq", 0, 2, 128, 256), 1.0); vset(G, pc("cq", 0, 1, 0, 128), 2050.0); vset(G, pc("cq", 0, 1, 128, 256), 43008.0)
-    vts(G, c("Dm"), c("CR"), PR, O.is_equal); vts(G, c("S01"), c("CR"), 0.0, O.not_equal); vts(G, c("TR"), c("CR"), PR, O.is_le); vset(G, c("TR", 0, 128, 16), 0.0)
+    vts(G, c("Sdn"), c("CI", 8, 136), P, O.is_equal, hb, O.mult); vts(G, k1, P, 8.0, O.add); vts(G, c("Sup"), c("CI", 0, 128), k1, O.is_equal, ha, O.mult)
+    vset(G, pc("one", 0, 1), 1.0); vset(G, pc("cq", 0, 1, 0, 128), 2050.0); vset(G, pc("cq", 0, 1, 128, 256), 0.0)
+    vts(G, c("S01"), c("CR"), 0.0, O.not_equal); vts(G, c("TR"), c("CR"), PR, O.is_le); vset(G, c("TR", 0, 128, 16), 0.0)
     vts(G, c("C8"), c("G16", 0, 8), PG, O.is_equal); vts(G, c("Pick"), c("C8"), R0, O.mult); vts(G, c("nC8"), c("C8"), -1.0, O.mult)
     vts(G, c("BX"), c("G16"), PG, O.is_equal, -8192.0, O.mult); vts(G, c("BM"), c("BX"), -2.0, O.mult)
     for h in (0, 136):
         vts(G, c("Perm", h, h + 136), c("CI"), SL, O.is_equal); vts(G, c("WN", h, h + 136), c("GC"), PG, O.is_equal, -8192.0, O.mult)
-        vts(G, c("SEG", h, h + 136), c("S1"), -1.0, O.is_equal, 2.0 ** 30, O.mult)
+    vset(G, c("SEG"), -512.0); vset(G, c("SEG", 0, 272, 17), 2.0 ** 30); vset(G, c("SEG", 1, 272, 17), 16720896.0)
     vset(G, c("WN", 0, 272, 17), 0.0); vts(G, c("BIGP"), c("Perm"), 2.0 ** 26, O.mult); vts(G, c("nPerm"), c("Perm", 0, 136), -1.0, O.mult)
-    vts(G, k1, P, 512.0, O.mult); vts(G, k2, P, -1.0, O.add, 2.0 ** 24, O.mult); vts(G, k3, P, -1.0, O.add, -2.0 ** 27, O.mult)
-    vts(G, k4, P, -16899584.0, O.mult, 2.0 ** 24, O.add)
-    r = lambda w: pc(w[0], 0, 2, w[2][1][0], w[2][1][1])
-    vts(G, r(c("cr", 0, 136)), r(c("S1")), r(k1), O.mult, r(k2), O.add)
-    for at, op in ((272, O.is_ge), (544, O.is_le)):
-        vts(G, r(c("TK")), r(c("S1")), 7.5, op, r(k3), O.mult); vtt(G, r(c("cr", at, at + 136)), r(c("cr", 0, 136)), r(c("TK")), O.add)
-    for at in (0, 272, 544): vcp(G, r(c("cr", at + 136, at + 272)), r(c("cr", at, at + 136)))
-    vts(G, pc("cr", 0, 2, 0, 816, 17), r(c("S1", 0, 48)), 0.0, O.mult, r(k4), O.add)
+    for at, op in ((0, O.is_ge), (272, O.is_le)):
+        r = pc("cr", 0, 1, at, at + 136); vts(G, r, pc("S1", 0, 1), 7.5, op, 2.0 ** 27, O.mult); vts(G, r, r, -255.0 * 65536, O.add); vcp(G, pc("cr", 0, 1, at + 136, at + 272), r)
+    vset(G, pc("cr", 0, 1, 0, 544, 17), 0.0)
+    for p_ in "AB": vset(G, c("qw" + p_, NA, 128), 127.5)
     for p_ in "AB": vset(G, c("SP" + p_), 0.0); vset(G, c("RT" + p_, 128, 144), 0.0)
     vset(G, c("E", 4096, 4112), 0.0)
 
 
 def ring_constants(G):
     ne, ge = O.not_equal, O.is_ge
-    vset(G, c("Zb"), 0.0); vset(G, c("Zh"), 0.0); vset(G, c("Zf"), 0.0); vset(G, c("SPJ"), 0.0); vset(G, c("SPY"), 0.0); vcp(G, c("Dmf"), c("Dm"))
+    for nm in ("Zb", "Zh", "TA", "TB", "HQ"): vset(G, c(nm), 0.0)
+    vset(G, c("h4", 0, 1), -2048.0)
     for t in range(RO): vset(G, c("CH%d" % t, 0, 8), 0.0)
-    Z = lambda w: c("Zf" if WIDE[w[0]] else ("Zh" if PLACE.get(w[0], ("",))[0] == "poolh" else "Zb"), 0, w[3])
 
     def put(w, items, fresh=True):
-        for pat, base, x in items: sel(G, w, Z(w) if fresh else w, pat, ne, x, base); fresh = False
+        for pat, base, x in items: sel(G, w, c("Zh" if w[0] in ("PQ2", "CQ2") else "Zb", 0, w[3]) if fresh else w, pat, ne, x, base); fresh = False
+
+    def fill(w, x): sel(G, w, w, [[0, w[3]]], O.is_gt, x, 0, 0)
     diag = lambda d, x: ([[-1, 8], [-8, 16]], -8 * d, x)
+    sides = lambda d, e, x: [([[-1, 8], [1000, 2], [-8, 8]], -8 * d, x), ([[-1, 8], [1000, 2], [-8, 8]], -8 * e - 1064, x)]
     rows = lambda r, x: ([[-16, 8], [0, 16]], -r, x)
-    rcol = [[0, 8], [1, 16]]
-    put(c("DC"), [([[-1, 8], [-8, 6], [0, 6]], -56, 1), ([[-1, 8], [0, 6], [8, 6]], -40, -1)])
-    sel(G, c("DJ"), c("Zh"), [[0, 288]], O.is_gt, 1 / 1024, 0, 0); sel(G, c("DJ"), c("DJ"), [[0, 48], [1, 6]], ne, 3 / 1024, 0, 0); sel(G, c("DJ"), c("DJ"), [[0, 8], [1, 36]], ge, -4, -2, 0)
-    sel(G, c("S06"), c("S01"), rcol, ne, 0, -6, 0); sel(G, c("S0n"), c("S01"), rcol, ne, -1, -6, 0)
-    q = lambda nm, a, b: pc(nm, 0, 16, a, b); one = [[0, 1]]
-    iota(G, q("R1", 0, 2), [[0, 2]], 1128, -8); sel(G, q("R1", 0, 2), q("R1", 0, 2), [[0, 2]], ge, 0, -6); iota(G, q("R1", 2, 3), one, 1, 0)
-    for k, x in ((1, -1000), (2, -1)):
-        for r in (6, 12): sel(G, q("R1", k, k + 1), q("R1", k, k + 1), one, ne, x, -r)
-    sel(G, q("R1", 1, 3), q("R1", 1, 3), [[0, 2]], ge, 0, 12, -1)
-    iota(G, q("R1", 3, 4), one, -1032, 0); sel(G, q("R1", 3, 4), q("R1", 3, 4), one, ge, 8, -6)
-    iota(G, q("R1", 4, 9), [[-1, 5]], 11, -1); iota(G, q("R1", 9, 10), one, 7, -1); iota(G, q("R1", 10, 11), one, -6, 1)
-    iota(G, q("R2", 0, 2), [[0, 2]], -8, 1); sel(G, q("R2", 0, 2), q("R2", 0, 2), [[0, 2]], ge, 0, 5, -1)
-    put(c("CN"), [diag(-1, 1)]); sel(G, c("CV1a"), c("CN"), rcol, ge, 0, -7, 0); sel(G, c("CN"), c("CN"), rcol, ne, 0, -12, 0)
-    put(c("CV1b"), [diag(1, 1)]); sel(G, c("CV1b"), c("CV1b"), [[0, 8], [-1, 16]], ge, 0, 5, 0); put(c("CV2"), [diag(0, 1)])
-    put(c("CQ1"), [diag(1, 4)]); put(c("CQ2"), [diag(0, 592)]); sel(G, c("CQ2"), c("CQ2"), rcol, ne, 0, -12, 0); put(c("CQ2"), [diag(1, 2050)], False)
-    for nm, x, lo, hi in (("SA", 1, 6, 15), ("SB4", 4, 0, 5)):
-        w = c(nm); sel(G, w, Z(w), rcol, ne, x, -12, 0); sel(G, w, w, [[-16, 8], [0, 16]], ge, 0, -lo); sel(G, w, w, [[16, 8], [0, 16]], ge, 0, hi, -1)
-    put(c("Cm8"), [([[-16, 8], [-1, 12]], -1, 32)])
+    up16, dn16 = [[0, 8], [1, 16]], [[0, 8], [-1, 16]]; byi, byj = [[-1, 8], [8, 6], [0, 6]], [[-1, 8], [0, 6], [-8, 6]]
+    put(c("DC"), [(byi, -96, 1), (byj, 0, -1)]); put(c("PU"), [(byi, -88, 1)]); put(c("PQ1"), [(byj, -8, 4)])
+    put(c("PQ2"), [(byj, -8, 2050), (byi, -88, 2050), (byi, -96, 592), ([[-1, 8], [1000, 6], [-8, 6]], 0, 592)])
+    for k in range(2): vset(G, pc("cp", 0, 1, 288 * k, 288 * k + 288), 0.0)
+    for k, a, x in ((0, 35, 4096), (1, 0, -4096), (1, 1, 4096)): fill(pc("cp", 0, 1, 288 * k + a, 288 * k + 288, 36), x)
+    for nm in ("PU", "PQ2"):
+        for a in (0, 35): fill(c(nm, a, 288, 36), 0)
+    sel(G, c("DJ"), c("Zh"), [[0, 288]], O.is_gt, 1 / 64, 0, 0); sel(G, c("DJ"), c("DJ"), [[0, 48], [1, 6]], ne, 3 / 64, 0, 0); fill(c("DJ", 0, 288, 36), 4)
+    put(c("CN"), sides(-1, -3, 1)); put(c("CQ1"), sides(-3, -1, 4)); put(c("CQ2"), sides(-3, -1, 2050) + [diag(-2, 592)])
+    for nm, x in (("CQ1", 4), ("CQ2", 2050)): put(c(nm, 2, 128, 16), [([[-1, 8]], -88, x)], False)
+    sel(G, pc("one1", 0, 1), pc("one", 0, 1), up16, ne, 0, -1, 0)
+    sel(G, c("MI"), c("S01"), up16, ge, 0, -4, 0); sel(G, c("SPI"), c("S01"), up16, ge, 0, -9, 0)
+    sel(G, c("MJ"), c("S01"), up16, ge, 0, -3, 0); sel(G, c("MJ"), c("MJ"), dn16, ge, 0, 7, 0); sel(G, c("SPJ"), c("Zh", 0, 128), dn16, ge, -1, 3, 0); sel(G, c("SPJ"), c("SPJ"), dn16, ge, 0, 7, 0)
+    for nm, r, x in (("MI", 8, -0.125), ("MI", 14, -1), ("MI", 15, 0), ("SPI", 0, 1), ("SPI", 1, 0.5), ("SPI", 8, 129), ("SPI", 14, 0), ("SPJ", 3, -1072)): fill(c(nm, r, 128, 16), x)
+    vts(G, c("col", 5, 6), c("pcf", 1, 2), -1.0, O.add); vts(G, c("col", 6, 7), c("pcf", 1, 2), -1.0, O.mult, 2.0, O.add); vts(G, c("col", 0, 5), c("CI", 0, 5), -1.0, O.mult, c("col", 6, 7), O.add)
+    put(c("Cm8"), [([[-16, 8], [-1, 12]], -2, 32), ([[-16, 8], [1000, 12]], -1, 32)])
     for k in range(2):
-        part = lambda nm: c(nm, 192 * k, 192 * k + 192); w = part("BlkC"); up = [[0, 4], [16, 4], [0, 12]]; dn = [[0, 4], [-16, 4], [0, 12]]; dg = [[0, 4], [-16, 4], [-1, 12]]
-        sel(G, w, Z(w), up, ge, 128, 64 * k - 1, -1); sel(G, w, w, up, ge, 0, 64 * k + 15, -1)
-        put(part("DC2"), [(dn, -64 * k - 6, -8192), (dn, -64 * k - 14, -1088)]); put(part("C9"), [(dg, -64 * k - 1, 1)])
-        w = part("DH"); iota(G, w, [[-1, 4], [0, 48]], -73, 0); sel(G, w, w, dn, O.is_equal, 0, -64 * k - 14); put(w, [(dg, -64 * k - 1, -256)], False)
-    for nm, a, x in (("I1k", "Ib", 1024), ("p4I", "Ib", 4096), ("I16", "Ib", 16), ("m4I", "Ib", -4096), ("SA592", "SA", 592), ("SB2050", "SB4", 512.5),
-                     ("Cmpf", "Cm8", 1 / 32), ("Cm5", "Cm8", -1), ("Cm9", "Cm8", -2), ("C5", "C9", 8), ("C8x", "C9", -64)): act(G, c(nm), c(a), F.Identity, 0.0, float(x))
-    for h in range(16): put(c("SelT", 128 * h, 128 * h + 128), [([[-64, 2], [-1, 4], [0, 16]], -32 * (h % 2) - 4 * (h // 2), 256 if h < 2 * KV else -256)])
-    put(c("PI"), [rows(6, -0.125)]); put(c("PZ"), [rows(6, -0.125), rows(0, -1)]); put(c("PD"), [rows(6, -4096)]); put(c("AR"), [diag(6, 1)])
+        part = lambda nm: c(nm, 192 * k, 192 * k + 192); w = part("BlkC"); up = [[0, 4], [16, 4], [0, 12]]; dn = [[0, 4], [-16, 4], [0, 12]]; dg = [[0, 4], [-16, 4], [-1, 12]]; d0 = [[0, 4], [-16, 4], [1000, 12]]
+        sel(G, w, c("Zb", 0, 192), up, ge, 64, 64 * k - 1, -1); sel(G, w, w, up, ge, 0, 64 * k + 15, -1)
+        put(part("DC2"), [(dn, -64 * k - 14, -8192), (dn, -64 * k - 15, -64)]); put(part("C9"), [(dg, -64 * k - 2, 1), (d0, -64 * k - 1, 1)])
+        w = part("DH"); iota(G, w, [[-1, 4], [0, 48]], -73, 0); sel(G, w, w, dn, O.is_equal, 0, -64 * k - 15); put(w, [(dg, -64 * k - 2, -256), (d0, -64 * k - 2, 0), (d0, -64 * k, -81)], False)
+    for nm, x in (("I4", 4), ("p4I", 4096), ("I16", 16), ("m4I", -4096)): act(G, c(nm), c("Ib"), F.Identity, 0.0, float(x))
+    for h in range(16): put(c("SelT", 128 * h, 128 * h + 128), [([[-64, 2], [-1, 4], [0, 16]], -32 * (h % 2) - 4 * (h // 2), -256 if h < 2 * KV else 1024)])
+    put(c("PI"), [rows(8, 1)]); put(c("PZ"), [rows(8, -1), rows(7, -1)]); put(c("PD"), [rows(14, -4096)]); put(c("AR"), [diag(6, 1)]); put(c("PN"), [rows(14, 64)])
     for l in range(1, 6): put(c("BRL", 128 * l - 128, 128 * l), [([[-1, 8], [0, 16]], -8 * (6 - l), 1)])
+
+    def scaled(after):
+        for nm, a, x in (("Cmpf", "Cm8", 1 / 32), ("Cm5", "Cm8", -1), ("Cm9", "Cm8", -2), ("C5", "C9", 8), ("C8x", "C9", -64)): behind(G, act(G, c(nm), c(a), F.Identity, 0.0, float(x)), after)
+        put(c("Cmpf"), [([[-16, 8], [1000, 12]], -15, 36928 / 4096)], False); behind(G, act(G, c("thf"), c("thi"), F.Identity, 0.5, -1.0), after)
+    return scaled
 
 
 def angles(G, p, Q2):
     vtt(G, c("t2" + p), c("t1" + p), Q2, O.add); vts(G, c("t3" + p), c("t2" + p), 4, O.arith_shift_right, 4095, O.bitwise_and)
 
 
-def first(G, t, gather):
-    sa, sb_ = c("stu", 8 * t, 8 * t + 8), c("sr%d" % t); oa, ob, nc = c("OA%d" % t), c("OB%d" % t), c("NC%d" % t); b = "pwB"
-    gather(G, oa, c("IDT"), sa); gather(G, c("tnA"), c("NB"), sa); gather(G, ob, c("IDT"), sb_); gather(G, c("tnB"), c("NB"), sb_)
-    group(G, c(b, 0, 128), [(c("dA"), c("tnA")), (c("dB"), c("tnB"))])
-    mm(G, c(b, 256, 512), pc("one", 0, 2), pc("cq", 0, 2), True, False)
-    for h, o in (("A", oa), ("B", ob)): mm(G, c(b, 256, 384), c("d%s4" % h), o, False, False); mm(G, c(b, 384, 512), c("d%s26" % h), o, False, h == "B")
-    group(G, c(b, 128, 256), [(c("dA"), oa), (c("dB"), ob)])
-    vcp(G, nc, c(b, 0, 128)); vtt(G, c("t1B"), nc, c(b, 256, 384), O.mult); angles(G, "B", c(b, 384, 512)); vcp(G, c("hu0%d" % t), c("t3B"))
-    vtt(G, c("mk0%d" % t), nc, c(b, 128, 256), O.is_equal); vts(G, c("wr0%d" % t), nc, 0.0, O.max)
+def first(G, t):
+    sa, sb_ = c("stu", 8 * t, 8 * t + 8), c("sr%d" % t); oa, ob = c("OA%d" % t), c("OB%d" % t); b = "pwB"; N2 = "pdB"
+    gat(G, ob, c("IDT"), sb_); G["tn"] = gat(G, c("tnB"), c("nbi"), sb_, -512.0); gat(G, oa, c("IDT"), sa); gat(G, c("tnA"), c("nbi"), sa, -512.0)
+    heads = [mm(G, c(b, 256, 512), pc("one", 0, 1), pc("cq", 0, 1), True, False)]
+    for p, at, ls in (("B", 0, ("Sdn", "dB")), ("A", 64, ("dA", "Sup"))):
+        heads.append(group(G, c(N2, 256 + at, 320 + at), [(c(ls[e]), c("tn" + p, e, 128, 2)) for e in range(2)])[0])
+        for e, h in enumerate("AB"):
+            o = c("O%s%d" % (p, t), e, 128, 2); mm(G, c(b, 256 + at, 320 + at), c("d%s4" % h), o, False, False); mm(G, c(b, 384 + at, 448 + at), c("d%s26" % h), o, False, at + e == 65)
+    nb = b if t else N2; names = lambda: (group(G, c(nb, 0, 128), [(c("dA"), c("tnA")), (c("dB"), c("tnB"))]), group(G, c(nb, 128, 256), [(c("dA"), oa), (c("dB"), ob)]))
+    nc = c("NC%d" % t, 0, 128)
+    if t:
+        for i in heads: behind(G, i, G["key"])
+        names(); act(G, c("N0"), c(N2, 256, 384)); act(G, c("NC%d" % t), c(b, 0, 384)); act(G, c("Q20"), c(b, 384, 512)); V0, Q1, Q2 = c("NC%d" % t, 128, 256), c("NC%d" % t, 256, 384), c("Q20")
+    else: vcp(G, c("N0"), c(N2, 256, 384)); V0, Q1, Q2 = c(nb, 128, 256), c(b, 256, 384), c(b, 384, 512)
 
-
-def maxima(G, x, m, W, a, b):
-    for r in range(4): vtt(G, c(m, 16 * a + r, 16 * b, 4), c(x, 16 * a + r, 16 * b, 4), c(W, 4 * a, 4 * b), O.max)
+    def rest(after=None):
+        i = vtt(G, c("t1B"), c("N0"), Q1, O.mult); angles(G, "B", Q2); vcp(G, c("hu0%d" % t), c("t3B"))
+        if not t: names(); vcp(G, nc, c(nb, 0, 128))
+        j = vtt(G, c("mk0%d" % t), nc, V0, O.is_equal); k = vts(G, c("wr0%d" % t), nc, 0.0, O.max)
+        for x in (i, j, k) if after else (): behind(G, x, after)
+    return rest
 
 
 def records(G, p):
@@ -353,22 +413,22 @@ def records(G, p):
     for a, b in zip(MCHUNKS, MCHUNKS[1:]):
         if a >= NV: vgat(G, c(x, 16 * a, 16 * b), c("E"), c(hu, a, b))
         else: last = gat(G, c(x, 16 * a, 16 * b), c("E"), c(hu, a, b))
-        maxima(G, x, m, "pw" + p, a, b)
+        for r in range(4): vtt(G, c(m, 16 * a + r, 16 * b, 4), c(x, 16 * a + r, 16 * b, 4), c("pw" + p, 4 * a, 4 * b), O.max)
     return last
 
 
-def scores(G, p, a, t, xb, mb, ks):
-    gid = ("key", p, a, t); pk = "pk" + p; key = c(pk, 0, 272); col = lambda k, n: pc(pk, 0, n, k + 1, 272, 17); at = 0 if a else (272 if p == "A" else 544)
-    nx = NA if a else 128
-    mm(G, key, pc("one", 0, 2), pc("cr", 0, 2, at, at + 272), True, False)
-    mm(G, pc(pk, 0, nx, 0, 272), c("qa" if p == "A" else "qr%d" % t, 0, nx), c("WN"), False, False, grp=gid)
+def scores(G, p, a, t, ks):
+    gid = ("key", p, a, t); pk = "pk" + p; key = c(pk, 0, 272); col = lambda k, n: pc(pk, 0, n, k + 1, 272, 17); at = 272 * (p == "B")
+    nx = NA if a else CHUNKS[p][-1]; w = len(ks)
+    if a: mm(G, key, c("qw" + p), c("WN"), True, False)
+    else: mm(G, key, pc("one", 0, 1), pc("cr", 0, 1, at, at + 272), True, False); mm(G, pc(pk, 0, nx, 0, 272), c("qa" if p == "A" else "qr%d" % t, 0, nx), c("WN"), False, False, grp=gid)
     if a: mm(G, c(pk, 0, 136, 17), c("Ib"), c("SP" + p, 0, 128, 16), False, False, grp=gid)
     else: mm(G, c(pk, 0, 136, 17), c("O%s%d" % (p, t)), c("Pick"), False, False, grp=gid)
     for l in [c("mk" + p, 128 * i, 128 * i + 128) for i in range(a + 1)] if a else [c("mk0%d" % t)]: mm(G, key, l, c("BIGP"), False, False, grp=gid)
-    for k in ks: mm(G, col(k, nx), c(xb, k, 16 * nx, 16), c("BX"), False, False, grp=gid)
-    for k in sorted(ks, key=lambda k: k % 4): mm(G, col(k, 128), c(mb, k, 2048, 16), c("BM"), False, False, grp=gid)
+    for k in ks: mm(G, col(k, nx), c("x" + p, k % w, w * nx, w), c("BX"), False, False, grp=gid)
+    for k in sorted(ks, key=lambda k: k % (w // 4)): mm(G, col(k, 128), c("m" + p, k % w, 128 * w, w), c("BM"), False, False, grp=gid)
     mm(G, key, c("wr" + p) if a else c("wr0%d" % t), c("Perm"), False, False)
-    mm(G, c(pk, 136, 272), c("n" + p) if a else c("NC%d" % t), c("nPerm"), False, True)
+    G["key"] = mm(G, c(pk, 136, 272), c("n" + p) if a else c("NC%d" % t, 0, 128), c("nPerm"), False, True)
 
 
 def atom(G, o, p, i, t, x, start, stop):
@@ -381,15 +441,14 @@ def slot(p, i): return c("ps" + p, 128 * i, 128 * i + 128) if i < 4 else (c("pw"
 
 def choose(G, p, a, t):
     RM = "RM" + p; SP = "SP" + p; RT = "RT" + p; pk = "pk" + p; sp = c(SP, 0, 128, 16)
-    path = c("CH%d" % t, 56 + 8 * a, 64 + 8 * a) if p == "A" else c("BL%d" % t, 40 - 8 * a, 48 - 8 * a)
+    path = (c("CH%d" % t, 56 + 8 * a, 64 + 8 * a) if a < ST - 1 else c("TA", 13, 141, 16)) if p == "A" else c("BL%d" % t, 40 - 8 * a, 48 - 8 * a)
     vscan(G, c(RM), c("SEG"), c(pk, 0, 272), O.add, O.min)
     vtt(G, sp if a < ST - 1 else path, c(RM, 16, 136, 17), c(RM, 152, 272, 17), O.subtract)
     if a == ST - 1: return
     vscan(G, c(RT, 0, 128), c("TR"), c(SP, 0, 128), O.mult, O.add); vscan(G, c("RR%d%s" % (a + 1, p)), c("S01"), c(SP, 0, 128), O.mult, O.add)
     li = c("pd" + p, 0, 8); group(G, li, [(c(SP, 1, 129), c("C8")), (c(RT, 0, 128), c("C8")), (c(RT, 1, 129), c("nC8"))]); vts(G, c("li" + p), li, 512.0, O.add)
-    Q2 = c(pk, 128, 256); mm(G, Q2, pc("one", 0, 2), pc("cq", 0, 2, 128, 256), True, False)
-    atom(G, Q2, p, a, t, "I2050", False, False); atom(G, Q2, p, a + 1, t, "I592", False, True); atom(G, slot(p, a + 1), p, a + 1, t, "Ib", True, True)
-    act(G, path, sp)
+    Q2 = c(pk, 128, 256); atom(G, Q2, p, a, t, "I2050", True, False); atom(G, Q2, p, a + 1, t, "I592", False, True); atom(G, slot(p, a + 1), p, a + 1, t, "Ib", True, True)
+    sel(G, path, sp, [[0, 8]], O.is_ge, 0, 0, 0)
 
 
 def front(G, p, a, t):
@@ -399,143 +458,170 @@ def front(G, p, a, t):
     for i in range(a, -1, -1): vtt(G, c("mk" + p, 128 * i, 128 * i + 128), n, slot(p, i), O.is_equal)
     last = records(G, p)
     if a < ST - 1: act(G, q1, slot(p, a), F.Identity, 2050.0, 4.0)
-    scores(G, p, a, t, "x" + p, "m" + p, list(range(16)))
+    scores(G, p, a, t, list(range(16)))
     return last
 
 
-def walk(G, t):
+def walk(G, t, atoms):
     qs = {"A": "qa", "B": "qr%d" % t}
-    for r in range(4): mm(G, c("pdA", r, 512, 4), c("Ib"), c(qs["A" if r < 2 else "B"]))
-    for a, b in zip(CHUNKS, CHUNKS[1:]): (vgat if b == 128 else gat)(G, c("xA", 16 * a, 16 * b), c("E"), c("hu0%d" % t, a, b)); maxima(G, "xA", "mA", "pdA", a, b)
     for p in "BA":
+        x, m, at, ch = "x" + p, "m" + p, 64 * (p == "A"), CHUNKS[p]; offs = lambda a, b: c("hu0%d" % t, at + a // 2, at + b // 2)
+        for r in range(4): mm(G, c("pw" + p, r, 512, 4), c("Ib"), c(qs[p]))
+        if ch[-1] < 128:
+            a = ch[-1]; d = "pd" + p; n = 1024 - 8 * a; gat(G, c(x, 8 * a, 1024), c("E"), offs(a, 128)); mm(G, c(d, 0, n), c("Ib"), c(x, 8 * a, 1024), True, False)
+            for r in range(8): mm(G, c(d, r, n, 8), c("nI"), c(qs[p], a, 128), False, r == 7)
+            act(G, c(m, 8 * a, 1024), c(d, 0, n), F.Abs, 0.0, 0.5)
+        for a, b in zip(ch, ch[1:]):
+            got = (gat if a else vgat)(G, c(x, 8 * a, 8 * b), c("E"), offs(a, b))
+            for r in range(2): vtt(G, c(m, 8 * a + r, 8 * b, 2), c(x, 8 * a + r, 8 * b, 2), c("pw" + p, 4 * a, 4 * b), O.max)
         atom(G, slot(p, 0), p, 0, t, "Ib", True, True); act(G, c("Q1" + p), c("O%s%d" % (p, t)), F.Identity, 2050.0, 4.0)
-        for r in range(4): mm(G, c("pw" + p, r, 4 * NA, 4), c("Ib"), c(qs[p], 0, NA))
-        if p == "B" or t == 0: gat(G, c("W4" + p), c(qs[p]), c("lW4"))
-    mm(G, c("pkA", 272, 280), c("OA%d" % t), c("Pick")); act(G, c("CH%d" % t, 48, 56), c("pkA", 272, 280))
-    scores(G, "B", 0, t, "xA", "mA", list(range(8, 16))); scores(G, "A", 0, t, "xA", "mA", list(range(8)))
+        if p == "B" or t == 0: gat(G, c("W4" + p), c(qs[p]), c("lW4")); act(G, c("qw" + p, 0, NA), c(qs[p], 0, NA), F.Identity, 127.5)
+        if p == "A": mm(G, c("pkA", 272, 280), c("OA%d" % t), c("Pick")); act(G, c("CH%d" % t, 48, 56), c("pkA", 272, 280))
+        scores(G, p, 0, t, list(range(8, 16) if p == "B" else range(8)))
+    if atoms: atoms(got)
     for a in range(1, ST):
         for p in "BA": choose(G, p, a - 1, t); last = front(G, p, a, t)
+        if a == ST - 2: G["late"] = last
     for p in "BA": choose(G, p, ST - 1, t)
     return last
 
 
+def pairs(G, t):
+    CH = "CH%d" % t; ct = pc("CT", 0, 96); k96 = lambda nm: pc(nm, 0, 96); one = pc("one", 0, 1); cp = lambda k: pc("cp", 0, 1, 288 * k, 288 * k + 288)
+    mm(G, pc("psB", 0, 96, 384, 512), c(CH, 0, 96), c("Ib")); vcp(G, ct, pc("psB", 0, 96, 384, 512))
+    mm(G, c("pdB", 0, 288), ct, k96("PU")); mm(G, c("pdB", 288, 416), k96("CN"), ct); act(G, c("UN"), c("pdB", 0, 416))
+    Q1, Q2, D = c("psB", 0, 288), c("pwB", 0, 288), c("pkB", 0, 288)
+    mm(G, Q1, ct, k96("PQ1")); mm(G, Q2, ct, k96("PQ2")); group(G, D, [(one, cp(0)), (ct, k96("DC"))])
+    vtt(G, c("h1"), c("UN", 0, 288), Q1, O.mult); vtt(G, c("h2"), c("h1"), Q2, O.add); vts(G, c("h3"), c("h2"), 4, O.arith_shift_right, 4095, O.bitwise_and)
+    act(G, c("h4", 1, 289), c("h3"), F.Identity, -2048.0); act(G, c("NA"), D, F.Abs); act(G, c("NE"), c("NA"), F.Sign)
+    group(G, D, [(one, cp(1)), (c("Ib"), c("h4", 0, 288)), (c("nI"), c("h4", 1, 289))])
+    mm(G, c("psA", 0, 256), pc("one1", 0, 1), pc("cq", 0, 1), True, False); mm(G, c("psA", 0, 128), k96("CQ1"), ct, False, False); mm(G, c("psA", 128, 256), k96("CQ2"), ct, False, False)
+
+
 def rings(G, t):
-    CH = "CH%d" % t; b6 = c("B6%d" % t); ct = pc("CT", 0, 104); col = lambda k: c("col", k, k + 1)
-    if t == 0:
-        mm(G, c("pdB", 0, 11), pc("Dmf", 0, 16), pc("R1", 0, 16, 0, 11), True, False); mm(G, c("pdB", 0, 2), pc("Dmf", 0, 16), pc("R2", 0, 16, 0, 2), False, True)
-        vcp(G, c("col", 0, 11), c("pdB", 0, 11))
-    mm(G, pc("psB", 0, 96, 384, 512), c(CH, 0, 96), c("Ib")); vcp(G, pc("CT", 0, 96), pc("psB", 0, 96, 384, 512))
-    mm(G, c("pkB", 0, 288), pc("CT", 0, 96), pc("DC", 0, 96)); vts(G, c("EQ"), c("pkB", 0, 288), 0.0, O.is_equal)
-    for i in range(1, 6): vtt(G, c("EQ", 6 * i - 1, 288, 36), c(CH, 48 + 8 * i, 56 + 8 * i), b6, O.is_equal)
-    for j in range(6): vtt(G, c("EQ", 30 + j, 288, 36), c(CH, 96, 104), c(CH, 40 - 8 * j, 48 - 8 * j) if j < 5 else b6, O.is_equal)
-    vscan(G, c("FJ"), c("DJ"), c("EQ"), O.add, O.max)
-    mm(G, pc("psB", 0, 8, 384, 512), b6, c("Ib")); vcp(G, pc("CT", 0, 8), pc("psB", 0, 8, 384, 512))
-    mm(G, pc("psB", 96, 104, 384, 512), c(CH, 96, 104), c("Ib")); vcp(G, pc("CT", 96, 104), pc("psB", 96, 104, 384, 512))
-    end = c("FJ", 35, 288, 36); vts(G, c("SPJ", 0, 128, 16), end, -1.0, O.mult, -5.5 / 1024, O.add); vcp(G, c("SPY", 0, 128, 16), end)
-    vscan(G, c("RRJ"), c("S0n"), c("SPJ"), O.mult, O.add); vscan(G, c("RRY"), c("S06"), c("SPY"), O.mult, O.add)
-    Z = c("pkA", 0, 128); group(G, Z, [(c("RRJ"), c("I1k")), (c("RRY"), c("I1k"))])
-    V1, V2, NN = [c("pdA", 128 * k, 128 * k + 128) for k in range(3)]; NP = c("pdB", 0, 128); Q1, Q2 = c("psA", 0, 128), c("psA", 128, 256); k104 = lambda nm: pc(nm, 0, 104)
-    group(G, V1, [(k104("CV1a"), ct), (k104("CV1b"), ct)]); mm(G, V2, k104("CV2"), ct); mm(G, NP, k104("CN"), ct, True, False)
-    mm(G, c("psA", 0, 256), pc("one", 0, 2), pc("cq", 0, 2), True, False); mm(G, Q1, k104("CQ1"), ct, False, False); mm(G, Q2, k104("CQ2"), ct, False, False)
-    vts(G, c("OH"), Z, col(0), O.is_equal); vtt(G, c("Y1"), c("OH"), V1, O.mult); vtt(G, c("Y2"), c("OH"), V2, O.mult)
-    vts(G, c("dead"), Z, col(2), O.mult, col(1), O.is_ge)
-    mm(G, NP, c("SA"), c("Y1"), False, True); mm(G, Q1, c("SB4"), c("Y1"), False, False); mm(G, Q2, c("SB2050"), c("Y1"), False, False); mm(G, Q2, c("SA592"), c("Y2"), False, True)
-    mm(G, NN, c("p4I"), c("dead")); act(G, c("Zs"), Z, F.Identity, col(3))
-    vcp(G, c("NR0"), NP); vtt(G, c("t1A"), c("NR0"), Q1, O.mult); angles(G, "A", Q2); vtt(G, c("HF"), c("t3A"), NN, O.max); vcp(G, c("huA"), c("HF"))
+    CH = "CH%d" % t; b6 = c("B6%d" % t); a6 = c("TA", 13, 141, 16); place = lambda k: c(CH, 8 * k, 8 * k + 8)
+    act(G, c("TB", 3, 128, 16), b6)
+    for i in range(1, 6): vtt(G, c("NE", 6 * i, 288, 36), place(12 - i), b6, O.not_equal)
+    for j in range(6): vtt(G, c("NE", j, 288, 36), a6, place(j) if j else b6, O.not_equal)
+    vscan(G, c("FJ"), c("DJ"), c("NE"), O.add, O.min); vscan(G, c("HS"), c("pkB", 0, 288), c("NE"), O.add, O.mult)
+    end = c("FJ", 35, 288, 36); vts(G, c("SPJ", 2, 128, 16), end, -64.0, O.mult, 45.0, O.add); vts(G, c("SPI", 3, 128, 16), end, 64.0, O.mult, 1029.5, O.add)
+    vts(G, c("HQ", 1, 128, 16), c("HS", 35, 288, 36), -2048.0, O.add)
+    vscan(G, c("RRJ"), c("MJ"), c("SPJ"), O.mult, O.add); vscan(G, c("RRI"), c("MI"), c("SPI"), O.mult, O.add)
+    Q1, Q2, ta = c("psA", 0, 128), c("psA", 128, 256), c("TA", 0, 128)
+    mm(G, Q1, c("TB"), c("I4"), False, False); mm(G, Q2, c("TB"), c("I2050"), False, False)
+    mm(G, Q1, ta, c("I4"), False, False); mm(G, Q2, ta, c("I2050"), False, False); mm(G, Q2, c("TA", 11, 139), c("I592"), False, True)
+    Z = c("pkA", 0, 128); group(G, Z, [(c("HQ"), c("Ib")), (c("RRJ"), c("p4I")), (c("RRI"), c("p4I"))])
+    vtt(G, c("t1A"), c("UN", 288, 416), Q1, O.mult); angles(G, "A", Q2); vtt(G, c("H0"), c("t3A"), Z, O.max)
+    vts(G, c("huA"), c("H0"), 4096.0, O.min); vts(G, c("HF"), c("H0"), 4096.0, O.min); vts(G, c("dead"), Z, 4096.0, O.is_ge); zs = act(G, c("Zs"), Z, F.Identity, 0.0, 1 / 4096)
+    mm(G, pc("pwA", 96, 104, 384, 512), a6, c("Ib")); act(G, pc("CT", 96, 104), pc("pwA", 96, 104, 384, 512))
     for nm, d, x in (("h5B", 32, 1025.0), ("h8B", 256, 129.0), ("h9B", 512, 129.0)):
         vts(G, c(nm), c("HF"), 1.0 / d, O.mult, x - (d - 1.0) / (2 * d), O.add)
     LO = c("psB", 0, 96); group(G, LO, [(c("HF"), c("Cmpf")), (c("h5B"), c("Cm5")), (c("h8B"), c("Cm8")), (c("h9B"), c("Cm9"))])
     for d in range(2): vts(G, c("LOT", 96 * d, 96 * d + 96), LO, 36928.0 - d, O.add)
     vts(G, c("LOT", 192, 384), c("LOT", 0, 192), -2.0, O.add)
-    for a, b in zip(RCHUNKS, RCHUNKS[1:]): (gat if a else vgat)(G, c("xA", 16 * a, 16 * b), c("E"), c("huA", a, b))
-    part = lambda nm, k: c(nm, 192 * k, 192 * k + 192); cnt = (c("pwB", 0, 192), c("psB", 96, 288))
-    for k, bank in enumerate(("pwA", "pkB")):
-        group(G, c(bank, 0, 192), [(c("dead"), part("DH", k)), (c("h5B"), part("C5", k)), (c("h8B"), part("C8x", k)), (c("h9B"), part("C9", k))]); act(G, part("HI0", k), c(bank, 0, 192))
+    got = [(gat if a else vgat)(G, c("xA", 16 * a, 16 * b), c("E"), c("huA", a, b)) for a, b in zip(RCHUNKS, RCHUNKS[1:])]
+    behind(G, zs, got[1]); behind(G, got[2], zs)
+    group(G, c("pkB", 0, 384), [(c("dead"), c("DH")), (c("h5B"), c("C5")), (c("h8B"), c("C8x")), (c("h9B"), c("C9"))]); act(G, c("HI0"), c("pkB", 0, 384)); cnt = c("psB", 96, 480)
     for u in range(0, 64, 4): vts(G, c("OHL", 96 * u, 96 * u + 384), c("LOT"), float(u), O.is_equal)
-    for a, b in zip(RCHUNKS, RCHUNKS[1:]): group(G, c("pdB", 128 + a, 128 + b), [(c("Ib"), c("xA", 16 * a + r, 16 * b, 16)) for r in range(1, 13)])
-    for k in range(2): mm(G, cnt[k], c("dead"), part("DC2", k), True, False)
-    vts(G, c("TH"), c("pdB", 128, 256), c("thf"), O.is_ge)
-    for k in range(2): mm(G, cnt[k], c("TH"), part("BlkC", k), False, True); vtt(G, part("HIT", k), part("HI0", k), cnt[k], O.min)
+    for a, b in ((0, RCHUNKS[2]), RCHUNKS[2:]): group(G, c("pdB", 128 + a, 128 + b), [(c("Ib"), c("xA", 16 * a + r, 16 * b, 16)) for r in range(1, 14)])
+    mm(G, cnt, c("dead"), c("DC2"), True, False); act(G, c("TH"), c("pdB", 128, 256), F.Sign, c("thf")); mm(G, cnt, c("TH"), c("BlkC"), False, True)
+    for k in range(2): vtt(G, c("HIT", 192 * k, 192 * k + 192), c("HI0", 192 * k, 192 * k + 192), c("psB", 96 + 192 * k, 288 + 192 * k), O.min)
 
 
 def ring_atoms(G, t):
-    ct = pc("CT", 0, 104); col = lambda k: c("col", k, k + 1); PL, PI, Y = [c("pkA", a, a + 128) for a in (128, 256, 384)]
-    mm(G, PI, c("PI"), c("Zs")); act(G, c("r1"), PI, F.Relu, col(9)); act(G, c("r2"), PI, F.Relu, col(10), -1.0)
-    group(G, PL, [(c("PZ"), c("Zs")), (c("I16"), c("r1"))])
-    for l in range(5): act(G, c("ZL", 128 * l, 128 * l + 128), PL, F.Abs, col(4 + l))
-    group(G, c("pdA", 0, 128), [(pc("AR", 0, 104), ct), (c("m4I"), c("r2")), (c("PD"), c("dead"))])
-    for l in range(5):
-        o = c("psA", 128 * l, 128 * l + 128) if l < 4 else c("pdA", 128, 256)
-        group(G, o, [(pc("BRL", 0, 104, 128 * l, 128 * l + 128), ct), (c("m4I"), c("ZL", 128 * l, 128 * l + 128))])
-    act(G, c("PB", 0, 256), c("pdA", 0, 256), F.Relu, 513.0); act(G, c("PB", 256, 768), c("psA"), F.Relu, 513.0)
-    group(G, Y, [(c("Ib"), c("PB", 128 * k, 128 * k + 128)) for k in range(6)])
-    y = c("YR", 128 * t, 128 * t + 128); act(G, y, Y, F.Identity, -1.0)
-    dma(G, lambda g, T: g.sync.dma_start(T.yr[:, 128 * t:128 * t + 128], ap(T, y)), [y], [], 2.0)
+    ct = pc("CT", 0, 104); col = lambda k: c("col", k, k + 1); PL, PI = c("pkA", 128, 256), c("pkA", 256, 384)
+    mm(G, PI, c("PI"), c("Zs")); act(G, c("r1"), PI, F.Relu, col(0), -1.0); act(G, c("r2"), PI, F.Relu, col(5))
+    group(G, PL, [(c("PZ"), c("Zs")), (c("PN"), c("dead")), (c("I16"), c("r1"))])
+    for l in range(5): act(G, c("ZL", 128 * l, 128 * l + 128), PL, F.Abs, col(l))
+
+    def rest(after=None):
+        group(G, c("psA", 256, 384), [(pc("AR", 0, 104), ct), (c("m4I"), c("r2")), (c("PD"), c("dead"))])
+        for l in range(5):
+            o = c("pdA", 128 * l, 128 * l + 128) if l < 4 else c("psA", 384, 512)
+            group(G, o, [(pc("BRL", 0, 104, 128 * l, 128 * l + 128), ct), (c("m4I"), c("ZL", 128 * l, 128 * l + 128))])
+        for j in (act(G, c("PB", 0, 256), c("psA", 256, 512), F.Relu, 513.0), act(G, c("PB", 256, 768), c("pdA"), F.Relu, 513.0)):
+            if after: behind(G, j, after)
+        G["atoms"] = j
+        Y = c("psA", 256, 384) if after else c("pkA", 384, 512); group(G, Y, [(c("Ib"), c("PB", 128 * k, 128 * k + 128)) for k in range(6)])
+        y = c("YR", 128 * t, 128 * t + 128); act(G, y, Y, F.Identity, -1.0)
+        dma(G, lambda g, T: g.sync.dma_start(T.yr[:, 128 * t:128 * t + 128], ap(T, y)), [y], [], 2.0)
+    return rest if t < RO - 1 else rest()
 
 
-def lessen(G, t, after):
-    for k in range(8):
-        behind(G, act(G, c("L16", 512 * k, 512 * k + 512), c("E", 512 * k, 512 * k + 512), F.Identity, *((1024.375, 0.75) if k < KV else (1023.625, 0.25))), after)
-    for k, bank in enumerate(("pwA", "pkB")):
-        hit = c("HIT", 192 * k, 192 * k + 192); th = "THH%d" % k; half = lambda nm: pc(nm, 64 * k, 64 * k + 64, 0, 256)
+def lessen(G, t, after, between):
+    eighth = lambda nm, k: c(nm, 512 * k, 512 * k + 512)
+    for k in range(KV, 8): behind(G, act(G, eighth("D16", k - KV), eighth("E", k), F.Identity, 1023.625, 0.25), after)
+    for k in range(KV): mm(G, c(BANKS[k]), c("Ib"), eighth("E", k), True, False)
+    for k in range(2):
+        hit = c("HIT", 192 * k, 192 * k + 192); th = "THH%d" % k
         for i in range(16):
             o = c(th, 192 * i, 192 * i + 192)
-            if i < NS: act(G, c("AB%d" % (i % 2)), hit, F.Abs, -4.0 * i); act(G, o, c("AB%d" % (i % 2)), F.Relu, 1.0, -1.0)
-            else: vts(G, o, hit, 4.0 * i, O.is_equal)
+            if i < NS: ab = c("AB", 192 * (NS * k + i), 192 * (NS * k + i + 1)); j = act(G, ab, hit, F.Abs, -4.0 * i); share = act(G, o, ab, F.Relu, 1.0, -1.0)
+            if i < NS and t == RO - 1: behind(G, j, G["atoms"])
+            if i >= NS: code = vts(G, o, hit, 4.0 * i, O.is_equal)
         for gl in range(4):
-            ms = group(G, pc(bank, 64 * k, 64 * k + 64, gl, 256, 4), [(c("OHL", 48 * k + 12 * gl + s, 6144, 96), c(th, 12 * gl + s, 3072, 48)) for s in range(12)])
-            if k and not gl: behind(G, ms[0], done)
-        done = ms[-1]
-        vts(G, half("NR"), half(bank), 0.0, O.is_equal, 4.0, O.subtract); vtr(G, half("NM"), half("NR"))
-    for k in (0, 6, 7, 1, 2, 3, 4, 5):
-        bank = ("pdA", "psA", "psB", "pdB")[k % 4] if k < KV else ("pkA", "pwA")[k % 2]; e = c("E", 512 * k, 512 * k + 512); o = c(bank, 0, 512)
-        mm(G, o, c("Ib"), c("L16", 512 * k, 512 * k + 512), True, False)
-        for h in range(2): mm(G, c(bank, 256 * h, 256 * h + 256), c("SelT", 256 * k + 128 * h, 256 * k + 128 * h + 128), c("NM"), False, h == 1)
-        if k < KV: vtt(G, e, e, o, O.min)
+            group(G, pc("pwA", 64 * k, 64 * k + 64, gl, 256, 4), [(c("OHL", 48 * k + 12 * gl + s, 6144, 96), c(th, 12 * gl + s, 3072, 48)) for s in range(12)])
+    between(code)
+    for k in range(KV): behind(G, act(G, eighth("L", k), eighth("E", k), F.Identity, 0.375, 0.75), share)
+    vts(G, c("NR"), c("pwA", 0, 256), 0.0, O.is_gt); vtr(G, c("NM"), c("NR")); prev = None
+    for k in EIGHTHS:
+        bank = BANKS[k]; e = eighth("E", k); o = c(bank)
+        if k >= KV: mm(G, o, c("Ib"), eighth("D16", k - KV), True, False)
+        for h in range(2):
+            i = mm(G, c(bank, 256 * h, 256 * h + 256), c("SelT", 256 * k + 128 * h, 256 * k + 128 * h + 128), c("NM"), False, h == 1)
+            if prev: behind(G, i, prev)
+            prev = i
+        if k < KV: vtt(G, e, eighth("L", k), o, O.max)
         else:
-            d = c("DD", 512 * (k % 2), 512 * (k % 2) + 512); act(G, d, o, F.Relu, -2048.0); o = c(("pwB", "pkB")[k % 2]); group(G, o, [(c("Ib"), e), (c("nI"), d)]); act(G, e, o)
-        if t == RO - 1 and (k % 2 or k == KV - 2):
-            a, b = 512 * (k if k in (KV - 2, KV - 1) else k - 1), 512 * k + 512
-            dma(G, lambda g, T, a=a, b=b: g.sync.dma_start(T.ye[:, a:b], T.E[:, a:b]), [c("E", a, b)], [], 1.5 + (b - a) / 1024)
+            d = c("DD", 512 * (k % 2), 512 * (k % 2) + 512); act(G, d, o, F.Relu, -2048.0); group(G, o, [(c("Ib"), e), (c("nI"), d)]); act(G, e, o)
+        if t == RO - 1 and (k % 2 or k >= KV - 2):
+            a, b = 512 * (k if k >= KV - 2 else k - 1), 512 * k + 512
+            for a, b in ((a, 4096 - TURN), (4096 - TURN, b)) if a < 4096 - TURN < b else ((a, b),):
+                dma(G, lambda g, T, a=a, b=b: g.sync.dma_start(T.ye[:, (a + TURN) % 4096:(b + TURN - 1) % 4096 + 1], T.E[:, a:b]), [c("E", a, b)], [], 1.5 + (b - a) / 1024)
 
 
 def build(rank, core, topo):
     G = {"ops": [], "acc": {}, "nd": [0]}; peers = [(rank + 1 + t) % N for t in range(RO)]; asks = [(rank - 1 - t) % N for t in range(RO)]; ne = 8
 
-    def send(src, dst, to):
-        def fn(g, T, sem):
-            a = topo.addr(T.cores[to]); m = 0
-            for e in topo.engines(core, T.cores[to])[:ne]: m |= 1 << e
-            return g.remote_dma(ap(T, dst), ap(T, src), T.sem[sem], T.sem.loc, a[1], a[0], m)
-        return fn
+    def exchange(moves, skip=0):
+        G["left"] = G.get("left", 0) + sum(m[4] for m in moves)
 
-    def exchange(sem, moves, dur):
-        sent = [add(G, "G", lambda g, T, fn=send(*m): fn(g, T, sem), [m[0]], [], 1.0, sem=("loc", 0)) for m in moves]
-        i = add(G, "N", None, [], [m[1] for m in moves], dur, sem=(sem, ne * len(moves)))
-        for s in sent: behind(G, i, s)
+        def fn(g, T):
+            go = []; used = skip
+            for sem, src, dst, to, k, dur in moves:
+                a = topo.addr(T.cores[to]); m = sum(1 << e for e in topo.engines(core, T.cores[to])[used:used + k]); used += k
+                if len(moves) == 1: return g.remote_dma(ap(T, dst), ap(T, src), T.sem[sem], T.sem.loc, a[1], a[0], m)
+                go.append(RemoteDMATransfer(dst_ids=[DstId(rid=a[0], pnc=a[1])], dma_engine_mask=m, remote_sem=T.sem[sem], src=ap(T, src), dst=ap(T, dst)))
+            return g.remote_dma_fused(go, local_sem=T.sem.loc)
+        before = G.get("sent"); G["sent"] = add(G, "G", fn, [m[1] for m in moves], [], ISSUE, sem=("loc", 0))
+        if before is not None: behind(G, G["sent"], before)
+        for sem in sorted({m[0] for m in moves}):
+            mine = [m for m in moves if m[0] == sem]; behind(G, add(G, "N", None, [], [m[2] for m in mine], mine[0][5], sem=(sem, sum(m[4] for m in mine))), G["sent"])
     dma(G, lambda g, T: g.sync.dma_start(T.sti[:], T.st[:]), [], [c("sti")], 1.5)
     dma(G, lambda g, T: g.sync.dma_start(T.qa[:], T.q[:]), [], [c("qa")], 1.6)
     dma(G, lambda g, T: g.sync.dma_start(T.nbi[:], T.nb[:]), [], [c("nbi")], 2.5)
-    dma(G, lambda g, T: g.sync.dma_start(T.E[:, 0:4096], T.ang[:]), [], [c("E", 0, 4096)], 4.5)
-    dma(G, lambda g, T: g.sync.dma_start(T.thi[:], T.th[:]), [], [c("thi")], 2.0)
+    for a, b in ((0, 4096 - TURN), (4096 - TURN, 4096)): dma(G, lambda g, T, a=a, b=b: g.sync.dma_start(T.E[:, a:b], T.ang[:, (a + TURN) % 4096:(b + TURN - 1) % 4096 + 1]), [], [c("E", a, b)], 4.5)
+    dma(G, lambda g, T: g.sync.dma_start(T.thi[:], T.th[:]), [], [c("thi")], 6.5)
     vcp(G, c("stu"), c("sti"))
-    for k, ts in enumerate(([0], [1, 2])):
-        exchange("as%d" % k, [(c("stu", 8 * t, 8 * t + 8), c("sr%d" % t), peers[t]) for t in ts], 6.0 if k else 1.2)
-        exchange("aq%d" % k, [(c("qa"), c("qr%d" % t), peers[t]) for t in ts], 6.0 if k else 1.2)
-    walk_constants(G)
-    vts(G, c("NB"), c("nbi"), -512.0, O.add); vcp(G, c("thf"), c("thi"))
-    first(G, 0, gat); ring_constants(G)
+    starts = lambda t, k, dur: ("as%d" % min(t, 1), c("stu", 8 * t, 8 * t + 8), c("sr%d" % t), peers[t], k, dur)
+    walk_constants(G); exchange([starts(0, ne, 0.7)])
+    exchange([("aq%d" % min(t, 1), c("qa"), c("qr%d" % t), peers[t], ne // 4 if t else ne // 2, 8.0 if t else 0.7) for t in range(RO)])
+    exchange([starts(t, ne // 2, 6.0) for t in (1, 2)], ne)
+    first(G, 0)(); behind(G, act(G, c("NB"), c("nbi"), F.Identity, -512.0), G["tn"]); atoms = None; scaled = ring_constants(G)
     for t in range(RO):
-        last = walk(G, t)
-        exchange("ar%d" % t, [(c("BL%d" % t, 8, 48), c("CH%d" % t, 8, 48), asks[t])], 4.5)
-        exchange("al%d" % t, [(c("BL%d" % t, 0, 8), c("B6%d" % t), asks[t])], 2.5)
-        if t < RO - 1: first(G, t + 1, vgat)
-        rings(G, t); ring_atoms(G, t); lessen(G, t, last)
+        last = walk(G, t, atoms)
+        if not t: scaled(G["late"])
+        exchange([("ar%d" % t, c("BL%d" % t, 8, 48), c("CH%d" % t, 8, 48), asks[t], 2 * ne, 3.2)])
+        exchange([("al%d" % t, c("BL%d" % t, 0, 8), c("B6%d" % t), asks[t], 2 * ne, 1.5)])
+        pairs(G, t); lists = first(G, t + 1) if t < RO - 1 else lambda i: None
+        rings(G, t); atoms = ring_atoms(G, t); lessen(G, t, last, lists)
     return G, ne
 
 
 def rank_program(g, core, T, topo):
     rank = T.rank_of(core)
     if rank is None: return
-    G, ne = build(rank, core, topo); emit(G, schedule(G), g, T)
-    g.wait_ge(T.sem.loc, ne * 4 * RO)
+    G, ne = build(rank, core, topo)
+    if not ORDER: ORDER["all"] = schedule(G)
+    emit(G, ORDER["all"], g, T)
+    g.wait_ge(T.sem.loc, G["left"])

from concourse.bass import DstId, RemoteDMATransfer
from concourse.mybir import AluOpType as O, ActivationFunctionType as F

N, RO, ST = 4, 3, 6
CHUNKS = {"B": (0, 48, 88, 128), "A": (0, 32, 64)}
MCHUNKS = (0, 32, 64, 80, 96)
NV, NA = 64, 96
RCHUNKS = (0, 24, 80, 128)
TURN = 2688
NS, KV = 2, 6
BANKS = ("pwB", "pkB", "pdB", "psB", "pdA", "psA", "pkA", "pwA"); EIGHTHS = (0, 6, 1, 7, 2, 3, 4, 5)
SCRATCH, SHAPE, WIDE, PLACE, ORDER = {}, {}, {}, {}, {}
SEMAPHORES = ["sv", "ss", "sp", "sg", "as0", "as1", "aq0", "aq1", "ar0", "ar1", "ar2", "al0", "al1", "al2", "loc"] + ["d%d" % i for i in range(20)]
QSEM = {"V": "sv", "S": "ss", "P": "sp", "G": "sg"}
POOL = {"float32": "poolf", "bfloat16": "poolb", "float16": "poolh", "int32": "pooli", "uint16": "poolu"}
APART = "stu sr0 sr1 sr2 qa qr0 qr1 qr2 sti thi CH0 CH1 CH2 BL0 BL1 BL2 B60 B61 B62 YR".split()


def many(dtype, cols, names):
    for n in names.split():
        if cols > 816 or n in APART: SCRATCH[n] = ("sbuf", [128, cols], dtype); continue
        pool = SCRATCH.setdefault(POOL[dtype], ("sbuf", [128, 0], dtype)); PLACE[n] = (POOL[dtype], pool[1][1]); SHAPE[n] = [128, cols]; WIDE[n] = dtype in ("float32", "int32")
        pool[1][1] += -(-cols // 32) * 32


many("int32", 1024, "nbi"); many("float32", 1024, "NB IDT"); many("bfloat16", 4112, "E"); many("int32", 512 * KV, "L"); many("float16", 4096 - 512 * KV, "D16")
many("bfloat16", 128, "qa qr0 qr1 qr2"); many("int32", 24, "sti"); many("uint16", 24, "stu"); many("uint16", 8, "sr0 sr1 sr2"); many("int32", 1, "thi"); many("float32", 1, "thf")
many("uint16", 8, "lW4"); many("int32", 4, "pci"); many("float32", 12, "pcf"); many("float32", 136, "CI S1 GC"); many("float32", 128, "CR"); many("float32", 16, "G16"); many("float32", 272, "SEG")
many("bfloat16", 128, "Sdn Sup Ib I592 dA dB dA4 dB4 S01 TR nI one W4A W4B"); many("float16", 128, "I2050 dA26 dB26"); many("float16", 256, "cq")
many("bfloat16", 272, "Perm BIGP WN"); many("bfloat16", 136, "nPerm"); many("bfloat16", 544, "cr"); many("float16", 128, "qwA qwB"); many("bfloat16", 16, "BX BM"); many("bfloat16", 8, "C8 nC8 Pick")
many("bfloat16", 288, "Zb DC PU PQ1"); many("bfloat16", 384, "BlkC DC2 C5 C8x C9 DH"); many("float16", 288, "Zh DJ PQ2"); many("float32", 8, "col"); many("float16", 576, "cp")
many("bfloat16", 128, "CN CQ1 one1 MI MJ PZ PI PD PN AR I4 I16 m4I p4I"); many("float16", 128, "CQ2"); many("bfloat16", 640, "BRL")
many("float32", 96, "Cmpf"); many("bfloat16", 96, "Cm5 Cm8 Cm9"); many("bfloat16", 2048, "SelT")
many("float16", 128, "CT N0 tnA tnB h5B SPJ RRJ TB HQ"); many("float16", 144, "TA"); many("float16", 288, "FJ"); many("float16", 289, "h4"); many("float16", 416, "UN"); many("bfloat16", 288, "NE NA")
many("float32", 288, "h1 HS"); many("int32", 288, "h2 h3"); many("bfloat16", 128, "dead h8B h9B TH Zs r1 r2 SPI RRI"); many("float32", 128, "H0 HF Q20")
many("bfloat16", 384, "LOT HI0 HIT"); many("bfloat16", 384 * NS, "AB"); many("bfloat16", 6144, "OHL"); many("bfloat16", 3072, "THH0 THH1")
many("bfloat16", 256, "NR NM"); many("bfloat16", 640, "ZL"); many("bfloat16", 1024, "DD"); many("float16", 768, "PB"); many("float32", 384, "YR")
for _p in "AB":
    for _d, _c, _l in (("float16", 128, "n wr RR1 RR2 RR3 RR4 RR5"), ("float16", 144, "SP RT"), ("float32", 128, "t1 Q1"), ("int32", 128, "t2 t3"), ("uint16", 128, "hu"),
                       ("bfloat16", 2048, "x m"), ("bfloat16", 768, "mk"), ("float32", 272, "RM"), ("uint16", 8, "li")):
        many(_d, _c, " ".join(n + _p for n in _l.split()))
    for _n in "kwds": SCRATCH["p" + _n + _p] = ("psum", [128, 512], "float32")
for _t in range(RO):
    many("uint16", 128, "hu0%d" % _t); many("bfloat16", 128, "mk0%d" % _t); many("float16", 128, "wr0%d OA%d OB%d" % (_t, _t, _t)); many("float16", 384, "NC%d" % _t)
    many("float16", 96, "CH%d" % _t); many("float16", 48, "BL%d" % _t); many("float16", 8, "B6%d" % _t)
SHAPE.update({k: s[1] for k, s in SCRATCH.items()})
PSUM = {k for k, s in SCRATCH.items() if s[0] == "psum"}
WIDE.update({k: s[2] in ("float32", "int32") for k, s in SCRATCH.items()})


def pc(name, p0, p1, a=None, b=None, s=None):
    a, b, s = slice(a, b, s).indices(SHAPE[name][1]); k = len(range(a, b, s)); b = a + (k - 1) * s + 1; off = PLACE[name][1] if name in PLACE else 0
    return (name, (slice(p0, p1), slice(a + off, b + off, s)), ((p0, p1, 1), (a, b, s)), k)


def c(name, a=None, b=None, s=None): return pc(name, 0, 128, a, b, s)


def ap(T, w): return T[PLACE[w[0]][0] if w[0] in PLACE else w[0]][w[1]]


def overlap(r, q):
    for (a, b, s), (d, e, u) in zip(r, q):
        if a >= e or d >= b: return False
        if s > 1 and u > 1 and (s % u == 0 or u % s == 0) and (a - d) % min(s, u): return False
    return True


def covers(r, q): return all(s == 1 and a <= d and b >= e for (a, b, s), (d, e, u) in zip(r, q)) or r == q


def add(G, q, fn, R, W, dur, grp=None, sem=None, gn=0):
    i = len(G["ops"]); deps = {}
    for w, isw in [(x, False) for x in R] + [(x, True) for x in W]:
        name, reg = w[0], w[2]; keep = []
        if name in PSUM:
            who, was, now = G["acc"].get(name, (q, [], []))
            if who != q: was, now = [j for j, g2 in now], []
            for j in was: deps[j] = True
            if q == "P":
                for j, g2 in now:
                    if j != i and (grp is None or grp != g2): deps.setdefault(j, False)
                if grp is None: now = []
            G["acc"][name] = (q, was, now + [(i, grp)]); continue
        for e in G["acc"].get(name, ()):
            j, r2, w2 = e
            if j == i: keep.append(e); continue
            ov = overlap(reg, r2)
            if ov and (isw or w2): deps[j] = True
            if not (isw and ov and covers(reg, r2)): keep.append(e)
        keep.append((i, reg, isw)); G["acc"][name] = keep
    G["ops"].append({"q": q, "fn": fn, "deps": deps, "dur": dur, "sem": sem, "to": W[0][0] if W else "", "gn": gn})
    return i


def behind(G, i, j): G["ops"][i]["deps"].setdefault(j, False)


VC, GR, PC = 0.00083, 1.56, 0.00042


def vcost(n, f): return max(64, n * f) * VC


def two(*ws): return all(not WIDE[w[0]] for w in ws)


def num(T, x): return ap(T, x) if isinstance(x, tuple) else x


def cols(*xs): return [x for x in xs if isinstance(x, tuple)]


def vtt(G, o, a, b, op):
    return add(G, "V", lambda g, T: g.vector.tensor_tensor(ap(T, o), ap(T, a), ap(T, b), op), [a, b], [o], vcost(o[3], 1 if (a[0] in PSUM or b[0] in PSUM) else 2))


def vts(G, o, a, s1, op0, s2=None, op1=None):
    def fn(g, T):
        if op1 is None: return g.vector.tensor_scalar(ap(T, o), ap(T, a), num(T, s1), None, op0)
        return g.vector.tensor_scalar(ap(T, o), ap(T, a), num(T, s1), num(T, s2), op0, op1)
    return add(G, "V", fn, [a] + cols(s1, s2), [o], vcost(o[3], 0.5 if two(o, a) else 1))


def vcp(G, o, a): return add(G, "V", lambda g, T: g.vector.tensor_copy(ap(T, o), ap(T, a)), [a], [o], vcost(o[3], 0.5 if two(o, a) else 1))


def vscan(G, o, a, b, op0, op1):
    add(G, "V", lambda g, T: g.vector.tensor_tensor_scan(ap(T, o), ap(T, a), ap(T, b), 0.0, op0, op1), [a, b], [o], vcost(o[3], 0.5 if two(o, a, b) else 1))


def vtr(G, o, a): add(G, "V", lambda g, T: g.vector.transpose(ap(T, o), ap(T, a)), [a], [o], vcost(o[3], 0.5 if two(o, a) else 1))


def vset(G, o, x): add(G, "V", lambda g, T: g.vector.memset(ap(T, o), x), [], [o], vcost(o[3], 0.5 if two(o) else 1))


def vgat(G, o, w, off):
    return add(G, "V", lambda g, T: g.vector.tensor_copy(ap(T, o), ap(T, w).indirect(ap(T, off))), [w, off], [o], o[3] * VC * GR + 0.05, gn=o[3])


def vgop(G, o, w, off, b, op):
    add(G, "V", lambda g, T: g.vector.tensor_tensor(ap(T, o), ap(T, w).indirect(ap(T, off)), ap(T, b), op), [w, off, b], [o], o[3] * VC * 2 + 0.05)


def act(G, o, a, func=F.Copy, bias=0.0, scale=1.0):
    return add(G, "S", lambda g, T: g.scalar.activation(ap(T, o), ap(T, a), func, bias=num(T, bias), scale=scale), [a] + cols(bias), [o], max(64, o[3]) * VC + 0.02)


def gat(G, o, w, off, bias=0.0):
    return add(G, "S", lambda g, T: g.scalar.activation(ap(T, o), ap(T, w).indirect(ap(T, off)), F.Identity if bias else F.Copy, bias=bias), [w, off], [o], o[3] * VC * GR + 0.065, gn=o[3])


def mm(G, o, l, r, start=True, stop=True, grp=None):
    return add(G, "P", lambda g, T: g.tensor.matmul(ap(T, o), ap(T, l), ap(T, r), start, stop), [l, r], [o], max(min(64, l[3]), r[3]) * (4 if WIDE[l[0]] else 1) * PC, grp=grp)


def group(G, o, terms):
    return [mm(G, o, l, r, i == 0, i == len(terms) - 1) for i, (l, r) in enumerate(terms)]


def iota(G, o, pat, base, cm, small=True):
    def fn(g, T):
        if small: return g.iota(ap(T, o), pat, base, cm, allow_small_or_imprecise_dtypes=True)
        return g.iota(ap(T, o), pat, base, cm)
    i = add(G, "G", fn, [], [o], 1.25 * (0.13 + o[3] * 2 * VC))
    if "sent" in G: behind(G, i, G["sent"])
    G["sent"] = i


def sel(G, o, a, pat, op, fill, base, cm=1):
    behind(G, add(G, "G", lambda g, T: g.affine_select(ap(T, o), ap(T, a), pat, op, float(fill), base, cm), [a], [o], 1.25 * (0.17 + o[3] * 2 * VC)), G["sent"])


def dma(G, fn, R, W, dur):
    k = "d%d" % G["nd"][0]; G["nd"][0] += 1; add(G, "Y", fn, R, W, dur, sem=(k, 16))


PASSES = 3; SAME, CROSS, ISSUE = 0.2, 0.27, 1.5
LATER = {"Vm": 2.0, "Vmk": 3.0, "Swr": 2.0, "Vx": 0.5}
PACES = ((1.0, 1.0, 1.5, 0.2, 0.27, 0.7), (1.3, 1.3, 1.2, 0.1, 0.15, 1.5), (1.3, 1.3, 1.9, 0.15, 0.2, 0.7), (1.15, 1.9, 1.3, 0.15, 0.2, 1.0))
TRIES, REACH, AHEAD = 2000, 6, 600


def schedule(G):
    ops = G["ops"]; n = len(ops); succ = [[] for _ in ops]; need = [0] * n
    for i, o in enumerate(ops):
        need[i] = len(o["deps"])
        for d in o["deps"]: succ[d].append(i)

    def lat(d, i): return 0.0 if not ops[i]["deps"][d] else (SAME if ops[d]["q"] == ops[i]["q"] else CROSS)
    far = [0.0] * n; pr = [0.0] * n
    for i in range(n - 1, -1, -1):
        far[i] = ops[i]["dur"] + max([far[s] + lat(i, s) for s in succ[i]] + [0.0]); pr[i] = far[i] - LATER.get(ops[i]["q"] + ops[i]["to"][:-1], 0.0)
    free = {q: 0.0 for q in "VSPGYN"}; ready = {q: [] for q in free}; rt = [0.0] * n; at = [0.0] * n
    for i in range(n):
        if not need[i]: ready[ops[i]["q"]].append(i)
    for _ in range(n):
        best = None
        for q in free:
            if not ready[q]: continue
            t0 = max(free[q], min(rt[i] for i in ready[q]))
            i = max((j for j in ready[q] if rt[j] <= t0 + 1e-9), key=lambda j: (pr[j], -j))
            if best is None or t0 < best[0]: best = (t0, i)
        t0, i = best; q = ops[i]["q"]; ready[q].remove(i); at[i] = t0; end = t0 + ops[i]["dur"]; free[q] = end if q in QSEM else t0 + 0.1
        for s in succ[i]:
            rt[s] = max(rt[s], end + lat(i, s)); need[s] -= 1
            if not need[s]: ready[ops[s]["q"]].append(s)
    pred = [list(o["deps"]) for o in ops]; dur = [o["dur"] for o in ops]

    def place(seq, before, gap):
        at = [0.0] * n; busy = {q: ([], []) for q in QSEM}
        for i in seq:
            t0 = max([at[d] + dur[d] + gap(d, i) for d in before[i]] + [0.0])
            if ops[i]["q"] in busy:
                a, b = busy[ops[i]["q"]]; lo, hi = 0, len(b)
                while lo < hi:
                    mid = (lo + hi) // 2
                    if b[mid] <= t0 + 1e-9: lo = mid + 1
                    else: hi = mid
                while lo < len(a) and a[lo] < t0 + dur[i] - 1e-9: t0 = max(t0, b[lo]); lo += 1
                a.insert(lo, t0); b.insert(lo, t0 + dur[i])
            at[i] = t0
        return at
    best = (max(at[i] + dur[i] for i in range(n)), at)
    for _ in range(PASSES):
        back = place(sorted(range(n), key=lambda i: -at[i] - dur[i]), succ, lambda d, i: lat(i, d))
        at = place(sorted(range(n), key=lambda i: -back[i] - dur[i]), pred, lat); end = max(at[i] + dur[i] for i in range(n))
        if end < best[0]: best = (end, at)
    return polish(ops, sorted(range(n), key=lambda i: (best[1][i], i)))


def polish(ops, order):
    n = len(ops); q = [o["q"] for o in ops]; deps = [set(o["deps"]) for o in ops]; S = range(len(PACES))
    dur = [[(o["dur"] + o["gn"] * VC * (gr - GR)) * (far if o["sem"] else (fp if o["q"] == "P" else f)) for o in ops] for f, fp, gr, a, b, far in PACES]
    wait = [[[(j, (a if q[j] == q[i] else b) if w else 0.0) for j, w in o["deps"].items() if w or q[i] == "N"] for i, o in enumerate(ops)] for f, fp, gr, a, b, far in PACES]
    end, free, why = [[[x] * n for s in S] for x in (0.0, 0.0, None)]

    def run(s, lo, hi, E, Fr, W):
        last = {}
        for x in order[max(0, lo - 900):lo]: last[q[x]] = x
        for i in order[lo:hi]:
            y = last.get(q[i]) if q[i] != "N" else None; t = 0.0 if y is None else Fr[y]
            for j, w in wait[s][i]:
                if E[j] + w > t: t = E[j] + w; y = j
            E[i] = t + dur[s][i]; Fr[i] = t + 0.1 if q[i] == "Y" else E[i]; W[i] = y; last[q[i]] = i
        return far(hi, E)

    def far(hi, E):
        last = {q[x]: E[x] for x in order[max(0, hi - 60):hi]}
        return max(last.values()) + sum(last.get(k, 0.0) for k in "VSP") / 12
    norm = [run(s, 0, n, end[s], free[s], why[s]) for s in S]; tried = set(); left = TRIES; gained = True
    while gained and left > 0:
        gained = False; pairs = set(); pos = {x: k for k, x in enumerate(order)}
        for s in S:
            j = max(range(n), key=lambda x: end[s][x])
            while why[s][j] is not None:
                i = why[s][j]
                if q[i] == q[j] and q[j] in QSEM and i not in deps[j]: pairs.add((pos[j], i, j))
                j = i
        for _, i, j in sorted(pairs):
            for ahead in (True, False):
                a, b = pos[i], pos[j]
                if (i, j, ahead) in tried or a > b or left <= 0: continue
                tried.add((i, j, ahead)); old = order[a:b + 1]; move = {j if ahead else i}
                for x in (old[-2::-1] if ahead else old[1:]):
                    if (any(x in deps[z] for z in move) if ahead else deps[x] & move): move.add(x)
                if (i in move and j in move) or len(move) > REACH or (ahead and sum(q[x] == q[j] for x in move) > 1): continue
                hi = min(n, b + AHEAD); was = sum(far(hi, end[s]) / norm[s] for s in S); left -= 1
                order[a:b + 1] = [x for x in old if (x in move) == ahead] + [x for x in old if (x in move) != ahead]
                if sum(run(s, a, hi, list(end[s]), list(free[s]), {}) / norm[s] for s in S) < was - 1e-6:
                    for s in S: run(s, a, n, end[s], free[s], why[s])
                    pos.update({x: a + k for k, x in enumerate(order[a:b + 1])}); gained = True; break
                order[a:b + 1] = old
    return order


def emit(G, order, g, T):
    ops = G["ops"]; eng = {"V": g.vector, "S": g.scalar, "P": g.tensor, "G": g, "Y": g.sync}
    clock = {q: {} for q in eng}; snap = {}; cnt = {q: 0 for q in QSEM}; done = {}
    for i in order:
        o = ops[i]; q = o["q"]
        if q == "N": done[i] = o["sem"]; snap[i] = {}; continue
        ck = clock[q]; want = {}
        for d, w in o["deps"].items():
            if w:
                s, x = done[d]
                if ck.get(s, 0) < x and want.get(s, (0, 0))[0] < x: want[s] = (x, d)
        for s, (x, d) in sorted(want.items(), key=lambda z: -z[1][1]):
            if ck.get(s, 0) >= x: continue
            eng[q].wait_ge(T.sem[s], x); ck[s] = x
            for s2, x2 in snap[d].items():
                if ck.get(s2, 0) < x2: ck[s2] = x2
        snap[i] = dict(ck); ins = o["fn"](g, T)
        if o["sem"] is not None:
            if q == "Y": ins.then_inc(T.sem[o["sem"][0]], o["sem"][1])
            done[i] = o["sem"]
        else:
            cnt[q] += 1; ins.then_inc(T.sem[QSEM[q]], 1); done[i] = (QSEM[q], cnt[q])
    for q in QSEM: g.wait_ge(T.sem[QSEM[q]], cnt[q])
    for k in range(G["nd"][0]): g.wait_ge(T.sem["d%d" % k], 16)


def walk_constants(G):
    iota(G, c("pci", 0, 1), [[0, 1]], 0, 1, False)
    iota(G, c("CI"), [[1, 136]], 0, 0); iota(G, c("G16"), [[0, 2], [1, 8]], 0, 0)
    for k in range(8): act(G, c("IDT", 128 * k, 128 * k + 128), c("CI", 0, 128), F.Identity, 128.0 * k - 512)
    iota(G, c("CR"), [[0, 8], [1, 16]], 0, 0); iota(G, c("S1"), [[0, 8], [1, 17]], -1, 0); iota(G, c("GC"), [[1, 8], [0, 17]], 0, 0)
    p = c("pci", 0, 1); vts(G, c("pci", 1, 2), p, 15, O.bitwise_and); vts(G, c("pci", 2, 3), p, 4, O.arith_shift_right); vcp(G, c("pcf", 0, 3), c("pci", 0, 3))
    vts(G, c("pci", 3, 4), p, 2, O.arith_shift_right, 3, O.bitwise_and); vts(G, c("pcf", 11, 12), c("pci", 3, 4), float(NA), O.add)
    vts(G, c("lW4"), c("CI", 0, 8), 4.0, O.mult, c("pcf", 11, 12), O.add)
    P, PR, PG, SL, ha, hb, R0, k1, k2, k3, k4 = [c("pcf", k, k + 1) for k in range(11)]
    vts(G, SL, P, PG, O.add, 1.0, O.add); vts(G, ha, PR, 7.5, O.is_le); vts(G, hb, PR, 7.5, O.is_ge); vts(G, R0, PR, 0.0, O.is_equal)
    vts(G, c("Ib"), c("CI", 0, 128), P, O.is_equal)
    for nm, x in (("I592", 592.0), ("I2050", 2050.0), ("nI", -1.0)): vts(G, c(nm), c("Ib"), x, O.mult)
    for h, col in (("A", ha), ("B", hb)):
        for nm, x in (("", 1.0), ("4", 4.0), ("26", 2642.0)): vts(G, c("d" + h + nm), c("Ib"), col, O.mult, x, O.mult)
    vts(G, c("Sdn"), c("CI", 8, 136), P, O.is_equal, hb, O.mult); vts(G, k1, P, 8.0, O.add); vts(G, c("Sup"), c("CI", 0, 128), k1, O.is_equal, ha, O.mult)
    vset(G, pc("one", 0, 1), 1.0); vset(G, pc("cq", 0, 1, 0, 128), 2050.0); vset(G, pc("cq", 0, 1, 128, 256), 0.0)
    vts(G, c("S01"), c("CR"), 0.0, O.not_equal); vts(G, c("TR"), c("CR"), PR, O.is_le); vset(G, c("TR", 0, 128, 16), 0.0)
    vts(G, c("C8"), c("G16", 0, 8), PG, O.is_equal); vts(G, c("Pick"), c("C8"), R0, O.mult); vts(G, c("nC8"), c("C8"), -1.0, O.mult)
    vts(G, c("BX"), c("G16"), PG, O.is_equal, -8192.0, O.mult); vts(G, c("BM"), c("BX"), -2.0, O.mult)
    for h in (0, 136):
        vts(G, c("Perm", h, h + 136), c("CI"), SL, O.is_equal); vts(G, c("WN", h, h + 136), c("GC"), PG, O.is_equal, -8192.0, O.mult)
    vset(G, c("SEG"), -512.0); vset(G, c("SEG", 0, 272, 17), 2.0 ** 30); vset(G, c("SEG", 1, 272, 17), 16720896.0)
    vset(G, c("WN", 0, 272, 17), 0.0); vts(G, c("BIGP"), c("Perm"), 2.0 ** 26, O.mult); vts(G, c("nPerm"), c("Perm", 0, 136), -1.0, O.mult)
    for at, op in ((0, O.is_ge), (272, O.is_le)):
        r = pc("cr", 0, 1, at, at + 136); vts(G, r, pc("S1", 0, 1), 7.5, op, 2.0 ** 27, O.mult); vts(G, r, r, -255.0 * 65536, O.add); vcp(G, pc("cr", 0, 1, at + 136, at + 272), r)
    vset(G, pc("cr", 0, 1, 0, 544, 17), 0.0)
    for p_ in "AB": vset(G, c("qw" + p_, NA, 128), 127.5)
    for p_ in "AB": vset(G, c("SP" + p_), 0.0); vset(G, c("RT" + p_, 128, 144), 0.0)
    vset(G, c("E", 4096, 4112), 0.0)


def ring_constants(G):
    ne, ge = O.not_equal, O.is_ge
    for nm in ("Zb", "Zh", "TA", "TB", "HQ"): vset(G, c(nm), 0.0)
    vset(G, c("h4", 0, 1), -2048.0)
    for t in range(RO): vset(G, c("CH%d" % t, 0, 8), 0.0)

    def put(w, items, fresh=True):
        for pat, base, x in items: sel(G, w, c("Zh" if w[0] in ("PQ2", "CQ2") else "Zb", 0, w[3]) if fresh else w, pat, ne, x, base); fresh = False

    def fill(w, x): sel(G, w, w, [[0, w[3]]], O.is_gt, x, 0, 0)
    diag = lambda d, x: ([[-1, 8], [-8, 16]], -8 * d, x)
    sides = lambda d, e, x: [([[-1, 8], [1000, 2], [-8, 8]], -8 * d, x), ([[-1, 8], [1000, 2], [-8, 8]], -8 * e - 1064, x)]
    rows = lambda r, x: ([[-16, 8], [0, 16]], -r, x)
    up16, dn16 = [[0, 8], [1, 16]], [[0, 8], [-1, 16]]; byi, byj = [[-1, 8], [8, 6], [0, 6]], [[-1, 8], [0, 6], [-8, 6]]
    put(c("DC"), [(byi, -96, 1), (byj, 0, -1)]); put(c("PU"), [(byi, -88, 1)]); put(c("PQ1"), [(byj, -8, 4)])
    put(c("PQ2"), [(byj, -8, 2050), (byi, -88, 2050), (byi, -96, 592), ([[-1, 8], [1000, 6], [-8, 6]], 0, 592)])
    for k in range(2): vset(G, pc("cp", 0, 1, 288 * k, 288 * k + 288), 0.0)
    for k, a, x in ((0, 35, 4096), (1, 0, -4096), (1, 1, 4096)): fill(pc("cp", 0, 1, 288 * k + a, 288 * k + 288, 36), x)
    for nm in ("PU", "PQ2"):
        for a in (0, 35): fill(c(nm, a, 288, 36), 0)
    sel(G, c("DJ"), c("Zh"), [[0, 288]], O.is_gt, 1 / 64, 0, 0); sel(G, c("DJ"), c("DJ"), [[0, 48], [1, 6]], ne, 3 / 64, 0, 0); fill(c("DJ", 0, 288, 36), 4)
    put(c("CN"), sides(-1, -3, 1)); put(c("CQ1"), sides(-3, -1, 4)); put(c("CQ2"), sides(-3, -1, 2050) + [diag(-2, 592)])
    for nm, x in (("CQ1", 4), ("CQ2", 2050)): put(c(nm, 2, 128, 16), [([[-1, 8]], -88, x)], False)
    sel(G, pc("one1", 0, 1), pc("one", 0, 1), up16, ne, 0, -1, 0)
    sel(G, c("MI"), c("S01"), up16, ge, 0, -4, 0); sel(G, c("SPI"), c("S01"), up16, ge, 0, -9, 0)
    sel(G, c("MJ"), c("S01"), up16, ge, 0, -3, 0); sel(G, c("MJ"), c("MJ"), dn16, ge, 0, 7, 0); sel(G, c("SPJ"), c("Zh", 0, 128), dn16, ge, -1, 3, 0); sel(G, c("SPJ"), c("SPJ"), dn16, ge, 0, 7, 0)
    for nm, r, x in (("MI", 8, -0.125), ("MI", 14, -1), ("MI", 15, 0), ("SPI", 0, 1), ("SPI", 1, 0.5), ("SPI", 8, 129), ("SPI", 14, 0), ("SPJ", 3, -1072)): fill(c(nm, r, 128, 16), x)
    vts(G, c("col", 5, 6), c("pcf", 1, 2), -1.0, O.add); vts(G, c("col", 6, 7), c("pcf", 1, 2), -1.0, O.mult, 2.0, O.add); vts(G, c("col", 0, 5), c("CI", 0, 5), -1.0, O.mult, c("col", 6, 7), O.add)
    put(c("Cm8"), [([[-16, 8], [-1, 12]], -2, 32), ([[-16, 8], [1000, 12]], -1, 32)])
    for k in range(2):
        part = lambda nm: c(nm, 192 * k, 192 * k + 192); w = part("BlkC"); up = [[0, 4], [16, 4], [0, 12]]; dn = [[0, 4], [-16, 4], [0, 12]]; dg = [[0, 4], [-16, 4], [-1, 12]]; d0 = [[0, 4], [-16, 4], [1000, 12]]
        sel(G, w, c("Zb", 0, 192), up, ge, 64, 64 * k - 1, -1); sel(G, w, w, up, ge, 0, 64 * k + 15, -1)
        put(part("DC2"), [(dn, -64 * k - 14, -8192), (dn, -64 * k - 15, -64)]); put(part("C9"), [(dg, -64 * k - 2, 1), (d0, -64 * k - 1, 1)])
        w = part("DH"); iota(G, w, [[-1, 4], [0, 48]], -73, 0); sel(G, w, w, dn, O.is_equal, 0, -64 * k - 15); put(w, [(dg, -64 * k - 2, -256), (d0, -64 * k - 2, 0), (d0, -64 * k, -81)], False)
    for nm, x in (("I4", 4), ("p4I", 4096), ("I16", 16), ("m4I", -4096)): act(G, c(nm), c("Ib"), F.Identity, 0.0, float(x))
    for h in range(16): put(c("SelT", 128 * h, 128 * h + 128), [([[-64, 2], [-1, 4], [0, 16]], -32 * (h % 2) - 4 * (h // 2), -256 if h < 2 * KV else 1024)])
    put(c("PI"), [rows(8, 1)]); put(c("PZ"), [rows(8, -1), rows(7, -1)]); put(c("PD"), [rows(14, -4096)]); put(c("AR"), [diag(6, 1)]); put(c("PN"), [rows(14, 64)])
    for l in range(1, 6): put(c("BRL", 128 * l - 128, 128 * l), [([[-1, 8], [0, 16]], -8 * (6 - l), 1)])

    def scaled(after):
        for nm, a, x in (("Cmpf", "Cm8", 1 / 32), ("Cm5", "Cm8", -1), ("Cm9", "Cm8", -2), ("C5", "C9", 8), ("C8x", "C9", -64)): behind(G, act(G, c(nm), c(a), F.Identity, 0.0, float(x)), after)
        put(c("Cmpf"), [([[-16, 8], [1000, 12]], -15, 36928 / 4096)], False); behind(G, act(G, c("thf"), c("thi"), F.Identity, 0.5, -1.0), after)
    return scaled


def angles(G, p, Q2):
    vtt(G, c("t2" + p), c("t1" + p), Q2, O.add); vts(G, c("t3" + p), c("t2" + p), 4, O.arith_shift_right, 4095, O.bitwise_and)


def first(G, t):
    sa, sb_ = c("stu", 8 * t, 8 * t + 8), c("sr%d" % t); oa, ob = c("OA%d" % t), c("OB%d" % t); b = "pwB"; N2 = "pdB"
    gat(G, ob, c("IDT"), sb_); G["tn"] = gat(G, c("tnB"), c("nbi"), sb_, -512.0); gat(G, oa, c("IDT"), sa); gat(G, c("tnA"), c("nbi"), sa, -512.0)
    heads = [mm(G, c(b, 256, 512), pc("one", 0, 1), pc("cq", 0, 1), True, False)]
    for p, at, ls in (("B", 0, ("Sdn", "dB")), ("A", 64, ("dA", "Sup"))):
        heads.append(group(G, c(N2, 256 + at, 320 + at), [(c(ls[e]), c("tn" + p, e, 128, 2)) for e in range(2)])[0])
        for e, h in enumerate("AB"):
            o = c("O%s%d" % (p, t), e, 128, 2); mm(G, c(b, 256 + at, 320 + at), c("d%s4" % h), o, False, False); mm(G, c(b, 384 + at, 448 + at), c("d%s26" % h), o, False, at + e == 65)
    nb = b if t else N2; names = lambda: (group(G, c(nb, 0, 128), [(c("dA"), c("tnA")), (c("dB"), c("tnB"))]), group(G, c(nb, 128, 256), [(c("dA"), oa), (c("dB"), ob)]))
    nc = c("NC%d" % t, 0, 128)
    if t:
        for i in heads: behind(G, i, G["key"])
        names(); act(G, c("N0"), c(N2, 256, 384)); act(G, c("NC%d" % t), c(b, 0, 384)); act(G, c("Q20"), c(b, 384, 512)); V0, Q1, Q2 = c("NC%d" % t, 128, 256), c("NC%d" % t, 256, 384), c("Q20")
    else: vcp(G, c("N0"), c(N2, 256, 384)); V0, Q1, Q2 = c(nb, 128, 256), c(b, 256, 384), c(b, 384, 512)

    def rest(after=None):
        i = vtt(G, c("t1B"), c("N0"), Q1, O.mult); angles(G, "B", Q2); vcp(G, c("hu0%d" % t), c("t3B"))
        if not t: names(); vcp(G, nc, c(nb, 0, 128))
        j = vtt(G, c("mk0%d" % t), nc, V0, O.is_equal); k = vts(G, c("wr0%d" % t), nc, 0.0, O.max)
        for x in (i, j, k) if after else (): behind(G, x, after)
    return rest


def records(G, p):
    x, m, hu, d = "x" + p, "m" + p, "hu" + p, "pd" + p; a = 16 * NA
    gat(G, c(x, a, 2048), c("E"), c(hu, NA, 128))
    mm(G, c(d), c("Ib"), c(x, a, 2048), True, False)
    for r in range(4): mm(G, c(d, r, 512, 4), c("nI"), c("W4" + p), False, r == 3)
    act(G, c(m, a, 2048), c(d), F.Abs, 0.0, 0.5)
    for a, b in zip(MCHUNKS, MCHUNKS[1:]):
        if a >= NV: vgat(G, c(x, 16 * a, 16 * b), c("E"), c(hu, a, b))
        else: last = gat(G, c(x, 16 * a, 16 * b), c("E"), c(hu, a, b))
        for r in range(4): vtt(G, c(m, 16 * a + r, 16 * b, 4), c(x, 16 * a + r, 16 * b, 4), c("pw" + p, 4 * a, 4 * b), O.max)
    return last


def scores(G, p, a, t, ks):
    gid = ("key", p, a, t); pk = "pk" + p; key = c(pk, 0, 272); col = lambda k, n: pc(pk, 0, n, k + 1, 272, 17); at = 272 * (p == "B")
    nx = NA if a else CHUNKS[p][-1]; w = len(ks)
    if a: mm(G, key, c("qw" + p), c("WN"), True, False)
    else: mm(G, key, pc("one", 0, 1), pc("cr", 0, 1, at, at + 272), True, False); mm(G, pc(pk, 0, nx, 0, 272), c("qa" if p == "A" else "qr%d" % t, 0, nx), c("WN"), False, False, grp=gid)
    if a: mm(G, c(pk, 0, 136, 17), c("Ib"), c("SP" + p, 0, 128, 16), False, False, grp=gid)
    else: mm(G, c(pk, 0, 136, 17), c("O%s%d" % (p, t)), c("Pick"), False, False, grp=gid)
    for l in [c("mk" + p, 128 * i, 128 * i + 128) for i in range(a + 1)] if a else [c("mk0%d" % t)]: mm(G, key, l, c("BIGP"), False, False, grp=gid)
    for k in ks: mm(G, col(k, nx), c("x" + p, k % w, w * nx, w), c("BX"), False, False, grp=gid)
    for k in sorted(ks, key=lambda k: k % (w // 4)): mm(G, col(k, 128), c("m" + p, k % w, 128 * w, w), c("BM"), False, False, grp=gid)
    mm(G, key, c("wr" + p) if a else c("wr0%d" % t), c("Perm"), False, False)
    G["key"] = mm(G, c(pk, 136, 272), c("n" + p) if a else c("NC%d" % t, 0, 128), c("nPerm"), False, True)


def atom(G, o, p, i, t, x, start, stop):
    if i: mm(G, o, c("RR%d%s" % (i, p)), c(x), start, stop)
    else: mm(G, o, c(x), c("O%s%d" % (p, t)), start, stop)


def slot(p, i): return c("ps" + p, 128 * i, 128 * i + 128) if i < 4 else (c("pw" + p, 384, 512) if i == 4 else c("pk" + p, 288, 416))


def choose(G, p, a, t):
    RM = "RM" + p; SP = "SP" + p; RT = "RT" + p; pk = "pk" + p; sp = c(SP, 0, 128, 16)
    path = (c("CH%d" % t, 56 + 8 * a, 64 + 8 * a) if a < ST - 1 else c("TA", 13, 141, 16)) if p == "A" else c("BL%d" % t, 40 - 8 * a, 48 - 8 * a)
    vscan(G, c(RM), c("SEG"), c(pk, 0, 272), O.add, O.min)
    vtt(G, sp if a < ST - 1 else path, c(RM, 16, 136, 17), c(RM, 152, 272, 17), O.subtract)
    if a == ST - 1: return
    vscan(G, c(RT, 0, 128), c("TR"), c(SP, 0, 128), O.mult, O.add); vscan(G, c("RR%d%s" % (a + 1, p)), c("S01"), c(SP, 0, 128), O.mult, O.add)
    li = c("pd" + p, 0, 8); group(G, li, [(c(SP, 1, 129), c("C8")), (c(RT, 0, 128), c("C8")), (c(RT, 1, 129), c("nC8"))]); vts(G, c("li" + p), li, 512.0, O.add)
    Q2 = c(pk, 128, 256); atom(G, Q2, p, a, t, "I2050", True, False); atom(G, Q2, p, a + 1, t, "I592", False, True); atom(G, slot(p, a + 1), p, a + 1, t, "Ib", True, True)
    sel(G, path, sp, [[0, 8]], O.is_ge, 0, 0, 0)


def front(G, p, a, t):
    n = c("n" + p); q1, li = c("Q1" + p), c("li" + p)
    vgop(G, c("t1" + p), c("NB"), li, q1, O.mult); gat(G, n, c("NB"), li)
    angles(G, p, c("pk" + p, 128, 256)); vcp(G, c("hu" + p), c("t3" + p)); act(G, c("wr" + p), n, F.Relu)
    for i in range(a, -1, -1): vtt(G, c("mk" + p, 128 * i, 128 * i + 128), n, slot(p, i), O.is_equal)
    last = records(G, p)
    if a < ST - 1: act(G, q1, slot(p, a), F.Identity, 2050.0, 4.0)
    scores(G, p, a, t, list(range(16)))
    return last


def walk(G, t, atoms):
    qs = {"A": "qa", "B": "qr%d" % t}
    for p in "BA":
        x, m, at, ch = "x" + p, "m" + p, 64 * (p == "A"), CHUNKS[p]; offs = lambda a, b: c("hu0%d" % t, at + a // 2, at + b // 2)
        for r in range(4): mm(G, c("pw" + p, r, 512, 4), c("Ib"), c(qs[p]))
        if ch[-1] < 128:
            a = ch[-1]; d = "pd" + p; n = 1024 - 8 * a; gat(G, c(x, 8 * a, 1024), c("E"), offs(a, 128)); mm(G, c(d, 0, n), c("Ib"), c(x, 8 * a, 1024), True, False)
            for r in range(8): mm(G, c(d, r, n, 8), c("nI"), c(qs[p], a, 128), False, r == 7)
            act(G, c(m, 8 * a, 1024), c(d, 0, n), F.Abs, 0.0, 0.5)
        for a, b in zip(ch, ch[1:]):
            got = (gat if a else vgat)(G, c(x, 8 * a, 8 * b), c("E"), offs(a, b))
            for r in range(2): vtt(G, c(m, 8 * a + r, 8 * b, 2), c(x, 8 * a + r, 8 * b, 2), c("pw" + p, 4 * a, 4 * b), O.max)
        atom(G, slot(p, 0), p, 0, t, "Ib", True, True); act(G, c("Q1" + p), c("O%s%d" % (p, t)), F.Identity, 2050.0, 4.0)
        if p == "B" or t == 0: gat(G, c("W4" + p), c(qs[p]), c("lW4")); act(G, c("qw" + p, 0, NA), c(qs[p], 0, NA), F.Identity, 127.5)
        if p == "A": mm(G, c("pkA", 272, 280), c("OA%d" % t), c("Pick")); act(G, c("CH%d" % t, 48, 56), c("pkA", 272, 280))
        scores(G, p, 0, t, list(range(8, 16) if p == "B" else range(8)))
    if atoms: atoms(got)
    for a in range(1, ST):
        for p in "BA": choose(G, p, a - 1, t); last = front(G, p, a, t)
        if a == ST - 2: G["late"] = last
    for p in "BA": choose(G, p, ST - 1, t)
    return last


def pairs(G, t):
    CH = "CH%d" % t; ct = pc("CT", 0, 96); k96 = lambda nm: pc(nm, 0, 96); one = pc("one", 0, 1); cp = lambda k: pc("cp", 0, 1, 288 * k, 288 * k + 288)
    mm(G, pc("psB", 0, 96, 384, 512), c(CH, 0, 96), c("Ib")); vcp(G, ct, pc("psB", 0, 96, 384, 512))
    mm(G, c("pdB", 0, 288), ct, k96("PU")); mm(G, c("pdB", 288, 416), k96("CN"), ct); act(G, c("UN"), c("pdB", 0, 416))
    Q1, Q2, D = c("psB", 0, 288), c("pwB", 0, 288), c("pkB", 0, 288)
    mm(G, Q1, ct, k96("PQ1")); mm(G, Q2, ct, k96("PQ2")); group(G, D, [(one, cp(0)), (ct, k96("DC"))])
    vtt(G, c("h1"), c("UN", 0, 288), Q1, O.mult); vtt(G, c("h2"), c("h1"), Q2, O.add); vts(G, c("h3"), c("h2"), 4, O.arith_shift_right, 4095, O.bitwise_and)
    act(G, c("h4", 1, 289), c("h3"), F.Identity, -2048.0); act(G, c("NA"), D, F.Abs); act(G, c("NE"), c("NA"), F.Sign)
    group(G, D, [(one, cp(1)), (c("Ib"), c("h4", 0, 288)), (c("nI"), c("h4", 1, 289))])
    mm(G, c("psA", 0, 256), pc("one1", 0, 1), pc("cq", 0, 1), True, False); mm(G, c("psA", 0, 128), k96("CQ1"), ct, False, False); mm(G, c("psA", 128, 256), k96("CQ2"), ct, False, False)


def rings(G, t):
    CH = "CH%d" % t; b6 = c("B6%d" % t); a6 = c("TA", 13, 141, 16); place = lambda k: c(CH, 8 * k, 8 * k + 8)
    act(G, c("TB", 3, 128, 16), b6)
    for i in range(1, 6): vtt(G, c("NE", 6 * i, 288, 36), place(12 - i), b6, O.not_equal)
    for j in range(6): vtt(G, c("NE", j, 288, 36), a6, place(j) if j else b6, O.not_equal)
    vscan(G, c("FJ"), c("DJ"), c("NE"), O.add, O.min); vscan(G, c("HS"), c("pkB", 0, 288), c("NE"), O.add, O.mult)
    end = c("FJ", 35, 288, 36); vts(G, c("SPJ", 2, 128, 16), end, -64.0, O.mult, 45.0, O.add); vts(G, c("SPI", 3, 128, 16), end, 64.0, O.mult, 1029.5, O.add)
    vts(G, c("HQ", 1, 128, 16), c("HS", 35, 288, 36), -2048.0, O.add)
    vscan(G, c("RRJ"), c("MJ"), c("SPJ"), O.mult, O.add); vscan(G, c("RRI"), c("MI"), c("SPI"), O.mult, O.add)
    Q1, Q2, ta = c("psA", 0, 128), c("psA", 128, 256), c("TA", 0, 128)
    mm(G, Q1, c("TB"), c("I4"), False, False); mm(G, Q2, c("TB"), c("I2050"), False, False)
    mm(G, Q1, ta, c("I4"), False, False); mm(G, Q2, ta, c("I2050"), False, False); mm(G, Q2, c("TA", 11, 139), c("I592"), False, True)
    Z = c("pkA", 0, 128); group(G, Z, [(c("HQ"), c("Ib")), (c("RRJ"), c("p4I")), (c("RRI"), c("p4I"))])
    vtt(G, c("t1A"), c("UN", 288, 416), Q1, O.mult); angles(G, "A", Q2); vtt(G, c("H0"), c("t3A"), Z, O.max)
    vts(G, c("huA"), c("H0"), 4096.0, O.min); vts(G, c("HF"), c("H0"), 4096.0, O.min); vts(G, c("dead"), Z, 4096.0, O.is_ge); zs = act(G, c("Zs"), Z, F.Identity, 0.0, 1 / 4096)
    mm(G, pc("pwA", 96, 104, 384, 512), a6, c("Ib")); act(G, pc("CT", 96, 104), pc("pwA", 96, 104, 384, 512))
    for nm, d, x in (("h5B", 32, 1025.0), ("h8B", 256, 129.0), ("h9B", 512, 129.0)):
        vts(G, c(nm), c("HF"), 1.0 / d, O.mult, x - (d - 1.0) / (2 * d), O.add)
    LO = c("psB", 0, 96); group(G, LO, [(c("HF"), c("Cmpf")), (c("h5B"), c("Cm5")), (c("h8B"), c("Cm8")), (c("h9B"), c("Cm9"))])
    for d in range(2): vts(G, c("LOT", 96 * d, 96 * d + 96), LO, 36928.0 - d, O.add)
    vts(G, c("LOT", 192, 384), c("LOT", 0, 192), -2.0, O.add)
    got = [(gat if a else vgat)(G, c("xA", 16 * a, 16 * b), c("E"), c("huA", a, b)) for a, b in zip(RCHUNKS, RCHUNKS[1:])]
    behind(G, zs, got[1]); behind(G, got[2], zs)
    group(G, c("pkB", 0, 384), [(c("dead"), c("DH")), (c("h5B"), c("C5")), (c("h8B"), c("C8x")), (c("h9B"), c("C9"))]); act(G, c("HI0"), c("pkB", 0, 384)); cnt = c("psB", 96, 480)
    for u in range(0, 64, 4): vts(G, c("OHL", 96 * u, 96 * u + 384), c("LOT"), float(u), O.is_equal)
    for a, b in ((0, RCHUNKS[2]), RCHUNKS[2:]): group(G, c("pdB", 128 + a, 128 + b), [(c("Ib"), c("xA", 16 * a + r, 16 * b, 16)) for r in range(1, 14)])
    mm(G, cnt, c("dead"), c("DC2"), True, False); act(G, c("TH"), c("pdB", 128, 256), F.Sign, c("thf")); mm(G, cnt, c("TH"), c("BlkC"), False, True)
    for k in range(2): vtt(G, c("HIT", 192 * k, 192 * k + 192), c("HI0", 192 * k, 192 * k + 192), c("psB", 96 + 192 * k, 288 + 192 * k), O.min)


def ring_atoms(G, t):
    ct = pc("CT", 0, 104); col = lambda k: c("col", k, k + 1); PL, PI = c("pkA", 128, 256), c("pkA", 256, 384)
    mm(G, PI, c("PI"), c("Zs")); act(G, c("r1"), PI, F.Relu, col(0), -1.0); act(G, c("r2"), PI, F.Relu, col(5))
    group(G, PL, [(c("PZ"), c("Zs")), (c("PN"), c("dead")), (c("I16"), c("r1"))])
    for l in range(5): act(G, c("ZL", 128 * l, 128 * l + 128), PL, F.Abs, col(l))

    def rest(after=None):
        group(G, c("psA", 256, 384), [(pc("AR", 0, 104), ct), (c("m4I"), c("r2")), (c("PD"), c("dead"))])
        for l in range(5):
            o = c("pdA", 128 * l, 128 * l + 128) if l < 4 else c("psA", 384, 512)
            group(G, o, [(pc("BRL", 0, 104, 128 * l, 128 * l + 128), ct), (c("m4I"), c("ZL", 128 * l, 128 * l + 128))])
        for j in (act(G, c("PB", 0, 256), c("psA", 256, 512), F.Relu, 513.0), act(G, c("PB", 256, 768), c("pdA"), F.Relu, 513.0)):
            if after: behind(G, j, after)
        G["atoms"] = j
        Y = c("psA", 256, 384) if after else c("pkA", 384, 512); group(G, Y, [(c("Ib"), c("PB", 128 * k, 128 * k + 128)) for k in range(6)])
        y = c("YR", 128 * t, 128 * t + 128); act(G, y, Y, F.Identity, -1.0)
        dma(G, lambda g, T: g.sync.dma_start(T.yr[:, 128 * t:128 * t + 128], ap(T, y)), [y], [], 2.0)
    return rest if t < RO - 1 else rest()


def lessen(G, t, after, between):
    eighth = lambda nm, k: c(nm, 512 * k, 512 * k + 512)
    for k in range(KV, 8): behind(G, act(G, eighth("D16", k - KV), eighth("E", k), F.Identity, 1023.625, 0.25), after)
    for k in range(KV): mm(G, c(BANKS[k]), c("Ib"), eighth("E", k), True, False)
    for k in range(2):
        hit = c("HIT", 192 * k, 192 * k + 192); th = "THH%d" % k
        for i in range(16):
            o = c(th, 192 * i, 192 * i + 192)
            if i < NS: ab = c("AB", 192 * (NS * k + i), 192 * (NS * k + i + 1)); j = act(G, ab, hit, F.Abs, -4.0 * i); share = act(G, o, ab, F.Relu, 1.0, -1.0)
            if i < NS and t == RO - 1: behind(G, j, G["atoms"])
            if i >= NS: code = vts(G, o, hit, 4.0 * i, O.is_equal)
        for gl in range(4):
            group(G, pc("pwA", 64 * k, 64 * k + 64, gl, 256, 4), [(c("OHL", 48 * k + 12 * gl + s, 6144, 96), c(th, 12 * gl + s, 3072, 48)) for s in range(12)])
    between(code)
    for k in range(KV): behind(G, act(G, eighth("L", k), eighth("E", k), F.Identity, 0.375, 0.75), share)
    vts(G, c("NR"), c("pwA", 0, 256), 0.0, O.is_gt); vtr(G, c("NM"), c("NR")); prev = None
    for k in EIGHTHS:
        bank = BANKS[k]; e = eighth("E", k); o = c(bank)
        if k >= KV: mm(G, o, c("Ib"), eighth("D16", k - KV), True, False)
        for h in range(2):
            i = mm(G, c(bank, 256 * h, 256 * h + 256), c("SelT", 256 * k + 128 * h, 256 * k + 128 * h + 128), c("NM"), False, h == 1)
            if prev: behind(G, i, prev)
            prev = i
        if k < KV: vtt(G, e, eighth("L", k), o, O.max)
        else:
            d = c("DD", 512 * (k % 2), 512 * (k % 2) + 512); act(G, d, o, F.Relu, -2048.0); group(G, o, [(c("Ib"), e), (c("nI"), d)]); act(G, e, o)
        if t == RO - 1 and (k % 2 or k >= KV - 2):
            a, b = 512 * (k if k >= KV - 2 else k - 1), 512 * k + 512
            for a, b in ((a, 4096 - TURN), (4096 - TURN, b)) if a < 4096 - TURN < b else ((a, b),):
                dma(G, lambda g, T, a=a, b=b: g.sync.dma_start(T.ye[:, (a + TURN) % 4096:(b + TURN - 1) % 4096 + 1], T.E[:, a:b]), [c("E", a, b)], [], 1.5 + (b - a) / 1024)


def build(rank, core, topo):
    G = {"ops": [], "acc": {}, "nd": [0]}; peers = [(rank + 1 + t) % N for t in range(RO)]; asks = [(rank - 1 - t) % N for t in range(RO)]; ne = 8

    def exchange(moves, skip=0):
        G["left"] = G.get("left", 0) + sum(m[4] for m in moves)

        def fn(g, T):
            go = []; used = skip
            for sem, src, dst, to, k, dur in moves:
                a = topo.addr(T.cores[to]); m = sum(1 << e for e in topo.engines(core, T.cores[to])[used:used + k]); used += k
                if len(moves) == 1: return g.remote_dma(ap(T, dst), ap(T, src), T.sem[sem], T.sem.loc, a[1], a[0], m)
                go.append(RemoteDMATransfer(dst_ids=[DstId(rid=a[0], pnc=a[1])], dma_engine_mask=m, remote_sem=T.sem[sem], src=ap(T, src), dst=ap(T, dst)))
            return g.remote_dma_fused(go, local_sem=T.sem.loc)
        before = G.get("sent"); G["sent"] = add(G, "G", fn, [m[1] for m in moves], [], ISSUE, sem=("loc", 0))
        if before is not None: behind(G, G["sent"], before)
        for sem in sorted({m[0] for m in moves}):
            mine = [m for m in moves if m[0] == sem]; behind(G, add(G, "N", None, [], [m[2] for m in mine], mine[0][5], sem=(sem, sum(m[4] for m in mine))), G["sent"])
    dma(G, lambda g, T: g.sync.dma_start(T.sti[:], T.st[:]), [], [c("sti")], 1.5)
    dma(G, lambda g, T: g.sync.dma_start(T.qa[:], T.q[:]), [], [c("qa")], 1.6)
    dma(G, lambda g, T: g.sync.dma_start(T.nbi[:], T.nb[:]), [], [c("nbi")], 2.5)
    for a, b in ((0, 4096 - TURN), (4096 - TURN, 4096)): dma(G, lambda g, T, a=a, b=b: g.sync.dma_start(T.E[:, a:b], T.ang[:, (a + TURN) % 4096:(b + TURN - 1) % 4096 + 1]), [], [c("E", a, b)], 4.5)
    dma(G, lambda g, T: g.sync.dma_start(T.thi[:], T.th[:]), [], [c("thi")], 6.5)
    vcp(G, c("stu"), c("sti"))
    starts = lambda t, k, dur: ("as%d" % min(t, 1), c("stu", 8 * t, 8 * t + 8), c("sr%d" % t), peers[t], k, dur)
    walk_constants(G); exchange([starts(0, ne, 0.7)])
    exchange([("aq%d" % min(t, 1), c("qa"), c("qr%d" % t), peers[t], ne // 4 if t else ne // 2, 8.0 if t else 0.7) for t in range(RO)])
    exchange([starts(t, ne // 2, 6.0) for t in (1, 2)], ne)
    first(G, 0)(); behind(G, act(G, c("NB"), c("nbi"), F.Identity, -512.0), G["tn"]); atoms = None; scaled = ring_constants(G)
    for t in range(RO):
        last = walk(G, t, atoms)
        if not t: scaled(G["late"])
        exchange([("ar%d" % t, c("BL%d" % t, 8, 48), c("CH%d" % t, 8, 48), asks[t], 2 * ne, 3.2)])
        exchange([("al%d" % t, c("BL%d" % t, 0, 8), c("B6%d" % t), asks[t], 2 * ne, 1.5)])
        pairs(G, t); lists = first(G, t + 1) if t < RO - 1 else lambda i: None
        rings(G, t); atoms = ring_atoms(G, t); lessen(G, t, last, lists)
    return G, ne


def rank_program(g, core, T, topo):
    rank = T.rank_of(core)
    if rank is None: return
    G, ne = build(rank, core, topo)
    if not ORDER: ORDER["all"] = schedule(G)
    emit(G, ORDER["all"], g, T)
    g.wait_ge(T.sem.loc, G["left"])
